import numpy as np
import ml_dtypes


def mxq(x, axis, fmt="e4m3"):
    dtype, down = {"e4m3": (ml_dtypes.float8_e4m3fn, 7), "e5m2": (ml_dtypes.float8_e5m2, 14)}[fmt]
    v = np.moveaxis(np.asarray(x, np.float32).astype(ml_dtypes.bfloat16).astype(np.float64), axis, -1)
    blocks = v.reshape(v.shape[:-1] + (-1, 32))
    amax = np.abs(blocks).max(-1, keepdims=True)
    byte = np.maximum(np.where(amax > 0, np.frexp(amax)[1] - 1 + 127, 0) - down, 1)
    scale = np.exp2(byte - 127.0)
    codes = (blocks / scale).astype(np.float32).astype(dtype).astype(np.float64)
    return np.moveaxis((codes * scale).reshape(v.shape), -1, axis)


WIDE = False


def mx_kscale(k):
    if not WIDE:
        return np.ones(k)
    levels = np.array([10, -10, 5, -5, 0])
    if k % 512:
        return np.exp2(np.random.permutation(np.resize(levels, k // 32))).repeat(32)
    a = np.empty((k // 512, 16))
    for p in range(k // 512):
        a[p, :8] = np.random.permutation(np.resize(levels, 8))
        for g in range(8):
            far = levels[np.abs(levels - a[p, g]) >= 10]
            a[p, g + 8] = far[np.random.randint(len(far))]
    return np.exp2(a.ravel()).repeat(32)


def f64(x):
    return np.asarray(x).astype(np.float64)


def striped(idx):
    return np.tile(np.asarray(idx).reshape(-1, 16).T, (8, 1)).astype(np.uint16)


def unstriped(offs):
    return offs[:16].T.reshape(-1).astype(np.int64)


E2M1 = np.array([0.0, 0.5, 1.0, 1.5, 2.0, 3.0, 4.0, 6.0, -0.0, -0.5, -1.0, -1.5, -2.0, -3.0, -4.0, -6.0])


def pack_weight(w, fmt):
    k, n = w.shape
    w = f64(np.asarray(w, np.float32).astype(ml_dtypes.bfloat16)).reshape(k // 32, 32, n)
    amax = np.abs(w).max(1)
    if fmt == "e4m3":
        byte = np.frexp(amax)[1] - 1 + 127 - 7
    else:
        mant, ex = np.frexp(amax / 6.0)
        byte = np.where(mant > 0.5, ex, ex - 1) + 127
    byte = np.clip(np.where(amax > 0, byte, 1), 1, 254)
    scaled = (w * np.exp2(127.0 - byte)[:, None, :]).reshape(k, n).astype(np.float32)
    by_word = np.ascontiguousarray(scaled.reshape(k // 512, 128, 4, n).transpose(0, 1, 3, 2))
    if fmt == "e4m3":
        words = by_word.astype(ml_dtypes.float8_e4m3fn).view(np.uint8)
    else:
        c = by_word.astype(ml_dtypes.float4_e2m1fn).view(np.uint8) & 0xF
        words = (c[..., 0::2] | (c[..., 1::2] << 4)).reshape(k // 512, 128, 2 * n)
    return np.ascontiguousarray(words), np.ascontiguousarray(byte.astype(np.uint8).reshape(k // 512, 16, n))


def unpack_weight(words, scales, fmt):
    g, _, n = scales.shape
    words = np.ascontiguousarray(words).reshape(g, 128, n, -1)
    if fmt == "e4m3":
        vals = words.view(ml_dtypes.float8_e4m3fn).astype(np.float64)
    else:
        nib = np.empty((g, 128, n, 4), np.uint8)
        nib[..., 0::2] = words & 0xF
        nib[..., 1::2] = words >> 4
        vals = E2M1[nib]
    vals = vals * np.repeat(np.exp2(scales.astype(np.float64) - 127.0), 8, axis=1)[..., None]
    return vals.transpose(0, 1, 3, 2).reshape(g * 512, n)


B, N, T, D, DV, NQ = 2, 512, 2048, 1024, 128, 128
PAGE = 128
CAP = 2.0


def setup_inputs():
    n = np.random.standard_normal
    pages = np.random.permutation(T // PAGE)[:B * N // PAGE]
    idx = (pages[:, None] * PAGE + np.arange(PAGE)[None, :]).reshape(-1)
    s = mx_kscale(D)[:, None]
    u = np.ones(T)
    u[idx] = mx_kscale(B * N)
    r = np.random.uniform(0.5, 2.0, T)
    qp = [pack_weight(x, "e4m3") for x in n((B, D, NQ)) * s * (1.00 / np.sqrt(D))]
    k = n((D, T)) / s
    v = n((DV, T)) / (u * r)
    kp = pack_weight(k, "e2m1")
    return {
        "q_words": np.stack([x[0] for x in qp]),
        "q_scales": np.stack([x[1] for x in qp]),
        "k_words": np.ascontiguousarray(kp[0].reshape(D // 1024, 2, 128, T, 2).transpose(0, 2, 3, 1, 4)).reshape(D // 1024, 128, T, 4),
        "k_scales": kp[1],
        "vT": v.astype(np.float32),
        "vs": np.tile(u * r, (128, 1)).astype(np.float32),
        "kb": np.tile(n(T), (128, 1)).astype(np.float32),
        "offs": striped(idx),
    }


def reference(q_words, q_scales, k_words, k_scales, vT, vs, kb, offs):
    idx = unstriped(offs)
    k = unpack_weight(k_words.reshape(D // 1024, 128, T, 2, 2).transpose(0, 3, 1, 2, 4).reshape(D // 512, 128, 2 * T), k_scales, "e2m1")
    v = f64(vT)
    pick = lambda x: x[:, idx].reshape(x.shape[0], B, N).transpose(1, 0, 2)
    q = np.stack([unpack_weight(q_words[b], q_scales[b], "e4m3") for b in range(B)])
    score = q.transpose(0, 2, 1) @ pick(k)
    score = score + pick(f64(kb))[:, :1, :]
    score = CAP * np.tanh(score / CAP)
    p = np.square(np.maximum(score, 0.0))
    total = p.sum(-1, keepdims=True) + 1.0
    w = p * pick(f64(vs))[:, :1, :]
    y = mxq(w, 2, "e4m3") @ mxq(pick(v).transpose(0, 2, 1), 1, "e4m3")
    y = y / total
    return y

@@ -1,0 +1,182 @@
+from contextlib import ExitStack
+
+import concourse.mybir as mybir
+from concourse.masks import make_identity
+
+B, N, T, D, DV, NQ = 2, 512, 2048, 1024, 128, 128
+CAP = 2.0
+FLOPS = 2 * B * NQ * N * (D + DV)
+
+F32 = mybir.dt.float32
+BF16 = mybir.dt.bfloat16
+I32 = mybir.dt.int32
+U32 = mybir.dt.uint32
+U16 = mybir.dt.uint16
+U8 = mybir.dt.uint8
+FP8X4 = mybir.dt.float8_e4m3fn_x4
+FP4X4 = mybir.dt.float4_e2m1fn_x4
+ACT = mybir.ActivationFunctionType
+ALU = mybir.AluOpType
+
+P = 128
+PACK = 4
+PASSES = D // (P * PACK)
+RUN = 8
+ROW = 8
+COLS = N // 16
+
+
+def tile_attend_rel2_cap_kb_pgb2q128n512t2048_kernel(
+    tc, q_words, q_scales, k_words, k_scales, vT, vs, kb, offs, out
+):
+    nc = tc.nc
+    with ExitStack() as ctx:
+        sb = ctx.enter_context(tc.tile_pool(name="sb", bufs=1))
+        ps = ctx.enter_context(tc.psum_pool(name="ps", bufs=1))
+
+        def placed(ap):
+            return ap.rearrange("p (j f i) -> p f j i", j=PACK, i=RUN)
+
+        offsets = sb.tile([P, B * COLS], U16, name="offsets")
+        nc.sync.dma_start(offsets[:], offs)
+
+        kw_pool = sb.tile([P, T], I32, name="kw_pool")
+        nc.scalar.dma_start(kw_pool[:], k_words[0].rearrange("p t r -> p (t r)").bitcast(I32))
+
+        ks_pool = sb.tile([P, PASSES, T // 4], I32, name="ks_pool")
+        nc.vector.memset(ks_pool[:], 0)
+        for quad in range(4):
+            nc.sync.dma_start(
+                ks_pool[32 * quad : 32 * quad + 4, :, :],
+                k_scales[:, 4 * quad : 4 * quad + 4, :].rearrange("o r t -> r o t").bitcast(I32),
+            )
+
+        qs = sb.tile([P, B * PASSES, NQ // 4], I32, name="qs", align_bytes=64)
+        nc.vector.memset(qs[:], 0)
+        ident = sb.tile([P, P], F32, name="ident")
+        nc.vector.memset(ident[:], 0.0)
+        make_identity(nc, ident[:], nomemset=True)
+        kb_pool = sb.tile([P, T], F32, name="kb_pool")
+        nc.vector.memset(kb_pool[:], 0.0)
+        vs_pool = sb.tile([P, T], F32, name="vs_pool")
+        nc.vector.memset(vs_pool[:], 0.0)
+
+        qw = sb.tile([P, B * PASSES, NQ], I32, name="qw", align_bytes=64)
+        nc.scalar.dma_start(qw[:], q_words.rearrange("b o g q r -> g (b o) (q r)").bitcast(I32))
+        v_pool = sb.tile([P, T], F32, name="v_pool")
+        nc.scalar.dma_start(v_pool[:], vT)
+
+        nc.sync.dma_start(kb_pool[ROW : ROW + 1, :], kb[0:1, :])
+        for quad in range(4):
+            nc.sync.dma_start(
+                qs[32 * quad : 32 * quad + 4, :, :],
+                q_scales[:, :, 4 * quad : 4 * quad + 4, :].rearrange("b o r q -> r (b o) q").bitcast(I32),
+            )
+        nc.sync.dma_start(vs_pool[ROW : ROW + 1, :], vs[0:1, :])
+
+        warm = sb.tile([P, 1], F32, name="warm")
+        nc.scalar.activation(warm[:], ident[:, 0:1], ACT.Tanh)
+
+        lists = [offsets[:, b * COLS : (b + 1) * COLS] for b in range(B)]
+
+        ident_bf = sb.tile([P, P], BF16, name="ident_bf")
+        nc.scalar.copy(ident_bf[:], ident[:])
+
+        def turn(src, tag, name, dtype=F32):
+            bank = ps.tile([P, PACK, P], dtype, name=name, tag=tag, bufs=2)
+            unit = ident if dtype == F32 else ident_bf
+            for j in range(PACK):
+                nc.tensor.transpose(bank[:, j, :], src[:, j * P : (j + 1) * P], unit[:])
+            return bank
+
+        ps_p = []
+        for b in range(B):
+            ksl = sb.tile([P, PASSES, N], U8, name=f"ksl{b}", align_bytes=64)
+            for o in range(PASSES):
+                nc.vector.tensor_copy(ksl[:, o, :], ks_pool[:, o, :].bitcast(U8).indirect(lists[b]))
+            kbg = sb.tile([P, N], F32, name=f"kbg{b}")
+            nc.vector.tensor_copy(placed(kbg[:].bitcast(U32)), kb_pool[:].bitcast(U32).indirect(lists[b]))
+            ksg = sb.tile([P, PASSES, N], U8, name=f"ksg{b}", align_bytes=64)
+            nc.vector.tensor_copy(
+                ksg[:].bitcast(I32).rearrange("p o (j f w) -> p o j f w", j=PACK, w=2),
+                ksl[:].bitcast(I32).rearrange("p o (f j w) -> p o j f w", j=PACK, w=2),
+            )
+            kwg = sb.tile([P, N], U32, name=f"kwg{b}")
+            nc.vector.tensor_copy(placed(kwg[:]), kw_pool[:].bitcast(U32).indirect(lists[b]))
+            kp = sb.tile([P, PASSES, 2 * N], U8, name=f"kp{b}", align_bytes=64)
+            nc.vector.tensor_copy(
+                kp[:].bitcast(U16), kwg[:].bitcast(U16).rearrange("p (n o) -> p o n", o=PASSES)
+            )
+
+            kbT = turn(kbg, "ta", f"kbT{b}")
+            bias = sb.tile([P, PACK], F32, name=f"bias{b}")
+            nc.scalar.activation(bias[:], kbT[:, :, ROW], ACT.Copy, scale=1.0 / CAP)
+
+            scores = ps.tile([P, PACK, NQ], F32, name=f"scores{b}", tag="s", bufs=2)
+            for j in range(PACK):
+                for o in range(PASSES):
+                    nc.tensor.matmul_mx(
+                        out=scores[:, j, :],
+                        lhsT=kp[:, o, 2 * P * j : 2 * P * (j + 1)].bitcast(FP4X4),
+                        lhsT_scale=ksg[:, o, P * j : P * (j + 1)],
+                        rhs=qw[:, b * PASSES + o, :].bitcast(FP8X4),
+                        rhs_scale=qs[:, b * PASSES + o, :].bitcast(U8),
+                        start=(o == 0),
+                        stop=(o == PASSES - 1),
+                    )
+            x = sb.tile([P, N], F32, name=f"x{b}")
+            for j in range(PACK):
+                nc.scalar.activation(
+                    x[:, j * NQ : (j + 1) * NQ], scores[:, j, :], ACT.Relu, bias=bias[:, j : j + 1], scale=1.0 / CAP
+                )
+            r = sb.tile([P, N], F32, name=f"r{b}")
+            nc.scalar.activation(r[:], x[:], ACT.Tanh)
+            p = sb.tile([P, N], F32, name=f"p{b}")
+            nc.scalar.activation(p[:], r[:], ACT.Square, scale=CAP)
+            ps_p.append(p)
+
+        vsT, vq, vqs = [], [], []
+        for b in range(B):
+            vsg = sb.tile([P, N], F32, name=f"vsg{b}")
+            nc.vector.tensor_copy(placed(vsg[:].bitcast(U32)), vs_pool[:].bitcast(U32).indirect(lists[b]))
+            vg = sb.tile([P, N], BF16, name=f"vg{b}")
+            nc.vector.tensor_copy(placed(vg[:]), v_pool[:].indirect(lists[b]))
+            vsT.append(turn(vsg, "ta", f"vsT{b}"))
+            vt = turn(vg, "tb", f"vt{b}", BF16)
+            vi = sb.tile([P, DV, PACK], BF16, name=f"vi{b}", align_bytes=64)
+            nc.scalar.copy(vi[:], vt[:].rearrange("p j e -> p e j"))
+            vq.append(vi)
+
+        for b in range(B):
+            p = ps_p[b]
+            w = sb.tile([P, NQ, PACK], BF16, name=f"w{b}", align_bytes=64)
+            nc.vector.tensor_tensor(
+                w[:],
+                p[:].rearrange("p (j q) -> p q j", j=PACK),
+                vsT[b][:, :, ROW : ROW + 1].rearrange("p j o -> p o j").to_broadcast([P, NQ, PACK]),
+                ALU.mult,
+            )
+            vc = sb.tile([P, DV], U32, name=f"vc{b}", align_bytes=64)
+            vsc = sb.tile([P, DV], U8, name=f"vsc{b}", align_bytes=64)
+            nc.vector.quantize_mx(vc[:].bitcast(FP8X4), vsc[:], vq[b][:].rearrange("p e j -> p (e j)"))
+            wc = sb.tile([P, NQ], U32, name=f"wc{b}", align_bytes=64)
+            wsc = sb.tile([P, NQ], U8, name=f"wsc{b}", align_bytes=64)
+            nc.vector.quantize_mx(wc[:].bitcast(FP8X4), wsc[:], w[:].rearrange("p q j -> p (q j)"))
+
+            pT = turn(p, "tb", f"pT{b}")
+            junk = sb.tile([P, N], BF16, name=f"junk{b}")
+            total = sb.tile([P, 1], F32, name=f"total{b}")
+            nc.scalar.activation(
+                junk[:], pT[:].rearrange("p j s -> p (j s)"), ACT.Copy, bias=1.0 / N, accum_out=total[:]
+            )
+            inv = sb.tile([P, 1], F32, name=f"inv{b}")
+            nc.vector.reciprocal(inv[:], total[:])
+
+            y = ps.tile([P, DV], F32, name=f"y{b}", tag="y", bufs=2)
+            nc.tensor.matmul_mx(
+                out=y[:], lhsT=wc[:].bitcast(FP8X4), lhsT_scale=wsc[:], rhs=vc[:].bitcast(FP8X4), rhs_scale=vsc[:],
+                start=True, stop=True,
+            )
+            res = sb.tile([P, DV], F32, name=f"res{b}")
+            nc.scalar.activation(res[:], y[:], ACT.Copy, scale=inv[:])
+            nc.sync.dma_start(out[b], res[:])

@@ -35,7 +35,10 @@ def tile_attend_rel2_cap_kb_pgb2q128n512t2048_kernel(
         ps = ctx.enter_context(tc.psum_pool(name="ps", bufs=1))
 
         def placed(ap):
-            return ap.rearrange("p (j f i) -> p f j i", j=PACK, i=RUN)
+            return ap.rearrange("p (j f i) -> p j f i", j=PACK, i=RUN)
+
+        def listed(ap):
+            return ap.rearrange("p (f j i) -> p j f i", j=PACK, i=RUN)
 
         offsets = sb.tile([P, B * COLS], U16, name="offsets")
         nc.sync.dma_start(offsets[:], offs)
@@ -51,6 +54,8 @@ def tile_attend_rel2_cap_kb_pgb2q128n512t2048_kernel(
                 k_scales[:, 4 * quad : 4 * quad + 4, :].rearrange("o r t -> r o t").bitcast(I32),
             )
 
+        seed = sb.tile([P, 2], F32, name="seed")
+        nc.vector.memset(seed[:], 0.0)
         qs = sb.tile([P, B * PASSES, NQ // 4], I32, name="qs", align_bytes=64)
         nc.vector.memset(qs[:], 0)
         ident = sb.tile([P, P], F32, name="ident")
@@ -63,19 +68,20 @@ def tile_attend_rel2_cap_kb_pgb2q128n512t2048_kernel(
 
         qw = sb.tile([P, B * PASSES, NQ], I32, name="qw", align_bytes=64)
         nc.scalar.dma_start(qw[:], q_words.rearrange("b o g q r -> g (b o) (q r)").bitcast(I32))
-        v_pool = sb.tile([P, T], F32, name="v_pool")
+
+        warm = sb.tile([P, 1], F32, name="warm", tag="v_pool")
+        nc.scalar.activation(warm[:], seed[:, 0:1], ACT.Tanh)
+        v_pool = sb.tile([P, T], F32, name="v_pool", tag="v_pool")
         nc.scalar.dma_start(v_pool[:], vT)
 
-        nc.sync.dma_start(kb_pool[ROW : ROW + 1, :], kb[0:1, :])
+        nc.scalar.dma_start(kb_pool[ROW : ROW + 1, :], kb[0:1, :])
         for quad in range(4):
             nc.sync.dma_start(
                 qs[32 * quad : 32 * quad + 4, :, :],
                 q_scales[:, :, 4 * quad : 4 * quad + 4, :].rearrange("b o r q -> r (b o) q").bitcast(I32),
             )
-        nc.sync.dma_start(vs_pool[ROW : ROW + 1, :], vs[0:1, :])
+        nc.scalar.dma_start(vs_pool[ROW : ROW + 1, :], vs[0:1, :])
 
-        warm = sb.tile([P, 1], F32, name="warm")
-        nc.scalar.activation(warm[:], ident[:, 0:1], ACT.Tanh)
 
         lists = [offsets[:, b * COLS : (b + 1) * COLS] for b in range(B)]
 
@@ -94,18 +100,21 @@ def tile_attend_rel2_cap_kb_pgb2q128n512t2048_kernel(
             ksl = sb.tile([P, PASSES, N], U8, name=f"ksl{b}", align_bytes=64)
             for o in range(PASSES):
                 nc.vector.tensor_copy(ksl[:, o, :], ks_pool[:, o, :].bitcast(U8).indirect(lists[b]))
+            kbl = sb.tile([P, N], F32, name=f"kbl{b}")
+            nc.vector.tensor_copy(kbl[:], kb_pool[:].indirect(lists[b]))
             kbg = sb.tile([P, N], F32, name=f"kbg{b}")
-            nc.vector.tensor_copy(placed(kbg[:].bitcast(U32)), kb_pool[:].bitcast(U32).indirect(lists[b]))
+            nc.scalar.copy(placed(kbg[:]), listed(kbl[:]))
             ksg = sb.tile([P, PASSES, N], U8, name=f"ksg{b}", align_bytes=64)
             nc.vector.tensor_copy(
                 ksg[:].bitcast(I32).rearrange("p o (j f w) -> p o j f w", j=PACK, w=2),
                 ksl[:].bitcast(I32).rearrange("p o (f j w) -> p o j f w", j=PACK, w=2),
             )
             kwg = sb.tile([P, N], U32, name=f"kwg{b}")
-            nc.vector.tensor_copy(placed(kwg[:]), kw_pool[:].bitcast(U32).indirect(lists[b]))
+            nc.vector.tensor_copy(kwg[:], kw_pool[:].bitcast(U32).indirect(lists[b]))
             kp = sb.tile([P, PASSES, 2 * N], U8, name=f"kp{b}", align_bytes=64)
             nc.vector.tensor_copy(
-                kp[:].bitcast(U16), kwg[:].bitcast(U16).rearrange("p (n o) -> p o n", o=PASSES)
+                kp[:].bitcast(U16).rearrange("p o (j f i) -> p o j f i", j=PACK, i=RUN),
+                kwg[:].bitcast(U16).rearrange("p (f j i o) -> p o j f i", j=PACK, i=RUN, o=PASSES),
             )
 
             kbT = turn(kbg, "ta", f"kbT{b}")
@@ -137,10 +146,14 @@ def tile_attend_rel2_cap_kb_pgb2q128n512t2048_kernel(
 
         vsT, vq, vqs = [], [], []
         for b in range(B):
+            vsl = sb.tile([P, N], F32, name=f"vsl{b}")
+            nc.vector.tensor_copy(vsl[:], vs_pool[:].indirect(lists[b]))
             vsg = sb.tile([P, N], F32, name=f"vsg{b}")
-            nc.vector.tensor_copy(placed(vsg[:].bitcast(U32)), vs_pool[:].bitcast(U32).indirect(lists[b]))
+            nc.scalar.copy(placed(vsg[:]), listed(vsl[:]))
+            vl = sb.tile([P, N], F32, name=f"vl{b}")
+            nc.vector.tensor_copy(vl[:], v_pool[:].indirect(lists[b]))
             vg = sb.tile([P, N], BF16, name=f"vg{b}")
-            nc.vector.tensor_copy(placed(vg[:]), v_pool[:].indirect(lists[b]))
+            nc.scalar.copy(placed(vg[:]), listed(vl[:]))
             vsT.append(turn(vsg, "ta", f"vsT{b}"))
             vt = turn(vg, "tb", f"vt{b}", BF16)
             vi = sb.tile([P, DV, PACK], BF16, name=f"vi{b}", align_bytes=64)

@@ -32,100 +32,98 @@ def tile_attend_rel2_cap_kb_pgb2q128n512t2048_kernel(
     nc = tc.nc
     with ExitStack() as ctx:
         sb = ctx.enter_context(tc.tile_pool(name="sb", bufs=1))
+        reuse = ctx.enter_context(tc.tile_pool(name="reuse", bufs=1))
         ps = ctx.enter_context(tc.psum_pool(name="ps", bufs=1))
 
         def placed(ap):
-            return ap.rearrange("p (j f i) -> p j f i", j=PACK, i=RUN)
-
-        def listed(ap):
-            return ap.rearrange("p (f j i) -> p j f i", j=PACK, i=RUN)
+            return ap.rearrange("p (j f i) -> p f j i", j=PACK, i=RUN)
 
         offsets = sb.tile([P, B * COLS], U16, name="offsets")
         nc.sync.dma_start(offsets[:], offs)
 
-        kw_pool = sb.tile([P, T], I32, name="kw_pool")
+        kw_pool = reuse.tile([P, T], I32, name="kw_pool", offset=0)
         nc.scalar.dma_start(kw_pool[:], k_words[0].rearrange("p t r -> p (t r)").bitcast(I32))
 
         ks_pool = sb.tile([P, PASSES, T // 4], I32, name="ks_pool")
-        nc.vector.memset(ks_pool[:], 0)
+        nc.gpsimd.memset(ks_pool[:], 0)
         for quad in range(4):
             nc.sync.dma_start(
                 ks_pool[32 * quad : 32 * quad + 4, :, :],
                 k_scales[:, 4 * quad : 4 * quad + 4, :].rearrange("o r t -> r o t").bitcast(I32),
             )
 
-        seed = sb.tile([P, 2], F32, name="seed")
-        nc.vector.memset(seed[:], 0.0)
-        qs = sb.tile([P, B * PASSES, NQ // 4], I32, name="qs", align_bytes=64)
-        nc.vector.memset(qs[:], 0)
-        ident = sb.tile([P, P], F32, name="ident")
-        nc.vector.memset(ident[:], 0.0)
-        make_identity(nc, ident[:], nomemset=True)
-        kb_pool = sb.tile([P, T], F32, name="kb_pool")
-        nc.vector.memset(kb_pool[:], 0.0)
-        vs_pool = sb.tile([P, T], F32, name="vs_pool")
-        nc.vector.memset(vs_pool[:], 0.0)
-
-        qw = sb.tile([P, B * PASSES, NQ], I32, name="qw", align_bytes=64)
-        nc.scalar.dma_start(qw[:], q_words.rearrange("b o g q r -> g (b o) (q r)").bitcast(I32))
-
+        seed = sb.tile([P, 1], F32, name="seed", tag="qw", align_bytes=64)
+        nc.gpsimd.memset(seed[:], 0.0)
         warm = sb.tile([P, 1], F32, name="warm", tag="v_pool")
-        nc.scalar.activation(warm[:], seed[:, 0:1], ACT.Tanh)
+        nc.scalar.activation(warm[:], seed[:], ACT.Tanh)
+        qw = sb.tile([P, B * PASSES, NQ], I32, name="qw", tag="qw", align_bytes=64)
+        nc.scalar.dma_start(qw[:], q_words.rearrange("b o g q r -> g (b o) (q r)").bitcast(I32))
         v_pool = sb.tile([P, T], F32, name="v_pool", tag="v_pool")
         nc.scalar.dma_start(v_pool[:], vT)
 
-        nc.scalar.dma_start(kb_pool[ROW : ROW + 1, :], kb[0:1, :])
+        kb_pool = reuse.tile([P, T], F32, name="kb_pool", offset=4 * T)
+        nc.vector.memset(kb_pool[:], 0.0)
+        nc.sync.dma_start(kb_pool[ROW : ROW + 1, :], kb[0:1, :])
+
+        ident = sb.tile([P, P], F32, name="ident")
+        make_identity(nc, ident[:])
+        ident_bf = sb.tile([P, P], BF16, name="ident_bf")
+        nc.scalar.copy(ident_bf[:], ident[:])
+
+        qs = sb.tile([P, B * PASSES, NQ // 4], I32, name="qs", align_bytes=64)
+        nc.gpsimd.memset(qs[:], 0)
         for quad in range(4):
             nc.sync.dma_start(
                 qs[32 * quad : 32 * quad + 4, :, :],
                 q_scales[:, :, 4 * quad : 4 * quad + 4, :].rearrange("b o r q -> r (b o) q").bitcast(I32),
             )
-        nc.scalar.dma_start(vs_pool[ROW : ROW + 1, :], vs[0:1, :])
-
+        vs_pool = sb.tile([P, T], F32, name="vs_pool")
+        nc.gpsimd.memset(vs_pool[:], 0.0)
+        nc.sync.dma_start(vs_pool[ROW : ROW + 1, :], vs[0:1, :])
 
         lists = [offsets[:, b * COLS : (b + 1) * COLS] for b in range(B)]
 
-        ident_bf = sb.tile([P, P], BF16, name="ident_bf")
-        nc.scalar.copy(ident_bf[:], ident[:])
-
-        def turn(src, tag, name, dtype=F32):
+        def turn(src, tag, name, dtype=F32, first=0, step=P):
             bank = ps.tile([P, PACK, P], dtype, name=name, tag=tag, bufs=2)
             unit = ident if dtype == F32 else ident_bf
             for j in range(PACK):
-                nc.tensor.transpose(bank[:, j, :], src[:, j * P : (j + 1) * P], unit[:])
+                nc.tensor.transpose(bank[:, j, :], src[:, first + j * step : first + j * step + P], unit[:])
             return bank
 
         ps_p = []
+        kbg = sb.tile([P, B * N], F32, name="kbg")
         for b in range(B):
-            ksl = sb.tile([P, PASSES, N], U8, name=f"ksl{b}", align_bytes=64)
+            if b == 0:
+                ksl = sb.tile([P, PASSES, N], U8, name="ksl0")
+                kwg = sb.tile([P, N], U32, name="kwg0")
+            else:
+                ksl = reuse.tile([P, PASSES, N], U8, name="ksl1", offset=4 * T)
+                kwg = reuse.tile([P, N], U32, name="kwg1", offset=4 * T + PASSES * N)
             for o in range(PASSES):
                 nc.vector.tensor_copy(ksl[:, o, :], ks_pool[:, o, :].bitcast(U8).indirect(lists[b]))
-            kbl = sb.tile([P, N], F32, name=f"kbl{b}")
-            nc.vector.tensor_copy(kbl[:], kb_pool[:].indirect(lists[b]))
-            kbg = sb.tile([P, N], F32, name=f"kbg{b}")
-            nc.scalar.copy(placed(kbg[:]), listed(kbl[:]))
+            nc.vector.tensor_copy(kwg[:], kw_pool[:].bitcast(U32).indirect(lists[b]))
+            if b == 0:
+                nc.vector.tensor_copy(placed(kbg[:].bitcast(U32)), kb_pool[:].bitcast(U32).indirect(offsets[:]))
             ksg = sb.tile([P, PASSES, N], U8, name=f"ksg{b}", align_bytes=64)
             nc.vector.tensor_copy(
                 ksg[:].bitcast(I32).rearrange("p o (j f w) -> p o j f w", j=PACK, w=2),
                 ksl[:].bitcast(I32).rearrange("p o (f j w) -> p o j f w", j=PACK, w=2),
             )
-            kwg = sb.tile([P, N], U32, name=f"kwg{b}")
-            nc.vector.tensor_copy(kwg[:], kw_pool[:].bitcast(U32).indirect(lists[b]))
             kp = sb.tile([P, PASSES, 2 * N], U8, name=f"kp{b}", align_bytes=64)
             nc.vector.tensor_copy(
                 kp[:].bitcast(U16).rearrange("p o (j f i) -> p o j f i", j=PACK, i=RUN),
                 kwg[:].bitcast(U16).rearrange("p (f j i o) -> p o j f i", j=PACK, i=RUN, o=PASSES),
             )
 
-            kbT = turn(kbg, "ta", f"kbT{b}")
+            kbT = turn(kbg, "ta", f"kbT{b}", F32, b * P, B * P)
             bias = sb.tile([P, PACK], F32, name=f"bias{b}")
             nc.scalar.activation(bias[:], kbT[:, :, ROW], ACT.Copy, scale=1.0 / CAP)
 
-            scores = ps.tile([P, PACK, NQ], F32, name=f"scores{b}", tag="s", bufs=2)
+            scores = [ps.tile([P, 2, NQ], F32, name=f"scores{b}{h}", tag="s", bufs=4) for h in range(2)]
             for j in range(PACK):
                 for o in range(PASSES):
                     nc.tensor.matmul_mx(
-                        out=scores[:, j, :],
+                        out=scores[j // 2][:, j % 2, :],
                         lhsT=kp[:, o, 2 * P * j : 2 * P * (j + 1)].bitcast(FP4X4),
                         lhsT_scale=ksg[:, o, P * j : P * (j + 1)],
                         rhs=qw[:, b * PASSES + o, :].bitcast(FP8X4),
@@ -136,7 +134,7 @@ def tile_attend_rel2_cap_kb_pgb2q128n512t2048_kernel(
             x = sb.tile([P, N], F32, name=f"x{b}")
             for j in range(PACK):
                 nc.scalar.activation(
-                    x[:, j * NQ : (j + 1) * NQ], scores[:, j, :], ACT.Relu, bias=bias[:, j : j + 1], scale=1.0 / CAP
+                    x[:, j * NQ : (j + 1) * NQ], scores[j // 2][:, j % 2, :], ACT.Relu, bias=bias[:, j : j + 1], scale=1.0 / CAP
                 )
             r = sb.tile([P, N], F32, name=f"r{b}")
             nc.scalar.activation(r[:], x[:], ACT.Tanh)
@@ -146,16 +144,12 @@ def tile_attend_rel2_cap_kb_pgb2q128n512t2048_kernel(
 
         vsT, vq, vqs = [], [], []
         for b in range(B):
-            vsl = sb.tile([P, N], F32, name=f"vsl{b}")
-            nc.vector.tensor_copy(vsl[:], vs_pool[:].indirect(lists[b]))
-            vsg = sb.tile([P, N], F32, name=f"vsg{b}")
-            nc.scalar.copy(placed(vsg[:]), listed(vsl[:]))
-            vl = sb.tile([P, N], F32, name=f"vl{b}")
-            nc.vector.tensor_copy(vl[:], v_pool[:].indirect(lists[b]))
-            vg = sb.tile([P, N], BF16, name=f"vg{b}")
-            nc.scalar.copy(placed(vg[:]), listed(vl[:]))
-            vsT.append(turn(vsg, "ta", f"vsT{b}"))
+            vg = reuse.tile([P, N], BF16, name=f"vg{b}", offset=6 * N * b)
+            nc.vector.tensor_copy(placed(vg[:]), v_pool[:].indirect(lists[b]))
+            vsg = reuse.tile([P, N], F32, name=f"vsg{b}", offset=6 * N * b + 2 * N)
+            nc.vector.tensor_copy(placed(vsg[:].bitcast(U32)), vs_pool[:].bitcast(U32).indirect(lists[b]))
             vt = turn(vg, "tb", f"vt{b}", BF16)
+            vsT.append(turn(vsg, "ta", f"vsT{b}"))
             vi = sb.tile([P, DV, PACK], BF16, name=f"vi{b}", align_bytes=64)
             nc.scalar.copy(vi[:], vt[:].rearrange("p j e -> p e j"))
             vq.append(vi)
@@ -176,16 +170,20 @@ def tile_attend_rel2_cap_kb_pgb2q128n512t2048_kernel(
             wsc = sb.tile([P, NQ], U8, name=f"wsc{b}", align_bytes=64)
             nc.vector.quantize_mx(wc[:].bitcast(FP8X4), wsc[:], w[:].rearrange("p q j -> p (q j)"))
 
-            pT = turn(p, "tb", f"pT{b}")
-            junk = sb.tile([P, N], BF16, name=f"junk{b}")
+            pT = ps.tile([P, P], F32, name=f"pT{b}", tag="s", bufs=4)
+            for j in range(PACK):
+                nc.tensor.matmul(
+                    pT[:], p[:, j * NQ : (j + 1) * NQ], ident[:], start=(j == 0), stop=(j == PACK - 1), is_transpose=True
+                )
+            junk = sb.tile([P, P], BF16, name=f"junk{b}")
             total = sb.tile([P, 1], F32, name=f"total{b}")
             nc.scalar.activation(
-                junk[:], pT[:].rearrange("p j s -> p (j s)"), ACT.Copy, bias=1.0 / N, accum_out=total[:]
+                junk[:], pT[:], ACT.Copy, bias=1.0 / P, accum_out=total[:]
             )
             inv = sb.tile([P, 1], F32, name=f"inv{b}")
             nc.vector.reciprocal(inv[:], total[:])
 
-            y = ps.tile([P, DV], F32, name=f"y{b}", tag="y", bufs=2)
+            y = ps.tile([P, DV], F32, name=f"y{b}", tag="s", bufs=4)
             nc.tensor.matmul_mx(
                 out=y[:], lhsT=wc[:].bitcast(FP8X4), lhsT_scale=wsc[:], rhs=vc[:].bitcast(FP8X4), rhs_scale=vsc[:],
                 start=True, stop=True,

@@ -23,6 +23,7 @@ PACK = 4
 PASSES = D // (P * PACK)
 RUN = 8
 ROW = 8
+HOME = 96
 COLS = N // 16
 
 
@@ -38,28 +39,33 @@ def tile_attend_rel2_cap_kb_pgb2q128n512t2048_kernel(
         def placed(ap):
             return ap.rearrange("p (j f i) -> p f j i", j=PACK, i=RUN)
 
+        def listed(ap):
+            return ap.rearrange("p (f j i) -> p f j i", j=PACK, i=RUN)
+
         offsets = sb.tile([P, B * COLS], U16, name="offsets")
         nc.sync.dma_start(offsets[:], offs)
 
+        v_raw = sb.tile([P, T], F32, name="v_raw")
+        nc.scalar.dma_start(v_raw[:], vT)
         kw_pool = reuse.tile([P, T], I32, name="kw_pool", offset=0)
         nc.scalar.dma_start(kw_pool[:], k_words[0].rearrange("p t r -> p (t r)").bitcast(I32))
 
-        ks_pool = sb.tile([P, PASSES, T // 4], I32, name="ks_pool")
-        nc.gpsimd.memset(ks_pool[:], 0)
-        for quad in range(4):
-            nc.sync.dma_start(
-                ks_pool[32 * quad : 32 * quad + 4, :, :],
-                k_scales[:, 4 * quad : 4 * quad + 4, :].rearrange("o r t -> r o t").bitcast(I32),
-            )
+        ks_pool = sb.tile([P, T // 4], I32, name="ks_pool")
+        nc.sync.dma_start(ks_pool[HOME:P, :], k_scales.rearrange("o f t -> (o f) t").bitcast(I32))
+        nc.vector.memset(ks_pool[0:HOME, :], 0)
 
-        seed = sb.tile([P, 1], F32, name="seed", tag="qw", align_bytes=64)
+        seed = sb.tile([P, 1], F32, name="seed")
         nc.gpsimd.memset(seed[:], 0.0)
-        warm = sb.tile([P, 1], F32, name="warm", tag="v_pool")
+        warm = sb.tile([P, 1], F32, name="warm")
         nc.scalar.activation(warm[:], seed[:], ACT.Tanh)
-        qw = sb.tile([P, B * PASSES, NQ], I32, name="qw", tag="qw", align_bytes=64)
-        nc.scalar.dma_start(qw[:], q_words.rearrange("b o g q r -> g (b o) (q r)").bitcast(I32))
-        v_pool = sb.tile([P, T], F32, name="v_pool", tag="v_pool")
-        nc.scalar.dma_start(v_pool[:], vT)
+
+        qs = sb.tile([P, B * PASSES, NQ // 4], I32, name="qs", align_bytes=64)
+        nc.gpsimd.memset(qs[:], 0)
+        for row in range(4):
+            nc.sync.dma_start(
+                qs[row:P:32, :, :],
+                q_scales[:, :, row:16:4, :].rearrange("b o f q -> f (b o) q").bitcast(I32),
+            )
 
         kb_pool = reuse.tile([P, T], F32, name="kb_pool", offset=4 * T)
         nc.vector.memset(kb_pool[:], 0.0)
@@ -70,67 +76,83 @@ def tile_attend_rel2_cap_kb_pgb2q128n512t2048_kernel(
         ident_bf = sb.tile([P, P], BF16, name="ident_bf")
         nc.scalar.copy(ident_bf[:], ident[:])
 
-        qs = sb.tile([P, B * PASSES, NQ // 4], I32, name="qs", align_bytes=64)
-        nc.gpsimd.memset(qs[:], 0)
-        for quad in range(4):
-            nc.sync.dma_start(
-                qs[32 * quad : 32 * quad + 4, :, :],
-                q_scales[:, :, 4 * quad : 4 * quad + 4, :].rearrange("b o r q -> r (b o) q").bitcast(I32),
-            )
+        ksg = sb.tile([P, PASSES, B * N // 4], I32, name="ksg", align_bytes=64)
+        nc.gpsimd.memset(ksg[:], 0)
+        qw = sb.tile([P, B * PASSES, NQ], I32, name="qw", align_bytes=64)
+        nc.gpsimd.dma_start(qw[:], q_words.rearrange("b o g q r -> g (b o) (q r)").bitcast(I32))
         vs_pool = sb.tile([P, T], F32, name="vs_pool")
         nc.gpsimd.memset(vs_pool[:], 0.0)
-        nc.sync.dma_start(vs_pool[ROW : ROW + 1, :], vs[0:1, :])
+        nc.gpsimd.dma_start(vs_pool[ROW : ROW + 1, :], vs[0:1, :])
 
         lists = [offsets[:, b * COLS : (b + 1) * COLS] for b in range(B)]
 
         def turn(src, tag, name, dtype=F32, first=0, step=P):
-            bank = ps.tile([P, PACK, P], dtype, name=name, tag=tag, bufs=2)
+            bank = ps.tile([P, PACK, P], dtype, name=name, tag=tag)
             unit = ident if dtype == F32 else ident_bf
             for j in range(PACK):
                 nc.tensor.transpose(bank[:, j, :], src[:, first + j * step : first + j * step + P], unit[:])
             return bank
 
-        ps_p = []
+        ksl = sb.tile([P, B * N], U8, name="ksl")
+        nc.vector.tensor_copy(ksl[:], ks_pool[:].bitcast(U8).indirect(offsets[:]))
+        ksr = sb.tile([P, B * N // 4], I32, name="ksr")
+        nc.vector.tensor_copy(
+            ksr[:].rearrange("p (j f w) -> p j f w", j=PACK, w=2),
+            ksl[:].bitcast(I32).rearrange("p (f j w) -> p j f w", j=PACK, w=2),
+        )
+        for o in range(PASSES):
+            for quad in range(4):
+                first = HOME + 16 * o + 4 * quad
+                nc.sync.dma_start(ksg[32 * quad : 32 * quad + 4, o, :], ksr[first : first + 4, :])
+
         kbg = sb.tile([P, B * N], F32, name="kbg")
+        nc.vector.tensor_copy(placed(kbg[:].bitcast(U32)), kb_pool[:].bitcast(U32).indirect(offsets[:]))
+
+        v_pool = sb.tile([P, T], BF16, name="v_pool")
+        nc.scalar.activation(v_pool[:], v_raw[:], ACT.Copy)
+        vq = []
         for b in range(B):
-            if b == 0:
-                ksl = sb.tile([P, PASSES, N], U8, name="ksl0")
-                kwg = sb.tile([P, N], U32, name="kwg0")
-            else:
-                ksl = reuse.tile([P, PASSES, N], U8, name="ksl1", offset=4 * T)
-                kwg = reuse.tile([P, N], U32, name="kwg1", offset=4 * T + PASSES * N)
-            for o in range(PASSES):
-                nc.vector.tensor_copy(ksl[:, o, :], ks_pool[:, o, :].bitcast(U8).indirect(lists[b]))
+            vg = sb.tile([P, N], BF16, name=f"vg{b}")
+            nc.scalar.activation(placed(vg[:]), v_pool[:].indirect(lists[b]), ACT.Copy)
+            vt = turn(vg, f"v{b}", f"vt{b}", BF16)
+            vi = sb.tile([P, DV, PACK], BF16, name=f"vi{b}", align_bytes=64)
+            nc.scalar.copy(vi[:], vt[:].rearrange("p j e -> p e j"))
+            vq.append(vi)
+
+        ps_p = []
+        for b in range(B):
+            kwg = reuse.tile([P, N], U32, name=f"kwg{b}", tag="kwg", offset=4 * T)
             nc.vector.tensor_copy(kwg[:], kw_pool[:].bitcast(U32).indirect(lists[b]))
-            if b == 0:
-                nc.vector.tensor_copy(placed(kbg[:].bitcast(U32)), kb_pool[:].bitcast(U32).indirect(offsets[:]))
-            ksg = sb.tile([P, PASSES, N], U8, name=f"ksg{b}", align_bytes=64)
-            nc.vector.tensor_copy(
-                ksg[:].bitcast(I32).rearrange("p o (j f w) -> p o j f w", j=PACK, w=2),
-                ksl[:].bitcast(I32).rearrange("p o (f j w) -> p o j f w", j=PACK, w=2),
-            )
             kp = sb.tile([P, PASSES, 2 * N], U8, name=f"kp{b}", align_bytes=64)
             nc.vector.tensor_copy(
                 kp[:].bitcast(U16).rearrange("p o (j f i) -> p o j f i", j=PACK, i=RUN),
                 kwg[:].bitcast(U16).rearrange("p (f j i o) -> p o j f i", j=PACK, i=RUN, o=PASSES),
             )
 
-            kbT = turn(kbg, "ta", f"kbT{b}", F32, b * P, B * P)
+            kbT = turn(kbg, f"a{b}", f"kbT{b}", F32, b * P, B * P)
             bias = sb.tile([P, PACK], F32, name=f"bias{b}")
             nc.scalar.activation(bias[:], kbT[:, :, ROW], ACT.Copy, scale=1.0 / CAP)
 
-            scores = [ps.tile([P, 2, NQ], F32, name=f"scores{b}{h}", tag="s", bufs=4) for h in range(2)]
+            scores = [ps.tile([P, 2, NQ], F32, name=f"scores{b}{h}", tag=f"s{b}{h}") for h in range(2)]
             for j in range(PACK):
                 for o in range(PASSES):
                     nc.tensor.matmul_mx(
                         out=scores[j // 2][:, j % 2, :],
                         lhsT=kp[:, o, 2 * P * j : 2 * P * (j + 1)].bitcast(FP4X4),
-                        lhsT_scale=ksg[:, o, P * j : P * (j + 1)],
+                        lhsT_scale=ksg[:, o, :].bitcast(U8)[:, P * (B * j + b) : P * (B * j + b + 1)],
                         rhs=qw[:, b * PASSES + o, :].bitcast(FP8X4),
                         rhs_scale=qs[:, b * PASSES + o, :].bitcast(U8),
                         start=(o == 0),
                         stop=(o == PASSES - 1),
                     )
+            if b in (1,):
+                t = sb.tile([P, N], F32, name=f"t{b}")
+                for j in range(PACK):
+                    nc.scalar.activation(
+                        t[:, j * NQ : (j + 1) * NQ], scores[j // 2][:, j % 2, :], ACT.Tanh, bias=bias[:, j : j + 1], scale=1.0 / CAP
+                    )
+                ps_p.append(t)
+                continue
             x = sb.tile([P, N], F32, name=f"x{b}")
             for j in range(PACK):
                 nc.scalar.activation(
@@ -139,28 +161,33 @@ def tile_attend_rel2_cap_kb_pgb2q128n512t2048_kernel(
             r = sb.tile([P, N], F32, name=f"r{b}")
             nc.scalar.activation(r[:], x[:], ACT.Tanh)
             p = sb.tile([P, N], F32, name=f"p{b}")
-            nc.scalar.activation(p[:], r[:], ACT.Square, scale=CAP)
+            nc.scalar.activation(p[:], r[:], ACT.Square)
             ps_p.append(p)
 
-        vsT, vq, vqs = [], [], []
+        vsT = []
         for b in range(B):
-            vg = reuse.tile([P, N], BF16, name=f"vg{b}", offset=6 * N * b)
-            nc.vector.tensor_copy(placed(vg[:]), v_pool[:].indirect(lists[b]))
-            vsg = reuse.tile([P, N], F32, name=f"vsg{b}", offset=6 * N * b + 2 * N)
+            vsg = reuse.tile([P, N], F32, name=f"vsg{b}", offset=4 * T - 2 * N + 4 * N * b)
             nc.vector.tensor_copy(placed(vsg[:].bitcast(U32)), vs_pool[:].bitcast(U32).indirect(lists[b]))
-            vt = turn(vg, "tb", f"vt{b}", BF16)
-            vsT.append(turn(vsg, "ta", f"vsT{b}"))
-            vi = sb.tile([P, DV, PACK], BF16, name=f"vi{b}", align_bytes=64)
-            nc.scalar.copy(vi[:], vt[:].rearrange("p j e -> p e j"))
-            vq.append(vi)
+            vsT.append(turn(vsg, f"s0{b}", f"vsT{b}"))
+
+        sq = []
+        for b in range(B):
+            if b in (1,):
+                p = sb.tile([P, N], F32, name=f"p{b}")
+                nc.vector.scalar_tensor_tensor(p[:], ps_p[b][:], 0.0, ps_p[b][:], ALU.max, ALU.mult)
+                sq.append(p)
+            else:
+                sq.append(ps_p[b])
 
         for b in range(B):
-            p = ps_p[b]
+            p = sq[b]
             w = sb.tile([P, NQ, PACK], BF16, name=f"w{b}", align_bytes=64)
-            nc.vector.tensor_tensor(
+            nc.vector.scalar_tensor_tensor(
                 w[:],
                 p[:].rearrange("p (j q) -> p q j", j=PACK),
+                CAP * CAP,
                 vsT[b][:, :, ROW : ROW + 1].rearrange("p j o -> p o j").to_broadcast([P, NQ, PACK]),
+                ALU.mult,
                 ALU.mult,
             )
             vc = sb.tile([P, DV], U32, name=f"vc{b}", align_bytes=64)
@@ -170,7 +197,7 @@ def tile_attend_rel2_cap_kb_pgb2q128n512t2048_kernel(
             wsc = sb.tile([P, NQ], U8, name=f"wsc{b}", align_bytes=64)
             nc.vector.quantize_mx(wc[:].bitcast(FP8X4), wsc[:], w[:].rearrange("p q j -> p (q j)"))
 
-            pT = ps.tile([P, P], F32, name=f"pT{b}", tag="s", bufs=4)
+            pT = ps.tile([P, P], F32, name=f"pT{b}", tag=f"s1{b}")
             for j in range(PACK):
                 nc.tensor.matmul(
                     pT[:], p[:, j * NQ : (j + 1) * NQ], ident[:], start=(j == 0), stop=(j == PACK - 1), is_transpose=True
@@ -178,12 +205,12 @@ def tile_attend_rel2_cap_kb_pgb2q128n512t2048_kernel(
             junk = sb.tile([P, P], BF16, name=f"junk{b}")
             total = sb.tile([P, 1], F32, name=f"total{b}")
             nc.scalar.activation(
-                junk[:], pT[:], ACT.Copy, bias=1.0 / P, accum_out=total[:]
+                junk[:], pT[:], ACT.Copy, bias=1.0 / P, scale=CAP * CAP, accum_out=total[:]
             )
             inv = sb.tile([P, 1], F32, name=f"inv{b}")
             nc.vector.reciprocal(inv[:], total[:])
 
-            y = ps.tile([P, DV], F32, name=f"y{b}", tag="s", bufs=4)
+            y = ps.tile([P, DV], F32, name=f"y{b}", tag=f"a{b}")
             nc.tensor.matmul_mx(
                 out=y[:], lhsT=wc[:].bitcast(FP8X4), lhsT_scale=wsc[:], rhs=vc[:].bitcast(FP8X4), rhs_scale=vsc[:],
                 start=True, stop=True,

@@ -22,7 +22,7 @@ P = 128
 PACK = 4
 PASSES = D // (P * PACK)
 RUN = 8
-ROW = 8
+ROW = 127
 HOME = 96
 COLS = N // 16
 
@@ -33,7 +33,6 @@ def tile_attend_rel2_cap_kb_pgb2q128n512t2048_kernel(
     nc = tc.nc
     with ExitStack() as ctx:
         sb = ctx.enter_context(tc.tile_pool(name="sb", bufs=1))
-        reuse = ctx.enter_context(tc.tile_pool(name="reuse", bufs=1))
         ps = ctx.enter_context(tc.psum_pool(name="ps", bufs=1))
 
         def placed(ap):
@@ -45,31 +44,35 @@ def tile_attend_rel2_cap_kb_pgb2q128n512t2048_kernel(
         offsets = sb.tile([P, B * COLS], U16, name="offsets")
         nc.sync.dma_start(offsets[:], offs)
 
-        v_raw = sb.tile([P, T], F32, name="v_raw")
-        nc.scalar.dma_start(v_raw[:], vT)
-        kw_pool = reuse.tile([P, T], I32, name="kw_pool", offset=0)
-        nc.scalar.dma_start(kw_pool[:], k_words[0].rearrange("p t r -> p (t r)").bitcast(I32))
-
         ks_pool = sb.tile([P, T // 4], I32, name="ks_pool")
         nc.sync.dma_start(ks_pool[HOME:P, :], k_scales.rearrange("o f t -> (o f) t").bitcast(I32))
         nc.vector.memset(ks_pool[0:HOME, :], 0)
+
+        kb_pool = sb.tile([P, T], F32, name="kb_pool")
+        nc.sync.dma_start(kb_pool[ROW : ROW + 1, :], kb[0:1, :])
+        nc.vector.memset(kb_pool[0:ROW, :], 0.0)
+
+        v_raw = [sb.tile([P, T // 2], F32, name=f"v_raw{h}") for h in range(2)]
+        for h in range(2):
+            nc.sync.dma_start(v_raw[h][:], vT[:, h * (T // 2) : (h + 1) * (T // 2)])
 
         seed = sb.tile([P, 1], F32, name="seed")
         nc.gpsimd.memset(seed[:], 0.0)
         warm = sb.tile([P, 1], F32, name="warm")
         nc.scalar.activation(warm[:], seed[:], ACT.Tanh)
 
+        qw = sb.tile([P, B * PASSES, NQ], I32, name="qw", align_bytes=64)
+        nc.sync.dma_start(qw[:], q_words.rearrange("b o g q r -> g (b o) (q r)").bitcast(I32))
         qs = sb.tile([P, B * PASSES, NQ // 4], I32, name="qs", align_bytes=64)
         nc.gpsimd.memset(qs[:], 0)
+        kw_pool = sb.tile([P, T], I32, name="kw_pool")
         for row in range(4):
+            if row == 2:
+                nc.sync.dma_start(kw_pool[:], k_words[0].rearrange("p t r -> p (t r)").bitcast(I32))
             nc.sync.dma_start(
                 qs[row:P:32, :, :],
                 q_scales[:, :, row:16:4, :].rearrange("b o f q -> f (b o) q").bitcast(I32),
             )
-
-        kb_pool = reuse.tile([P, T], F32, name="kb_pool", offset=4 * T)
-        nc.vector.memset(kb_pool[:], 0.0)
-        nc.sync.dma_start(kb_pool[ROW : ROW + 1, :], kb[0:1, :])
 
         ident = sb.tile([P, P], F32, name="ident")
         make_identity(nc, ident[:])
@@ -77,23 +80,18 @@ def tile_attend_rel2_cap_kb_pgb2q128n512t2048_kernel(
         nc.scalar.copy(ident_bf[:], ident[:])
 
         ksg = sb.tile([P, PASSES, B * N // 4], I32, name="ksg", align_bytes=64)
-        nc.gpsimd.memset(ksg[:], 0)
-        qw = sb.tile([P, B * PASSES, NQ], I32, name="qw", align_bytes=64)
-        nc.gpsimd.dma_start(qw[:], q_words.rearrange("b o g q r -> g (b o) (q r)").bitcast(I32))
-        vs_pool = sb.tile([P, T], F32, name="vs_pool")
-        nc.gpsimd.memset(vs_pool[:], 0.0)
-        nc.gpsimd.dma_start(vs_pool[ROW : ROW + 1, :], vs[0:1, :])
+        nc.vector.memset(ksg[:], 0)
 
         lists = [offsets[:, b * COLS : (b + 1) * COLS] for b in range(B)]
 
-        def turn(src, tag, name, dtype=F32, first=0, step=P):
+        def turn(src, tag, name, dtype=F32):
             bank = ps.tile([P, PACK, P], dtype, name=name, tag=tag)
             unit = ident if dtype == F32 else ident_bf
             for j in range(PACK):
-                nc.tensor.transpose(bank[:, j, :], src[:, first + j * step : first + j * step + P], unit[:])
+                nc.tensor.transpose(bank[:, j, :], src[:, j * P : (j + 1) * P], unit[:])
             return bank
 
-        ksl = sb.tile([P, B * N], U8, name="ksl")
+        ksl = sb.tile([P, B * N], U8, name="ksl", tag="ksl")
         nc.vector.tensor_copy(ksl[:], ks_pool[:].bitcast(U8).indirect(offsets[:]))
         ksr = sb.tile([P, B * N // 4], I32, name="ksr")
         nc.vector.tensor_copy(
@@ -104,34 +102,47 @@ def tile_attend_rel2_cap_kb_pgb2q128n512t2048_kernel(
             for quad in range(4):
                 first = HOME + 16 * o + 4 * quad
                 nc.sync.dma_start(ksg[32 * quad : 32 * quad + 4, o, :], ksr[first : first + 4, :])
+        vs_pool = sb.tile([P, T], F32, name="vs_pool", tag="ksl")
+        nc.sync.dma_start(vs_pool[:], vs)
 
-        kbg = sb.tile([P, B * N], F32, name="kbg")
-        nc.vector.tensor_copy(placed(kbg[:].bitcast(U32)), kb_pool[:].bitcast(U32).indirect(offsets[:]))
+        kbT = []
+        for b in range(B):
+            kbg = sb.tile([P, N], F32, name=f"kbg{b}")
+            nc.vector.tensor_copy(placed(kbg[:].bitcast(U32)), kb_pool[:].bitcast(U32).indirect(lists[b]))
+            kbT.append(turn(kbg, f"a{b}", f"kbT{b}"))
 
         v_pool = sb.tile([P, T], BF16, name="v_pool")
-        nc.scalar.activation(v_pool[:], v_raw[:], ACT.Copy)
+        for h in range(2):
+            nc.scalar.activation(v_pool[:, h * (T // 2) : (h + 1) * (T // 2)], v_raw[h][:], ACT.Copy)
         vq = []
         for b in range(B):
-            vg = sb.tile([P, N], BF16, name=f"vg{b}")
+            vg = sb.tile([P, N], BF16, name=f"vg{b}", tag=f"vg{b}")
             nc.scalar.activation(placed(vg[:]), v_pool[:].indirect(lists[b]), ACT.Copy)
             vt = turn(vg, f"v{b}", f"vt{b}", BF16)
             vi = sb.tile([P, DV, PACK], BF16, name=f"vi{b}", align_bytes=64)
             nc.scalar.copy(vi[:], vt[:].rearrange("p j e -> p e j"))
             vq.append(vi)
-
-        ps_p = []
+        biases = []
         for b in range(B):
-            kwg = reuse.tile([P, N], U32, name=f"kwg{b}", tag="kwg", offset=4 * T)
-            nc.vector.tensor_copy(kwg[:], kw_pool[:].bitcast(U32).indirect(lists[b]))
-            kp = sb.tile([P, PASSES, 2 * N], U8, name=f"kp{b}", align_bytes=64)
-            nc.vector.tensor_copy(
-                kp[:].bitcast(U16).rearrange("p o (j f i) -> p o j f i", j=PACK, i=RUN),
-                kwg[:].bitcast(U16).rearrange("p (f j i o) -> p o j f i", j=PACK, i=RUN, o=PASSES),
-            )
+            bias = sb.tile([P, PACK], F32, name=f"bias{b}", tag=f"vg{b}")
+            nc.scalar.activation(bias[:], kbT[b][:, :, ROW], ACT.Copy, scale=1.0 / CAP)
+            biases.append(bias)
 
-            kbT = turn(kbg, f"a{b}", f"kbT{b}", F32, b * P, B * P)
-            bias = sb.tile([P, PACK], F32, name=f"bias{b}")
-            nc.scalar.activation(bias[:], kbT[:, :, ROW], ACT.Copy, scale=1.0 / CAP)
+        sq = []
+        for b in range(B):
+            bias = biases[b]
+            kp = sb.tile([P, PASSES, 2 * N], U8, name=f"kp{b}", align_bytes=64)
+            halves = []
+            for h in range(2):
+                kwg = sb.tile([P, N // 2], U32, name=f"kwg{b}{h}", tag=f"half{h}", align_bytes=64)
+                first = b * COLS + h * (COLS // 2)
+                nc.vector.tensor_copy(kwg[:], kw_pool[:].bitcast(U32).indirect(offsets[:, first : first + COLS // 2]))
+                halves.append(kwg)
+            for h in range(2):
+                nc.vector.tensor_copy(
+                    kp[:].bitcast(U16).rearrange("p o (j f i) -> p o j f i", j=PACK, i=RUN)[:, :, :, 8 * h : 8 * h + 8, :],
+                    halves[h][:].bitcast(U16).rearrange("p (f j i o) -> p o j f i", j=PACK, i=RUN, o=PASSES),
+                )
 
             scores = [ps.tile([P, 2, NQ], F32, name=f"scores{b}{h}", tag=f"s{b}{h}") for h in range(2)]
             for j in range(PACK):
@@ -145,39 +156,22 @@ def tile_attend_rel2_cap_kb_pgb2q128n512t2048_kernel(
                         start=(o == 0),
                         stop=(o == PASSES - 1),
                     )
-            if b in (1,):
-                t = sb.tile([P, N], F32, name=f"t{b}")
-                for j in range(PACK):
-                    nc.scalar.activation(
-                        t[:, j * NQ : (j + 1) * NQ], scores[j // 2][:, j % 2, :], ACT.Tanh, bias=bias[:, j : j + 1], scale=1.0 / CAP
-                    )
-                ps_p.append(t)
-                continue
             x = sb.tile([P, N], F32, name=f"x{b}")
             for j in range(PACK):
                 nc.scalar.activation(
                     x[:, j * NQ : (j + 1) * NQ], scores[j // 2][:, j % 2, :], ACT.Relu, bias=bias[:, j : j + 1], scale=1.0 / CAP
                 )
-            r = sb.tile([P, N], F32, name=f"r{b}")
+            r = sb.tile([P, N], F32, name=f"r{b}", tag=f"r{b}")
             nc.scalar.activation(r[:], x[:], ACT.Tanh)
             p = sb.tile([P, N], F32, name=f"p{b}")
             nc.scalar.activation(p[:], r[:], ACT.Square)
-            ps_p.append(p)
+            sq.append(p)
 
         vsT = []
         for b in range(B):
-            vsg = reuse.tile([P, N], F32, name=f"vsg{b}", offset=4 * T - 2 * N + 4 * N * b)
+            vsg = sb.tile([P, N], F32, name=f"vsg{b}", tag=f"half{b}", align_bytes=64)
             nc.vector.tensor_copy(placed(vsg[:].bitcast(U32)), vs_pool[:].bitcast(U32).indirect(lists[b]))
-            vsT.append(turn(vsg, f"s0{b}", f"vsT{b}"))
-
-        sq = []
-        for b in range(B):
-            if b in (1,):
-                p = sb.tile([P, N], F32, name=f"p{b}")
-                nc.vector.scalar_tensor_tensor(p[:], ps_p[b][:], 0.0, ps_p[b][:], ALU.max, ALU.mult)
-                sq.append(p)
-            else:
-                sq.append(ps_p[b])
+            vsT.append(turn(vsg, f"v{b}", f"vsT{b}"))
 
         for b in range(B):
             p = sq[b]
@@ -190,19 +184,19 @@ def tile_attend_rel2_cap_kb_pgb2q128n512t2048_kernel(
                 ALU.mult,
                 ALU.mult,
             )
-            vc = sb.tile([P, DV], U32, name=f"vc{b}", align_bytes=64)
+            vc = sb.tile([P, DV], U32, name=f"vc{b}", tag=f"half{b}", align_bytes=64)
             vsc = sb.tile([P, DV], U8, name=f"vsc{b}", align_bytes=64)
             nc.vector.quantize_mx(vc[:].bitcast(FP8X4), vsc[:], vq[b][:].rearrange("p e j -> p (e j)"))
             wc = sb.tile([P, NQ], U32, name=f"wc{b}", align_bytes=64)
             wsc = sb.tile([P, NQ], U8, name=f"wsc{b}", align_bytes=64)
             nc.vector.quantize_mx(wc[:].bitcast(FP8X4), wsc[:], w[:].rearrange("p q j -> p (q j)"))
 
-            pT = ps.tile([P, P], F32, name=f"pT{b}", tag=f"s1{b}")
+            pT = ps.tile([P, P], F32, name=f"pT{b}", tag=f"a{b}")
             for j in range(PACK):
                 nc.tensor.matmul(
                     pT[:], p[:, j * NQ : (j + 1) * NQ], ident[:], start=(j == 0), stop=(j == PACK - 1), is_transpose=True
                 )
-            junk = sb.tile([P, P], BF16, name=f"junk{b}")
+            junk = sb.tile([P, P], BF16, name=f"junk{b}", tag="r1")
             total = sb.tile([P, 1], F32, name=f"total{b}")
             nc.scalar.activation(
                 junk[:], pT[:], ACT.Copy, bias=1.0 / P, scale=CAP * CAP, accum_out=total[:]
@@ -210,7 +204,7 @@ def tile_attend_rel2_cap_kb_pgb2q128n512t2048_kernel(
             inv = sb.tile([P, 1], F32, name=f"inv{b}")
             nc.vector.reciprocal(inv[:], total[:])
 
-            y = ps.tile([P, DV], F32, name=f"y{b}", tag=f"a{b}")
+            y = ps.tile([P, DV], F32, name=f"y{b}", tag=f"s{b}0")
             nc.tensor.matmul_mx(
                 out=y[:], lhsT=wc[:].bitcast(FP8X4), lhsT_scale=wsc[:], rhs=vc[:].bitcast(FP8X4), rhs_scale=vsc[:],
                 start=True, stop=True,

@@ -91,7 +91,7 @@ def tile_attend_rel2_cap_kb_pgb2q128n512t2048_kernel(
                 nc.tensor.transpose(bank[:, j, :], src[:, j * P : (j + 1) * P], unit[:])
             return bank
 
-        ksl = sb.tile([P, B * N], U8, name="ksl", tag="ksl")
+        ksl = sb.tile([P, B * N], U8, name="ksl", tag="ksl", align_bytes=64)
         nc.vector.tensor_copy(ksl[:], ks_pool[:].bitcast(U8).indirect(offsets[:]))
         ksr = sb.tile([P, B * N // 4], I32, name="ksr")
         nc.vector.tensor_copy(
@@ -102,7 +102,7 @@ def tile_attend_rel2_cap_kb_pgb2q128n512t2048_kernel(
             for quad in range(4):
                 first = HOME + 16 * o + 4 * quad
                 nc.sync.dma_start(ksg[32 * quad : 32 * quad + 4, o, :], ksr[first : first + 4, :])
-        vs_pool = sb.tile([P, T], F32, name="vs_pool", tag="ksl")
+        vs_pool = sb.tile([P, T], F32, name="vs_pool", tag="ksl", align_bytes=64)
         nc.sync.dma_start(vs_pool[:], vs)
 
         kbT = []
@@ -156,22 +156,26 @@ def tile_attend_rel2_cap_kb_pgb2q128n512t2048_kernel(
                         start=(o == 0),
                         stop=(o == PASSES - 1),
                     )
-            x = sb.tile([P, N], F32, name=f"x{b}")
+            x = sb.tile([P, N], F32, name=f"x{b}", tag="x")
             for j in range(PACK):
                 nc.scalar.activation(
                     x[:, j * NQ : (j + 1) * NQ], scores[j // 2][:, j % 2, :], ACT.Relu, bias=bias[:, j : j + 1], scale=1.0 / CAP
                 )
             r = sb.tile([P, N], F32, name=f"r{b}", tag=f"r{b}")
             nc.scalar.activation(r[:], x[:], ACT.Tanh)
-            p = sb.tile([P, N], F32, name=f"p{b}")
-            nc.scalar.activation(p[:], r[:], ACT.Square)
-            sq.append(p)
+            if b == 0:
+                p = sb.tile([P, N], F32, name="p0")
+                nc.scalar.activation(p[:], r[:], ACT.Square)
+                sq.append(p)
 
         vsT = []
         for b in range(B):
             vsg = sb.tile([P, N], F32, name=f"vsg{b}", tag=f"half{b}", align_bytes=64)
             nc.vector.tensor_copy(placed(vsg[:].bitcast(U32)), vs_pool[:].bitcast(U32).indirect(lists[b]))
             vsT.append(turn(vsg, f"v{b}", f"vsT{b}"))
+        p = sb.tile([P, N], F32, name="p1", tag="half1", align_bytes=64)
+        nc.scalar.activation(p[:], r[:], ACT.Square)
+        sq.append(p)
 
         for b in range(B):
             p = sq[b]
@@ -184,14 +188,14 @@ def tile_attend_rel2_cap_kb_pgb2q128n512t2048_kernel(
                 ALU.mult,
                 ALU.mult,
             )
-            vc = sb.tile([P, DV], U32, name=f"vc{b}", tag=f"half{b}", align_bytes=64)
+            vc = sb.tile([P, DV], U32, name=f"vc{b}", tag=("half0", "ksl")[b], align_bytes=64)
             vsc = sb.tile([P, DV], U8, name=f"vsc{b}", align_bytes=64)
             nc.vector.quantize_mx(vc[:].bitcast(FP8X4), vsc[:], vq[b][:].rearrange("p e j -> p (e j)"))
             wc = sb.tile([P, NQ], U32, name=f"wc{b}", align_bytes=64)
             wsc = sb.tile([P, NQ], U8, name=f"wsc{b}", align_bytes=64)
             nc.vector.quantize_mx(wc[:].bitcast(FP8X4), wsc[:], w[:].rearrange("p q j -> p (q j)"))
 
-            pT = ps.tile([P, P], F32, name=f"pT{b}", tag=f"a{b}")
+            pT = ps.tile([P, P], F32, name=f"pT{b}", tag=("v0", "a1")[b])
             for j in range(PACK):
                 nc.tensor.matmul(
                     pT[:], p[:, j * NQ : (j + 1) * NQ], ident[:], start=(j == 0), stop=(j == PACK - 1), is_transpose=True

@@ -144,7 +144,7 @@ def tile_attend_rel2_cap_kb_pgb2q128n512t2048_kernel(
                     halves[h][:].bitcast(U16).rearrange("p (f j i o) -> p o j f i", j=PACK, i=RUN, o=PASSES),
                 )
 
-            scores = [ps.tile([P, 2, NQ], F32, name=f"scores{b}{h}", tag=f"s{b}{h}") for h in range(2)]
+            scores = [ps.tile([P, 2, NQ], F32, name=f"scores{b}{h}", tag=f"s{h}") for h in range(2)]
             for j in range(PACK):
                 for o in range(PASSES):
                     nc.tensor.matmul_mx(
@@ -208,7 +208,7 @@ def tile_attend_rel2_cap_kb_pgb2q128n512t2048_kernel(
             inv = sb.tile([P, 1], F32, name=f"inv{b}")
             nc.vector.reciprocal(inv[:], total[:])
 
-            y = ps.tile([P, DV], F32, name=f"y{b}", tag=f"s{b}0")
+            y = ps.tile([P, DV], F32, name=f"y{b}", tag=f"y{b}")
             nc.tensor.matmul_mx(
                 out=y[:], lhsT=wc[:].bitcast(FP8X4), lhsT_scale=wsc[:], rhs=vc[:].bitcast(FP8X4), rhs_scale=vsc[:],
                 start=True, stop=True,

@@ -103,7 +103,8 @@ def tile_attend_rel2_cap_kb_pgb2q128n512t2048_kernel(
                 first = HOME + 16 * o + 4 * quad
                 nc.sync.dma_start(ksg[32 * quad : 32 * quad + 4, o, :], ksr[first : first + 4, :])
         vs_pool = sb.tile([P, T], F32, name="vs_pool", tag="ksl", align_bytes=64)
-        nc.sync.dma_start(vs_pool[:], vs)
+        nc.sync.dma_start(vs_pool[ROW : ROW + 1, :], vs[0:1, :])
+        nc.gpsimd.memset(vs_pool[0:ROW, :], 0.0)
 
         kbT = []
         for b in range(B):

@@ -23,7 +23,6 @@ PACK = 4
 PASSES = D // (P * PACK)
 RUN = 8
 ROW = 127
-HOME = 96
 COLS = N // 16
 
 
@@ -45,12 +44,12 @@ def tile_attend_rel2_cap_kb_pgb2q128n512t2048_kernel(
         nc.sync.dma_start(offsets[:], offs)
 
         ks_pool = sb.tile([P, T // 4], I32, name="ks_pool")
-        nc.sync.dma_start(ks_pool[HOME:P, :], k_scales.rearrange("o f t -> (o f) t").bitcast(I32))
-        nc.vector.memset(ks_pool[0:HOME, :], 0)
+        nc.sync.dma_start(ks_pool[0:32, :], k_scales.rearrange("o f t -> (o f) t").bitcast(I32))
+        nc.vector.memset(ks_pool[64:P, :], 0)
+        nc.vector.memset(ks_pool[32:64, :], 0)
 
         kb_pool = sb.tile([P, T], F32, name="kb_pool")
         nc.sync.dma_start(kb_pool[ROW : ROW + 1, :], kb[0:1, :])
-        nc.vector.memset(kb_pool[0:ROW, :], 0.0)
 
         v_raw = [sb.tile([P, T // 2], F32, name=f"v_raw{h}") for h in range(2)]
         for h in range(2):
@@ -61,26 +60,27 @@ def tile_attend_rel2_cap_kb_pgb2q128n512t2048_kernel(
         warm = sb.tile([P, 1], F32, name="warm")
         nc.scalar.activation(warm[:], seed[:], ACT.Tanh)
 
-        qw = sb.tile([P, B * PASSES, NQ], I32, name="qw", align_bytes=64)
-        nc.sync.dma_start(qw[:], q_words.rearrange("b o g q r -> g (b o) (q r)").bitcast(I32))
         qs = sb.tile([P, B * PASSES, NQ // 4], I32, name="qs", align_bytes=64)
         nc.gpsimd.memset(qs[:], 0)
         kw_pool = sb.tile([P, T], I32, name="kw_pool")
         for row in range(4):
-            if row == 2:
+            if row == 3:
                 nc.sync.dma_start(kw_pool[:], k_words[0].rearrange("p t r -> p (t r)").bitcast(I32))
             nc.sync.dma_start(
                 qs[row:P:32, :, :],
                 q_scales[:, :, row:16:4, :].rearrange("b o f q -> f (b o) q").bitcast(I32),
             )
+        qw = sb.tile([P, B * PASSES, NQ], I32, name="qw", align_bytes=64)
+        nc.sync.dma_start(qw[:], q_words.rearrange("b o g q r -> g (b o) (q r)").bitcast(I32))
 
         ident = sb.tile([P, P], F32, name="ident")
         make_identity(nc, ident[:])
         ident_bf = sb.tile([P, P], BF16, name="ident_bf")
         nc.scalar.copy(ident_bf[:], ident[:])
 
-        ksg = sb.tile([P, PASSES, B * N // 4], I32, name="ksg", align_bytes=64)
-        nc.vector.memset(ksg[:], 0)
+        ks1 = sb.tile([P, B * N // 4], I32, name="ks1", align_bytes=64)
+        nc.gpsimd.memset(kb_pool[0:ROW, :], 0.0)
+        nc.vector.memset(ks1[:], 0)
 
         lists = [offsets[:, b * COLS : (b + 1) * COLS] for b in range(B)]
 
@@ -93,15 +93,17 @@ def tile_attend_rel2_cap_kb_pgb2q128n512t2048_kernel(
 
         ksl = sb.tile([P, B * N], U8, name="ksl", tag="ksl", align_bytes=64)
         nc.vector.tensor_copy(ksl[:], ks_pool[:].bitcast(U8).indirect(offsets[:]))
-        ksr = sb.tile([P, B * N // 4], I32, name="ksr")
+        ksr = sb.tile([P, B * N // 4], I32, name="ksr", align_bytes=64)
         nc.vector.tensor_copy(
             ksr[:].rearrange("p (j f w) -> p j f w", j=PACK, w=2),
             ksl[:].bitcast(I32).rearrange("p (f j w) -> p j f w", j=PACK, w=2),
         )
+        ksg = [ksr, ks1]
         for o in range(PASSES):
             for quad in range(4):
-                first = HOME + 16 * o + 4 * quad
-                nc.sync.dma_start(ksg[32 * quad : 32 * quad + 4, o, :], ksr[first : first + 4, :])
+                first = 16 * o + 4 * quad
+                if first > 0:
+                    nc.sync.dma_start(ksg[o][32 * quad : 32 * quad + 4, :], ksr[first : first + 4, :])
         vs_pool = sb.tile([P, T], F32, name="vs_pool", tag="ksl", align_bytes=64)
         nc.sync.dma_start(vs_pool[ROW : ROW + 1, :], vs[0:1, :])
         nc.gpsimd.memset(vs_pool[0:ROW, :], 0.0)
@@ -116,13 +118,18 @@ def tile_attend_rel2_cap_kb_pgb2q128n512t2048_kernel(
         for h in range(2):
             nc.scalar.activation(v_pool[:, h * (T // 2) : (h + 1) * (T // 2)], v_raw[h][:], ACT.Copy)
         vq = []
+        vts = []
         for b in range(B):
             vg = sb.tile([P, N], BF16, name=f"vg{b}", tag=f"vg{b}")
             nc.scalar.activation(placed(vg[:]), v_pool[:].indirect(lists[b]), ACT.Copy)
-            vt = turn(vg, f"v{b}", f"vt{b}", BF16)
-            vi = sb.tile([P, DV, PACK], BF16, name=f"vi{b}", align_bytes=64)
-            nc.scalar.copy(vi[:], vt[:].rearrange("p j e -> p e j"))
+            vts.append(turn(vg, f"v{b}", f"vt{b}", BF16))
+
+        def weave_v(b):
+            vi = sb.tile([P, DV, PACK], BF16, name=f"vi{b}", tag=("vi0", "r1")[b], align_bytes=64)
+            nc.scalar.copy(vi[:], vts[b][:].rearrange("p j e -> p e j"))
             vq.append(vi)
+
+        weave_v(0)
         biases = []
         for b in range(B):
             bias = sb.tile([P, PACK], F32, name=f"bias{b}", tag=f"vg{b}")
@@ -151,7 +158,7 @@ def tile_attend_rel2_cap_kb_pgb2q128n512t2048_kernel(
                     nc.tensor.matmul_mx(
                         out=scores[j // 2][:, j % 2, :],
                         lhsT=kp[:, o, 2 * P * j : 2 * P * (j + 1)].bitcast(FP4X4),
-                        lhsT_scale=ksg[:, o, :].bitcast(U8)[:, P * (B * j + b) : P * (B * j + b + 1)],
+                        lhsT_scale=ksg[o][:].bitcast(U8)[:, P * (B * j + b) : P * (B * j + b + 1)],
                         rhs=qw[:, b * PASSES + o, :].bitcast(FP8X4),
                         rhs_scale=qs[:, b * PASSES + o, :].bitcast(U8),
                         start=(o == 0),
@@ -162,21 +169,18 @@ def tile_attend_rel2_cap_kb_pgb2q128n512t2048_kernel(
                 nc.scalar.activation(
                     x[:, j * NQ : (j + 1) * NQ], scores[j // 2][:, j % 2, :], ACT.Relu, bias=bias[:, j : j + 1], scale=1.0 / CAP
                 )
-            r = sb.tile([P, N], F32, name=f"r{b}", tag=f"r{b}")
+            r = sb.tile([P, N], F32, name=f"r{b}", tag=f"r{b}", align_bytes=64)
             nc.scalar.activation(r[:], x[:], ACT.Tanh)
-            if b == 0:
-                p = sb.tile([P, N], F32, name="p0")
-                nc.scalar.activation(p[:], r[:], ACT.Square)
-                sq.append(p)
+            p = sb.tile([P, N], F32, name=f"p{b}")
+            nc.scalar.activation(p[:], r[:], ACT.Square)
+            sq.append(p)
+        weave_v(1)
 
         vsT = []
         for b in range(B):
             vsg = sb.tile([P, N], F32, name=f"vsg{b}", tag=f"half{b}", align_bytes=64)
             nc.vector.tensor_copy(placed(vsg[:].bitcast(U32)), vs_pool[:].bitcast(U32).indirect(lists[b]))
-            vsT.append(turn(vsg, f"v{b}", f"vsT{b}"))
-        p = sb.tile([P, N], F32, name="p1", tag="half1", align_bytes=64)
-        nc.scalar.activation(p[:], r[:], ACT.Square)
-        sq.append(p)
+            vsT.append(turn(vsg, ("v0", "y1")[b], f"vsT{b}"))
 
         for b in range(B):
             p = sq[b]
@@ -189,7 +193,7 @@ def tile_attend_rel2_cap_kb_pgb2q128n512t2048_kernel(
                 ALU.mult,
                 ALU.mult,
             )
-            vc = sb.tile([P, DV], U32, name=f"vc{b}", tag=("half0", "ksl")[b], align_bytes=64)
+            vc = sb.tile([P, DV], U32, name=f"vc{b}", tag=("half0", "vc1")[b], align_bytes=64)
             vsc = sb.tile([P, DV], U8, name=f"vsc{b}", align_bytes=64)
             nc.vector.quantize_mx(vc[:].bitcast(FP8X4), vsc[:], vq[b][:].rearrange("p e j -> p (e j)"))
             wc = sb.tile([P, NQ], U32, name=f"wc{b}", align_bytes=64)
@@ -201,7 +205,7 @@ def tile_attend_rel2_cap_kb_pgb2q128n512t2048_kernel(
                 nc.tensor.matmul(
                     pT[:], p[:, j * NQ : (j + 1) * NQ], ident[:], start=(j == 0), stop=(j == PACK - 1), is_transpose=True
                 )
-            junk = sb.tile([P, P], BF16, name=f"junk{b}", tag="r1")
+            junk = sb.tile([P, P], BF16, name=f"junk{b}", tag="x")
             total = sb.tile([P, 1], F32, name=f"total{b}")
             nc.scalar.activation(
                 junk[:], pT[:], ACT.Copy, bias=1.0 / P, scale=CAP * CAP, accum_out=total[:]

@@ -51,25 +51,22 @@ def tile_attend_rel2_cap_kb_pgb2q128n512t2048_kernel(
         kb_pool = sb.tile([P, T], F32, name="kb_pool")
         nc.sync.dma_start(kb_pool[ROW : ROW + 1, :], kb[0:1, :])
 
+        vs_pool = sb.tile([P, T], F32, name="vs_pool")
+        nc.sync.dma_start(vs_pool[ROW : ROW + 1, :], vs[0:1, :])
+
         v_raw = [sb.tile([P, T // 2], F32, name=f"v_raw{h}") for h in range(2)]
         for h in range(2):
             nc.sync.dma_start(v_raw[h][:], vT[:, h * (T // 2) : (h + 1) * (T // 2)])
-
-        seed = sb.tile([P, 1], F32, name="seed")
-        nc.gpsimd.memset(seed[:], 0.0)
-        warm = sb.tile([P, 1], F32, name="warm")
-        nc.scalar.activation(warm[:], seed[:], ACT.Tanh)
 
         qs = sb.tile([P, B * PASSES, NQ // 4], I32, name="qs", align_bytes=64)
         nc.gpsimd.memset(qs[:], 0)
         kw_pool = sb.tile([P, T], I32, name="kw_pool")
         for row in range(4):
-            if row == 3:
-                nc.sync.dma_start(kw_pool[:], k_words[0].rearrange("p t r -> p (t r)").bitcast(I32))
             nc.sync.dma_start(
                 qs[row:P:32, :, :],
                 q_scales[:, :, row:16:4, :].rearrange("b o f q -> f (b o) q").bitcast(I32),
             )
+        nc.sync.dma_start(kw_pool[:], k_words[0].rearrange("p t r -> p (t r)").bitcast(I32))
         qw = sb.tile([P, B * PASSES, NQ], I32, name="qw", align_bytes=64)
         nc.sync.dma_start(qw[:], q_words.rearrange("b o g q r -> g (b o) (q r)").bitcast(I32))
 
@@ -79,8 +76,9 @@ def tile_attend_rel2_cap_kb_pgb2q128n512t2048_kernel(
         nc.scalar.copy(ident_bf[:], ident[:])
 
         ks1 = sb.tile([P, B * N // 4], I32, name="ks1", align_bytes=64)
-        nc.gpsimd.memset(kb_pool[0:ROW, :], 0.0)
-        nc.vector.memset(ks1[:], 0)
+        nc.vector.memset(kb_pool[0:ROW, :], 0.0)
+        nc.vector.memset(vs_pool[0:ROW, :], 0.0)
+        nc.gpsimd.memset(ks1[:], 0)
 
         lists = [offsets[:, b * COLS : (b + 1) * COLS] for b in range(B)]
 
@@ -104,9 +102,6 @@ def tile_attend_rel2_cap_kb_pgb2q128n512t2048_kernel(
                 first = 16 * o + 4 * quad
                 if first > 0:
                     nc.sync.dma_start(ksg[o][32 * quad : 32 * quad + 4, :], ksr[first : first + 4, :])
-        vs_pool = sb.tile([P, T], F32, name="vs_pool", tag="ksl", align_bytes=64)
-        nc.sync.dma_start(vs_pool[ROW : ROW + 1, :], vs[0:1, :])
-        nc.gpsimd.memset(vs_pool[0:ROW, :], 0.0)
 
         kbT = []
         for b in range(B):
@@ -114,6 +109,14 @@ def tile_attend_rel2_cap_kb_pgb2q128n512t2048_kernel(
             nc.vector.tensor_copy(placed(kbg[:].bitcast(U32)), kb_pool[:].bitcast(U32).indirect(lists[b]))
             kbT.append(turn(kbg, f"a{b}", f"kbT{b}"))
 
+        vsgs = []
+
+        def gather_vs(b):
+            vsg = sb.tile([P, N], F32, name=f"vsg{b}", tag=("vsg0", "half1")[b], align_bytes=64)
+            nc.vector.tensor_copy(placed(vsg[:].bitcast(U32)), vs_pool[:].bitcast(U32).indirect(lists[b]))
+            vsgs.append(vsg)
+
+        gather_vs(0)
         v_pool = sb.tile([P, T], BF16, name="v_pool")
         for h in range(2):
             nc.scalar.activation(v_pool[:, h * (T // 2) : (h + 1) * (T // 2)], v_raw[h][:], ACT.Copy)
@@ -152,11 +155,11 @@ def tile_attend_rel2_cap_kb_pgb2q128n512t2048_kernel(
                     halves[h][:].bitcast(U16).rearrange("p (f j i o) -> p o j f i", j=PACK, i=RUN, o=PASSES),
                 )
 
-            scores = [ps.tile([P, 2, NQ], F32, name=f"scores{b}{h}", tag=f"s{h}") for h in range(2)]
+            scores = [ps.tile([P, NQ], F32, name=f"scores{b}{j}", tag=("s0", "s1", "y0", "y1")[j]) for j in range(PACK)]
             for j in range(PACK):
                 for o in range(PASSES):
                     nc.tensor.matmul_mx(
-                        out=scores[j // 2][:, j % 2, :],
+                        out=scores[j][:],
                         lhsT=kp[:, o, 2 * P * j : 2 * P * (j + 1)].bitcast(FP4X4),
                         lhsT_scale=ksg[o][:].bitcast(U8)[:, P * (B * j + b) : P * (B * j + b + 1)],
                         rhs=qw[:, b * PASSES + o, :].bitcast(FP8X4),
@@ -167,20 +170,21 @@ def tile_attend_rel2_cap_kb_pgb2q128n512t2048_kernel(
             x = sb.tile([P, N], F32, name=f"x{b}", tag="x")
             for j in range(PACK):
                 nc.scalar.activation(
-                    x[:, j * NQ : (j + 1) * NQ], scores[j // 2][:, j % 2, :], ACT.Relu, bias=bias[:, j : j + 1], scale=1.0 / CAP
+                    x[:, j * NQ : (j + 1) * NQ], scores[j][:], ACT.Relu, bias=bias[:, j : j + 1], scale=1.0 / CAP
                 )
             r = sb.tile([P, N], F32, name=f"r{b}", tag=f"r{b}", align_bytes=64)
-            nc.scalar.activation(r[:], x[:], ACT.Tanh)
             p = sb.tile([P, N], F32, name=f"p{b}")
-            nc.scalar.activation(p[:], r[:], ACT.Square)
+            for h in range(2):
+                half = slice(h * N // 2, (h + 1) * N // 2)
+                nc.scalar.activation(r[:, half], x[:, half], ACT.Tanh)
+            for h in range(2):
+                half = slice(h * N // 2, (h + 1) * N // 2)
+                nc.scalar.activation(p[:, half], r[:, half], ACT.Square)
             sq.append(p)
         weave_v(1)
 
-        vsT = []
-        for b in range(B):
-            vsg = sb.tile([P, N], F32, name=f"vsg{b}", tag=f"half{b}", align_bytes=64)
-            nc.vector.tensor_copy(placed(vsg[:].bitcast(U32)), vs_pool[:].bitcast(U32).indirect(lists[b]))
-            vsT.append(turn(vsg, ("v0", "y1")[b], f"vsT{b}"))
+        gather_vs(1)
+        vsT = [turn(vsgs[b], ("v0", "s0")[b], f"vsT{b}") for b in range(B)]
 
         for b in range(B):
             p = sq[b]
@@ -193,14 +197,14 @@ def tile_attend_rel2_cap_kb_pgb2q128n512t2048_kernel(
                 ALU.mult,
                 ALU.mult,
             )
-            vc = sb.tile([P, DV], U32, name=f"vc{b}", tag=("half0", "vc1")[b], align_bytes=64)
+            vc = sb.tile([P, DV], U32, name=f"vc{b}", tag=("half1", "vc1")[b], align_bytes=64)
             vsc = sb.tile([P, DV], U8, name=f"vsc{b}", align_bytes=64)
             nc.vector.quantize_mx(vc[:].bitcast(FP8X4), vsc[:], vq[b][:].rearrange("p e j -> p (e j)"))
             wc = sb.tile([P, NQ], U32, name=f"wc{b}", align_bytes=64)
             wsc = sb.tile([P, NQ], U8, name=f"wsc{b}", align_bytes=64)
             nc.vector.quantize_mx(wc[:].bitcast(FP8X4), wsc[:], w[:].rearrange("p q j -> p (q j)"))
 
-            pT = ps.tile([P, P], F32, name=f"pT{b}", tag=("v0", "a1")[b])
+            pT = ps.tile([P, P], F32, name=f"pT{b}", tag=("s1", "a1")[b])
             for j in range(PACK):
                 nc.tensor.matmul(
                     pT[:], p[:, j * NQ : (j + 1) * NQ], ident[:], start=(j == 0), stop=(j == PACK - 1), is_transpose=True

@@ -76,9 +76,10 @@ def tile_attend_rel2_cap_kb_pgb2q128n512t2048_kernel(
         nc.scalar.copy(ident_bf[:], ident[:])
 
         ks1 = sb.tile([P, B * N // 4], I32, name="ks1", align_bytes=64)
+        nc.vector.memset(ks1[:], 0)
         nc.vector.memset(kb_pool[0:ROW, :], 0.0)
-        nc.vector.memset(vs_pool[0:ROW, :], 0.0)
-        nc.gpsimd.memset(ks1[:], 0)
+        nc.vector.memset(vs_pool[0:ROW, 0 : T // 2], 0.0)
+        nc.gpsimd.memset(vs_pool[0:ROW, T // 2 - RUN : T], 0.0)
 
         lists = [offsets[:, b * COLS : (b + 1) * COLS] for b in range(B)]
 

@@ -24,6 +24,7 @@ PASSES = D // (P * PACK)
 RUN = 8
 ROW = 127
 COLS = N // 16
+V_CUTS = ((0, 512), (512, 1280), (1280, 2048))
 
 
 def tile_attend_rel2_cap_kb_pgb2q128n512t2048_kernel(
@@ -36,9 +37,6 @@ def tile_attend_rel2_cap_kb_pgb2q128n512t2048_kernel(
 
         def placed(ap):
             return ap.rearrange("p (j f i) -> p f j i", j=PACK, i=RUN)
-
-        def listed(ap):
-            return ap.rearrange("p (f j i) -> p f j i", j=PACK, i=RUN)
 
         offsets = sb.tile([P, B * COLS], U16, name="offsets")
         nc.sync.dma_start(offsets[:], offs)
@@ -54,9 +52,9 @@ def tile_attend_rel2_cap_kb_pgb2q128n512t2048_kernel(
         vs_pool = sb.tile([P, T], F32, name="vs_pool")
         nc.sync.dma_start(vs_pool[ROW : ROW + 1, :], vs[0:1, :])
 
-        v_raw = [sb.tile([P, T // 2], F32, name=f"v_raw{h}") for h in range(2)]
-        for h in range(2):
-            nc.sync.dma_start(v_raw[h][:], vT[:, h * (T // 2) : (h + 1) * (T // 2)])
+        v_raw = [sb.tile([P, hi - lo], F32, name=f"v_raw{lo}") for lo, hi in V_CUTS]
+        for h, (lo, hi) in enumerate(V_CUTS):
+            nc.sync.dma_start(v_raw[h][:], vT[:, lo:hi])
 
         qs = sb.tile([P, B * PASSES, NQ // 4], I32, name="qs", align_bytes=64)
         nc.gpsimd.memset(qs[:], 0)
@@ -66,9 +64,9 @@ def tile_attend_rel2_cap_kb_pgb2q128n512t2048_kernel(
                 qs[row:P:32, :, :],
                 q_scales[:, :, row:16:4, :].rearrange("b o f q -> f (b o) q").bitcast(I32),
             )
-        nc.sync.dma_start(kw_pool[:], k_words[0].rearrange("p t r -> p (t r)").bitcast(I32))
         qw = sb.tile([P, B * PASSES, NQ], I32, name="qw", align_bytes=64)
         nc.sync.dma_start(qw[:], q_words.rearrange("b o g q r -> g (b o) (q r)").bitcast(I32))
+        nc.sync.dma_start(kw_pool[:], k_words[0].rearrange("p t r -> p (t r)").bitcast(I32))
 
         ident = sb.tile([P, P], F32, name="ident")
         make_identity(nc, ident[:])
@@ -113,15 +111,15 @@ def tile_attend_rel2_cap_kb_pgb2q128n512t2048_kernel(
         vsgs = []
 
         def gather_vs(b):
-            vsg = sb.tile([P, N], F32, name=f"vsg{b}", tag=("vsg0", "half1")[b], align_bytes=64)
+            vsg = sb.tile([P, N], F32, name=f"vsg{b}", tag=("vsg0", "half0")[b], align_bytes=64)
             nc.vector.tensor_copy(placed(vsg[:].bitcast(U32)), vs_pool[:].bitcast(U32).indirect(lists[b]))
             vsgs.append(vsg)
 
         gather_vs(0)
         v_pool = sb.tile([P, T], BF16, name="v_pool")
-        for h in range(2):
-            nc.scalar.activation(v_pool[:, h * (T // 2) : (h + 1) * (T // 2)], v_raw[h][:], ACT.Copy)
-        vq = []
+        for h, (lo, hi) in enumerate(V_CUTS):
+            nc.scalar.activation(v_pool[:, lo:hi], v_raw[h][:], ACT.Copy)
+        vi = sb.tile([P, B, DV, PACK], BF16, name="vi", align_bytes=64)
         vts = []
         for b in range(B):
             vg = sb.tile([P, N], BF16, name=f"vg{b}", tag=f"vg{b}")
@@ -129,9 +127,7 @@ def tile_attend_rel2_cap_kb_pgb2q128n512t2048_kernel(
             vts.append(turn(vg, f"v{b}", f"vt{b}", BF16))
 
         def weave_v(b):
-            vi = sb.tile([P, DV, PACK], BF16, name=f"vi{b}", tag=("vi0", "r1")[b], align_bytes=64)
-            nc.scalar.copy(vi[:], vts[b][:].rearrange("p j e -> p e j"))
-            vq.append(vi)
+            nc.scalar.copy(vi[:, b, :, :], vts[b][:].rearrange("p j e -> p e j"))
 
         weave_v(0)
         biases = []
@@ -139,6 +135,7 @@ def tile_attend_rel2_cap_kb_pgb2q128n512t2048_kernel(
             bias = sb.tile([P, PACK], F32, name=f"bias{b}", tag=f"vg{b}")
             nc.scalar.activation(bias[:], kbT[b][:, :, ROW], ACT.Copy, scale=1.0 / CAP)
             biases.append(bias)
+        weave_v(1)
 
         sq = []
         for b in range(B):
@@ -158,15 +155,15 @@ def tile_attend_rel2_cap_kb_pgb2q128n512t2048_kernel(
 
             scores = [ps.tile([P, NQ], F32, name=f"scores{b}{j}", tag=("s0", "s1", "y0", "y1")[j]) for j in range(PACK)]
             for j in range(PACK):
-                for o in range(PASSES):
+                for o in reversed(range(PASSES)):
                     nc.tensor.matmul_mx(
                         out=scores[j][:],
                         lhsT=kp[:, o, 2 * P * j : 2 * P * (j + 1)].bitcast(FP4X4),
                         lhsT_scale=ksg[o][:].bitcast(U8)[:, P * (B * j + b) : P * (B * j + b + 1)],
                         rhs=qw[:, b * PASSES + o, :].bitcast(FP8X4),
                         rhs_scale=qs[:, b * PASSES + o, :].bitcast(U8),
-                        start=(o == 0),
-                        stop=(o == PASSES - 1),
+                        start=(o == PASSES - 1),
+                        stop=(o == 0),
                     )
             x = sb.tile([P, N], F32, name=f"x{b}", tag="x")
             for j in range(PACK):
@@ -182,10 +179,13 @@ def tile_attend_rel2_cap_kb_pgb2q128n512t2048_kernel(
                 half = slice(h * N // 2, (h + 1) * N // 2)
                 nc.scalar.activation(p[:, half], r[:, half], ACT.Square)
             sq.append(p)
-        weave_v(1)
 
         gather_vs(1)
         vsT = [turn(vsgs[b], ("v0", "s0")[b], f"vsT{b}") for b in range(B)]
+
+        vc = sb.tile([P, B * DV], U32, name="vc", tag="half1", align_bytes=64)
+        vsc = sb.tile([P, B * DV], U8, name="vsc", align_bytes=64)
+        nc.vector.quantize_mx(vc[:].bitcast(FP8X4), vsc[:], vi[:].rearrange("p b e j -> p (b e j)"))
 
         for b in range(B):
             p = sq[b]
@@ -198,9 +198,6 @@ def tile_attend_rel2_cap_kb_pgb2q128n512t2048_kernel(
                 ALU.mult,
                 ALU.mult,
             )
-            vc = sb.tile([P, DV], U32, name=f"vc{b}", tag=("half1", "vc1")[b], align_bytes=64)
-            vsc = sb.tile([P, DV], U8, name=f"vsc{b}", align_bytes=64)
-            nc.vector.quantize_mx(vc[:].bitcast(FP8X4), vsc[:], vq[b][:].rearrange("p e j -> p (e j)"))
             wc = sb.tile([P, NQ], U32, name=f"wc{b}", align_bytes=64)
             wsc = sb.tile([P, NQ], U8, name=f"wsc{b}", align_bytes=64)
             nc.vector.quantize_mx(wc[:].bitcast(FP8X4), wsc[:], w[:].rearrange("p q j -> p (q j)"))
@@ -220,7 +217,8 @@ def tile_attend_rel2_cap_kb_pgb2q128n512t2048_kernel(
 
             y = ps.tile([P, DV], F32, name=f"y{b}", tag=f"y{b}")
             nc.tensor.matmul_mx(
-                out=y[:], lhsT=wc[:].bitcast(FP8X4), lhsT_scale=wsc[:], rhs=vc[:].bitcast(FP8X4), rhs_scale=vsc[:],
+                out=y[:], lhsT=wc[:].bitcast(FP8X4), lhsT_scale=wsc[:],
+                rhs=vc[:, b * DV : (b + 1) * DV].bitcast(FP8X4), rhs_scale=vsc[:, b * DV : (b + 1) * DV],
                 start=True, stop=True,
             )
             res = sb.tile([P, DV], F32, name=f"res{b}")

@@ -49,9 +49,6 @@ def tile_attend_rel2_cap_kb_pgb2q128n512t2048_kernel(
         kb_pool = sb.tile([P, T], F32, name="kb_pool")
         nc.sync.dma_start(kb_pool[ROW : ROW + 1, :], kb[0:1, :])
 
-        vs_pool = sb.tile([P, T], F32, name="vs_pool")
-        nc.sync.dma_start(vs_pool[ROW : ROW + 1, :], vs[0:1, :])
-
         v_raw = [sb.tile([P, hi - lo], F32, name=f"v_raw{lo}") for lo, hi in V_CUTS]
         for h, (lo, hi) in enumerate(V_CUTS):
             nc.sync.dma_start(v_raw[h][:], vT[:, lo:hi])
@@ -65,8 +62,8 @@ def tile_attend_rel2_cap_kb_pgb2q128n512t2048_kernel(
                 q_scales[:, :, row:16:4, :].rearrange("b o f q -> f (b o) q").bitcast(I32),
             )
         qw = sb.tile([P, B * PASSES, NQ], I32, name="qw", align_bytes=64)
-        nc.sync.dma_start(qw[:], q_words.rearrange("b o g q r -> g (b o) (q r)").bitcast(I32))
         nc.sync.dma_start(kw_pool[:], k_words[0].rearrange("p t r -> p (t r)").bitcast(I32))
+        nc.sync.dma_start(qw[:], q_words.rearrange("b o g q r -> g (b o) (q r)").bitcast(I32))
 
         ident = sb.tile([P, P], F32, name="ident")
         make_identity(nc, ident[:])
@@ -76,8 +73,6 @@ def tile_attend_rel2_cap_kb_pgb2q128n512t2048_kernel(
         ks1 = sb.tile([P, B * N // 4], I32, name="ks1", align_bytes=64)
         nc.vector.memset(ks1[:], 0)
         nc.vector.memset(kb_pool[0:ROW, :], 0.0)
-        nc.vector.memset(vs_pool[0:ROW, 0 : T // 2], 0.0)
-        nc.gpsimd.memset(vs_pool[0:ROW, T // 2 - RUN : T], 0.0)
 
         lists = [offsets[:, b * COLS : (b + 1) * COLS] for b in range(B)]
 
@@ -102,6 +97,9 @@ def tile_attend_rel2_cap_kb_pgb2q128n512t2048_kernel(
                 if first > 0:
                     nc.sync.dma_start(ksg[o][32 * quad : 32 * quad + 4, :], ksr[first : first + 4, :])
 
+        vs_pool = sb.tile([P, T], F32, name="vs_pool", tag="ksl", align_bytes=64)
+        nc.sync.dma_start(vs_pool[:], vs)
+
         kbT = []
         for b in range(B):
             kbg = sb.tile([P, N], F32, name=f"kbg{b}")
@@ -111,11 +109,10 @@ def tile_attend_rel2_cap_kb_pgb2q128n512t2048_kernel(
         vsgs = []
 
         def gather_vs(b):
-            vsg = sb.tile([P, N], F32, name=f"vsg{b}", tag=("vsg0", "half0")[b], align_bytes=64)
+            vsg = sb.tile([P, N], F32, name=f"vsg{b}", tag=("half0", "vsg1")[b], align_bytes=64)
             nc.vector.tensor_copy(placed(vsg[:].bitcast(U32)), vs_pool[:].bitcast(U32).indirect(lists[b]))
             vsgs.append(vsg)
 
-        gather_vs(0)
         v_pool = sb.tile([P, T], BF16, name="v_pool")
         for h, (lo, hi) in enumerate(V_CUTS):
             nc.scalar.activation(v_pool[:, lo:hi], v_raw[h][:], ACT.Copy)
@@ -180,8 +177,9 @@ def tile_attend_rel2_cap_kb_pgb2q128n512t2048_kernel(
                 nc.scalar.activation(p[:, half], r[:, half], ACT.Square)
             sq.append(p)
 
+        gather_vs(0)
         gather_vs(1)
-        vsT = [turn(vsgs[b], ("v0", "s0")[b], f"vsT{b}") for b in range(B)]
+        vsT = [turn(vsgs[b], ("s0", "a0")[b], f"vsT{b}") for b in range(B)]
 
         vc = sb.tile([P, B * DV], U32, name="vc", tag="half1", align_bytes=64)
         vsc = sb.tile([P, B * DV], U8, name="vsc", align_bytes=64)

@@ -24,7 +24,7 @@ PASSES = D // (P * PACK)
 RUN = 8
 ROW = 127
 COLS = N // 16
-V_CUTS = ((0, 512), (512, 1280), (1280, 2048))
+V_CUTS = ((0, 768), (768, 1536), (1536, 2048))
 
 
 def tile_attend_rel2_cap_kb_pgb2q128n512t2048_kernel(
@@ -33,6 +33,7 @@ def tile_attend_rel2_cap_kb_pgb2q128n512t2048_kernel(
     nc = tc.nc
     with ExitStack() as ctx:
         sb = ctx.enter_context(tc.tile_pool(name="sb", bufs=1))
+        late = ctx.enter_context(tc.tile_pool(name="late", bufs=1))
         ps = ctx.enter_context(tc.psum_pool(name="ps", bufs=1))
 
         def placed(ap):
@@ -67,8 +68,6 @@ def tile_attend_rel2_cap_kb_pgb2q128n512t2048_kernel(
 
         ident = sb.tile([P, P], F32, name="ident")
         make_identity(nc, ident[:])
-        ident_bf = sb.tile([P, P], BF16, name="ident_bf")
-        nc.scalar.copy(ident_bf[:], ident[:])
 
         ks1 = sb.tile([P, B * N // 4], I32, name="ks1", align_bytes=64)
         nc.vector.memset(ks1[:], 0)
@@ -76,11 +75,10 @@ def tile_attend_rel2_cap_kb_pgb2q128n512t2048_kernel(
 
         lists = [offsets[:, b * COLS : (b + 1) * COLS] for b in range(B)]
 
-        def turn(src, tag, name, dtype=F32):
-            bank = ps.tile([P, PACK, P], dtype, name=name, tag=tag)
-            unit = ident if dtype == F32 else ident_bf
+        def turn(src, tag, name):
+            bank = ps.tile([P, PACK, P], F32, name=name, tag=tag)
             for j in range(PACK):
-                nc.tensor.transpose(bank[:, j, :], src[:, j * P : (j + 1) * P], unit[:])
+                nc.tensor.transpose(bank[:, j, :], src[:, j * P : (j + 1) * P], ident[:])
             return bank
 
         ksl = sb.tile([P, B * N], U8, name="ksl", tag="ksl", align_bytes=64)
@@ -116,23 +114,29 @@ def tile_attend_rel2_cap_kb_pgb2q128n512t2048_kernel(
         v_pool = sb.tile([P, T], BF16, name="v_pool")
         for h, (lo, hi) in enumerate(V_CUTS):
             nc.scalar.activation(v_pool[:, lo:hi], v_raw[h][:], ACT.Copy)
-        vi = sb.tile([P, B, DV, PACK], BF16, name="vi", align_bytes=64)
         vts = []
         for b in range(B):
             vg = sb.tile([P, N], BF16, name=f"vg{b}", tag=f"vg{b}")
-            nc.scalar.activation(placed(vg[:]), v_pool[:].indirect(lists[b]), ACT.Copy)
-            vts.append(turn(vg, f"v{b}", f"vt{b}", BF16))
+            nc.scalar.activation(
+                vg[:].rearrange("p (f i j) -> p f j i", j=PACK, i=RUN), v_pool[:].indirect(lists[b]), ACT.Copy
+            )
+            bank = ps.tile([P, 2, P], F32, name=f"vt{b}", tag=f"v{b}")
+            for u in range(2):
+                nc.tensor.transpose(bank[:, u, :], vg[:].bitcast(F32)[:, u : N // 2 : 2], ident[:])
+            vts.append(bank)
 
-        def weave_v(b):
-            nc.scalar.copy(vi[:, b, :, :], vts[b][:].rearrange("p j e -> p e j"))
+        def weave_v(b, vi):
+            nc.scalar.copy(
+                vi[:].bitcast(F32).rearrange("p (e u) -> p e u", u=2), vts[b][:].rearrange("p u e -> p e u")
+            )
 
-        weave_v(0)
+        vi0 = sb.tile([P, DV * PACK], BF16, name="vi0", align_bytes=64)
+        weave_v(0, vi0)
         biases = []
         for b in range(B):
             bias = sb.tile([P, PACK], F32, name=f"bias{b}", tag=f"vg{b}")
             nc.scalar.activation(bias[:], kbT[b][:, :, ROW], ACT.Copy, scale=1.0 / CAP)
             biases.append(bias)
-        weave_v(1)
 
         sq = []
         for b in range(B):
@@ -167,7 +171,7 @@ def tile_attend_rel2_cap_kb_pgb2q128n512t2048_kernel(
                 nc.scalar.activation(
                     x[:, j * NQ : (j + 1) * NQ], scores[j][:], ACT.Relu, bias=bias[:, j : j + 1], scale=1.0 / CAP
                 )
-            r = sb.tile([P, N], F32, name=f"r{b}", tag=f"r{b}", align_bytes=64)
+            r = late.tile([P, N], F32, name=f"r{b}", offset=4096 * b, align_bytes=64)
             p = sb.tile([P, N], F32, name=f"p{b}")
             for h in range(2):
                 half = slice(h * N // 2, (h + 1) * N // 2)
@@ -181,10 +185,18 @@ def tile_attend_rel2_cap_kb_pgb2q128n512t2048_kernel(
         gather_vs(1)
         vsT = [turn(vsgs[b], ("s0", "a0")[b], f"vsT{b}") for b in range(B)]
 
-        vc = sb.tile([P, B * DV], U32, name="vc", tag="half1", align_bytes=64)
-        vsc = sb.tile([P, B * DV], U8, name="vsc", align_bytes=64)
-        nc.vector.quantize_mx(vc[:].bitcast(FP8X4), vsc[:], vi[:].rearrange("p b e j -> p (b e j)"))
+        vi1 = late.tile([P, DV * PACK], BF16, name="vi1", offset=4096 + 1024, align_bytes=64)
+        weave_v(1, vi1)
 
+        def quantise(src, name, codes):
+            scales = sb.tile([P, P], U8, name=f"{name}_scales", align_bytes=64)
+            nc.vector.quantize_mx(codes[:].bitcast(FP8X4), scales[:], src)
+            return codes, scales
+
+        vq = [quantise(vi0[:], "v0", sb.tile([P, DV], U32, name="vc0", tag="half1", align_bytes=64))]
+
+        ws = []
+        totals = []
         for b in range(B):
             p = sq[b]
             w = sb.tile([P, NQ, PACK], BF16, name=f"w{b}", align_bytes=64)
@@ -196,10 +208,7 @@ def tile_attend_rel2_cap_kb_pgb2q128n512t2048_kernel(
                 ALU.mult,
                 ALU.mult,
             )
-            wc = sb.tile([P, NQ], U32, name=f"wc{b}", align_bytes=64)
-            wsc = sb.tile([P, NQ], U8, name=f"wsc{b}", align_bytes=64)
-            nc.vector.quantize_mx(wc[:].bitcast(FP8X4), wsc[:], w[:].rearrange("p q j -> p (q j)"))
-
+            ws.append(w)
             pT = ps.tile([P, P], F32, name=f"pT{b}", tag=("s1", "a1")[b])
             for j in range(PACK):
                 nc.tensor.matmul(
@@ -210,14 +219,32 @@ def tile_attend_rel2_cap_kb_pgb2q128n512t2048_kernel(
             nc.scalar.activation(
                 junk[:], pT[:], ACT.Copy, bias=1.0 / P, scale=CAP * CAP, accum_out=total[:]
             )
-            inv = sb.tile([P, 1], F32, name=f"inv{b}")
-            nc.vector.reciprocal(inv[:], total[:])
+            totals.append(total)
 
+        wq = [
+            quantise(
+                ws[0][:].rearrange("p q j -> p (q j)"),
+                "w0",
+                late.tile([P, NQ], U32, name="wc0", offset=4096, align_bytes=64),
+            )
+        ]
+        vq.append(quantise(vi1[:], "v1", sb.tile([P, DV], U32, name="vc1", align_bytes=64)))
+        wq.append(
+            quantise(ws[1][:].rearrange("p q j -> p (q j)"), "w1", sb.tile([P, NQ], U32, name="wc1", align_bytes=64))
+        )
+
+        for b in range(B):
+            inv = sb.tile([P, 1], F32, name=f"inv{b}")
+            nc.vector.reciprocal(inv[:], totals[b][:])
             y = ps.tile([P, DV], F32, name=f"y{b}", tag=f"y{b}")
             nc.tensor.matmul_mx(
-                out=y[:], lhsT=wc[:].bitcast(FP8X4), lhsT_scale=wsc[:],
-                rhs=vc[:, b * DV : (b + 1) * DV].bitcast(FP8X4), rhs_scale=vsc[:, b * DV : (b + 1) * DV],
-                start=True, stop=True,
+                out=y[:],
+                lhsT=wq[b][0][:].bitcast(FP8X4),
+                lhsT_scale=wq[b][1][:],
+                rhs=vq[b][0][:].bitcast(FP8X4),
+                rhs_scale=vq[b][1][:],
+                start=True,
+                stop=True,
             )
             res = sb.tile([P, DV], F32, name=f"res{b}")
             nc.scalar.activation(res[:], y[:], ACT.Copy, scale=inv[:])

@@ -21,10 +21,8 @@ ALU = mybir.AluOpType
 P = 128
 PACK = 4
 PASSES = D // (P * PACK)
-RUN = 8
 ROW = 127
 COLS = N // 16
-V_CUTS = ((0, 768), (768, 1536), (1536, 2048))
 
 
 def tile_attend_rel2_cap_kb_pgb2q128n512t2048_kernel(
@@ -33,216 +31,169 @@ def tile_attend_rel2_cap_kb_pgb2q128n512t2048_kernel(
     nc = tc.nc
     with ExitStack() as ctx:
         sb = ctx.enter_context(tc.tile_pool(name="sb", bufs=1))
-        late = ctx.enter_context(tc.tile_pool(name="late", bufs=1))
+        early = ctx.enter_context(tc.tile_pool(name="early", bufs=1))
         ps = ctx.enter_context(tc.psum_pool(name="ps", bufs=1))
 
-        def placed(ap):
-            return ap.rearrange("p (j f i) -> p f j i", j=PACK, i=RUN)
+        ident_room = early.tile([P, 8 * N], BF16, name="ident_room", offset=0)
+        ident_bf = ident_room[:, 0:P]
+        make_identity(nc, ident_bf)
+        ident = sb.tile([P, P], F32, name="ident")
+        nc.scalar.activation(ident[:], ident_bf, ACT.Copy)
 
         offsets = sb.tile([P, B * COLS], U16, name="offsets")
         nc.sync.dma_start(offsets[:], offs)
-
-        ks_pool = sb.tile([P, T // 4], I32, name="ks_pool")
-        nc.sync.dma_start(ks_pool[0:32, :], k_scales.rearrange("o f t -> (o f) t").bitcast(I32))
-        nc.vector.memset(ks_pool[64:P, :], 0)
-        nc.vector.memset(ks_pool[32:64, :], 0)
+        lists = [offsets[:, b * COLS : (b + 1) * COLS] for b in range(B)]
 
         kb_pool = sb.tile([P, T], F32, name="kb_pool")
         nc.sync.dma_start(kb_pool[ROW : ROW + 1, :], kb[0:1, :])
+        vs_pool = sb.tile([P, T], F32, name="vs_pool")
+        nc.sync.dma_start(vs_pool[ROW : ROW + 1, :], vs[0:1, :])
 
-        v_raw = [sb.tile([P, hi - lo], F32, name=f"v_raw{lo}") for lo, hi in V_CUTS]
-        for h, (lo, hi) in enumerate(V_CUTS):
-            nc.sync.dma_start(v_raw[h][:], vT[:, lo:hi])
+        ks_pool = sb.tile([P, T // 4], I32, name="ks_pool")
+        nc.vector.memset(ks_pool[:], 0)
+        nc.vector.memset(kb_pool[0:ROW, :], 0.0)
+        nc.vector.memset(vs_pool[0:ROW, :], 0.0)
+        by_parity = k_scales.rearrange("o (a h r) t -> h (o a) r t", h=2, r=4)
+        for h in range(2):
+            nc.sync.dma_start(ks_pool[32 * h : 32 * h + 16, :], by_parity[h].bitcast(I32))
+
+        kw_pool = sb.tile([P, T], I32, name="kw_pool")
+        nc.sync.dma_start(kw_pool[:], k_words[0].rearrange("p t r -> p (t r)").bitcast(I32))
+        qw = sb.tile([P, B * PASSES, NQ], I32, name="qw", align_bytes=64)
+        nc.sync.dma_start(qw[:], q_words.rearrange("b o g q r -> g (b o) (q r)").bitcast(I32))
+        v_pool = sb.tile([P, T], F32, name="v_pool")
+        nc.sync.dma_start(v_pool[:], vT)
 
         qs = sb.tile([P, B * PASSES, NQ // 4], I32, name="qs", align_bytes=64)
         nc.gpsimd.memset(qs[:], 0)
-        kw_pool = sb.tile([P, T], I32, name="kw_pool")
         for row in range(4):
             nc.sync.dma_start(
                 qs[row:P:32, :, :],
                 q_scales[:, :, row:16:4, :].rearrange("b o f q -> f (b o) q").bitcast(I32),
             )
-        qw = sb.tile([P, B * PASSES, NQ], I32, name="qw", align_bytes=64)
-        nc.sync.dma_start(kw_pool[:], k_words[0].rearrange("p t r -> p (t r)").bitcast(I32))
-        nc.sync.dma_start(qw[:], q_words.rearrange("b o g q r -> g (b o) (q r)").bitcast(I32))
 
-        ident = sb.tile([P, P], F32, name="ident")
-        make_identity(nc, ident[:])
-
-        ks1 = sb.tile([P, B * N // 4], I32, name="ks1", align_bytes=64)
-        nc.vector.memset(ks1[:], 0)
-        nc.vector.memset(kb_pool[0:ROW, :], 0.0)
-
-        lists = [offsets[:, b * COLS : (b + 1) * COLS] for b in range(B)]
-
-        def turn(src, tag, name):
-            bank = ps.tile([P, PACK, P], F32, name=name, tag=tag)
-            for j in range(PACK):
-                nc.tensor.transpose(bank[:, j, :], src[:, j * P : (j + 1) * P], ident[:])
-            return bank
-
-        ksl = sb.tile([P, B * N], U8, name="ksl", tag="ksl", align_bytes=64)
-        nc.vector.tensor_copy(ksl[:], ks_pool[:].bitcast(U8).indirect(offsets[:]))
-        ksr = sb.tile([P, B * N // 4], I32, name="ksr", align_bytes=64)
+        ksg = sb.tile([P, B * N], U8, name="ksg", align_bytes=64)
         nc.vector.tensor_copy(
-            ksr[:].rearrange("p (j f w) -> p j f w", j=PACK, w=2),
-            ksl[:].bitcast(I32).rearrange("p (f j w) -> p j f w", j=PACK, w=2),
+            ksg[:].rearrange("p (b j m) -> p b m j", b=B, j=PACK), ks_pool[:].bitcast(U8).indirect(offsets[:])
         )
-        ksg = [ksr, ks1]
+        planes = []
         for o in range(PASSES):
-            for quad in range(4):
-                first = 16 * o + 4 * quad
-                if first > 0:
-                    nc.sync.dma_start(ksg[o][32 * quad : 32 * quad + 4, :], ksr[first : first + 4, :])
+            plane = sb.tile([P, B * N // 4], I32, name=f"plane{o}", align_bytes=64)
+            for h in range(2):
+                first = 8 * o + 4 * h
+                nc.sync.dma_start(plane[64 * h : 64 * h + 64, :], ksg[:].bitcast(I32)[first : first + 64, :])
+            planes.append(plane[:].bitcast(U8))
 
-        vs_pool = sb.tile([P, T], F32, name="vs_pool", tag="ksl", align_bytes=64)
-        nc.sync.dma_start(vs_pool[:], vs)
-
-        kbT = []
-        for b in range(B):
-            kbg = sb.tile([P, N], F32, name=f"kbg{b}")
-            nc.vector.tensor_copy(placed(kbg[:].bitcast(U32)), kb_pool[:].bitcast(U32).indirect(lists[b]))
-            kbT.append(turn(kbg, f"a{b}", f"kbT{b}"))
-
-        vsgs = []
-
-        def gather_vs(b):
-            vsg = sb.tile([P, N], F32, name=f"vsg{b}", tag=("half0", "vsg1")[b], align_bytes=64)
-            nc.vector.tensor_copy(placed(vsg[:].bitcast(U32)), vs_pool[:].bitcast(U32).indirect(lists[b]))
-            vsgs.append(vsg)
-
-        v_pool = sb.tile([P, T], BF16, name="v_pool")
-        for h, (lo, hi) in enumerate(V_CUTS):
-            nc.scalar.activation(v_pool[:, lo:hi], v_raw[h][:], ACT.Copy)
-        vts = []
-        for b in range(B):
-            vg = sb.tile([P, N], BF16, name=f"vg{b}", tag=f"vg{b}")
-            nc.scalar.activation(
-                vg[:].rearrange("p (f i j) -> p f j i", j=PACK, i=RUN), v_pool[:].indirect(lists[b]), ACT.Copy
-            )
-            bank = ps.tile([P, 2, P], F32, name=f"vt{b}", tag=f"v{b}")
-            for u in range(2):
-                nc.tensor.transpose(bank[:, u, :], vg[:].bitcast(F32)[:, u : N // 2 : 2], ident[:])
-            vts.append(bank)
-
-        def weave_v(b, vi):
-            nc.scalar.copy(
-                vi[:].bitcast(F32).rearrange("p (e u) -> p e u", u=2), vts[b][:].rearrange("p u e -> p e u")
-            )
-
-        vi0 = sb.tile([P, DV * PACK], BF16, name="vi0", align_bytes=64)
-        weave_v(0, vi0)
         biases = []
         for b in range(B):
-            bias = sb.tile([P, PACK], F32, name=f"bias{b}", tag=f"vg{b}")
-            nc.scalar.activation(bias[:], kbT[b][:, :, ROW], ACT.Copy, scale=1.0 / CAP)
+            kbg = early.tile([P, N], F32, name=f"kbg{b}", offset=4 * N * b)
+            nc.scalar.activation(kbg[:], kb_pool[:].indirect(lists[b]), ACT.Copy)
+            bank = ps.tile([P, PACK, P], F32, name=f"kbT{b}", tag=f"a{b}")
+            for j in range(PACK):
+                nc.tensor.transpose(bank[:, j, :], kbg[:, j:N:PACK], ident[:])
+            bias = sb.tile([P, PACK], F32, name=f"bias{b}", tag=f"bias{b}")
+            nc.scalar.activation(bias[:], bank[:, :, ROW], ACT.Copy, scale=1.0 / CAP)
             biases.append(bias)
 
-        sq = []
+        vsp = []
         for b in range(B):
-            bias = biases[b]
+            vsg = early.tile([P, N], F32, name=f"vsg{b}", offset=4 * N * (B + b))
+            nc.scalar.activation(vsg[:], vs_pool[:].indirect(lists[b]), ACT.Copy)
+            col = sb.tile([P, PACK], F32, name=f"vsp{b}")
+            nc.sync.dma_start(col[:], vsg[ROW : ROW + 1, :].rearrange("o (p j) -> o p j", j=PACK))
+            vsp.append(col)
+
+        def turn_values(b, vg):
+            bank = ps.tile([P, 2, P], F32, name=f"vt{b}", tag=f"a{b}")
+            for u in range(2):
+                nc.tensor.transpose(bank[:, u, :], vg[:].bitcast(F32)[:, u : N // 2 : 2], ident[:])
+            vi = sb.tile([P, DV * PACK], BF16, name=f"vi{b}", align_bytes=64)
+            nc.scalar.copy(vi[:].bitcast(F32).rearrange("p (e u) -> p e u", u=2), bank[:].rearrange("p u e -> p e u"))
+            return vi
+
+        vg0 = sb.tile([P, N], BF16, name="vg0")
+        nc.scalar.activation(vg0[:], v_pool[:].indirect(lists[0]), ACT.Copy)
+
+        th = []
+        for b in range(B):
             kp = sb.tile([P, PASSES, 2 * N], U8, name=f"kp{b}", align_bytes=64)
             halves = []
             for h in range(2):
                 kwg = sb.tile([P, N // 2], U32, name=f"kwg{b}{h}", tag=f"half{h}", align_bytes=64)
                 first = b * COLS + h * (COLS // 2)
-                nc.vector.tensor_copy(kwg[:], kw_pool[:].bitcast(U32).indirect(offsets[:, first : first + COLS // 2]))
+                nc.vector.tensor_copy(
+                    kwg[:].rearrange("p (j m) -> p m j", j=PACK),
+                    kw_pool[:].bitcast(U32).indirect(offsets[:, first : first + COLS // 2]),
+                )
                 halves.append(kwg)
             for h in range(2):
                 nc.vector.tensor_copy(
-                    kp[:].bitcast(U16).rearrange("p o (j f i) -> p o j f i", j=PACK, i=RUN)[:, :, :, 8 * h : 8 * h + 8, :],
-                    halves[h][:].bitcast(U16).rearrange("p (f j i o) -> p o j f i", j=PACK, i=RUN, o=PASSES),
+                    kp[:].bitcast(U16).rearrange("p o (j m) -> p o j m", j=PACK)[:, :, :, 64 * h : 64 * h + 64],
+                    halves[h][:].bitcast(U16).rearrange("p (j m o) -> p o j m", j=PACK, o=PASSES),
                 )
 
-            scores = [ps.tile([P, NQ], F32, name=f"scores{b}{j}", tag=("s0", "s1", "y0", "y1")[j]) for j in range(PACK)]
+            t = sb.tile([P, N], F32, name=f"t{b}")
             for j in range(PACK):
-                for o in reversed(range(PASSES)):
+                score = ps.tile([P, NQ], F32, name=f"score{b}{j}", tag=f"s{j}")
+                for o in range(PASSES):
                     nc.tensor.matmul_mx(
-                        out=scores[j][:],
+                        out=score[:],
                         lhsT=kp[:, o, 2 * P * j : 2 * P * (j + 1)].bitcast(FP4X4),
-                        lhsT_scale=ksg[o][:].bitcast(U8)[:, P * (B * j + b) : P * (B * j + b + 1)],
+                        lhsT_scale=planes[o][:, P * (PACK * b + j) : P * (PACK * b + j + 1)],
                         rhs=qw[:, b * PASSES + o, :].bitcast(FP8X4),
                         rhs_scale=qs[:, b * PASSES + o, :].bitcast(U8),
-                        start=(o == PASSES - 1),
-                        stop=(o == 0),
+                        start=(o == 0),
+                        stop=(o == PASSES - 1),
                     )
-            x = sb.tile([P, N], F32, name=f"x{b}", tag="x")
-            for j in range(PACK):
                 nc.scalar.activation(
-                    x[:, j * NQ : (j + 1) * NQ], scores[j][:], ACT.Relu, bias=bias[:, j : j + 1], scale=1.0 / CAP
+                    t[:, j * NQ : (j + 1) * NQ], score[:], ACT.Tanh, bias=biases[b][:, j : j + 1], scale=1.0 / CAP
                 )
-            r = late.tile([P, N], F32, name=f"r{b}", offset=4096 * b, align_bytes=64)
-            p = sb.tile([P, N], F32, name=f"p{b}")
-            for h in range(2):
-                half = slice(h * N // 2, (h + 1) * N // 2)
-                nc.scalar.activation(r[:, half], x[:, half], ACT.Tanh)
-            for h in range(2):
-                half = slice(h * N // 2, (h + 1) * N // 2)
-                nc.scalar.activation(p[:, half], r[:, half], ACT.Square)
-            sq.append(p)
+            th.append(t)
 
-        gather_vs(0)
-        gather_vs(1)
-        vsT = [turn(vsgs[b], ("s0", "a0")[b], f"vsT{b}") for b in range(B)]
+        vg1 = sb.tile([P, N], BF16, name="vg1", tag="bias0")
+        nc.scalar.activation(vg1[:], v_pool[:].indirect(lists[1]), ACT.Copy)
+        vis = [turn_values(0, vg0), turn_values(1, vg1)]
 
-        vi1 = late.tile([P, DV * PACK], BF16, name="vi1", offset=4096 + 1024, align_bytes=64)
-        weave_v(1, vi1)
-
-        def quantise(src, name, codes):
+        def quantise(src, name):
+            codes = sb.tile([P, P], U32, name=f"{name}_codes", align_bytes=64)
             scales = sb.tile([P, P], U8, name=f"{name}_scales", align_bytes=64)
             nc.vector.quantize_mx(codes[:].bitcast(FP8X4), scales[:], src)
             return codes, scales
 
-        vq = [quantise(vi0[:], "v0", sb.tile([P, DV], U32, name="vc0", tag="half1", align_bytes=64))]
-
-        ws = []
-        totals = []
         for b in range(B):
-            p = sq[b]
+            t = th[b]
+            p = sb.tile([P, N], F32, name=f"p{b}")
+            for h in range(2):
+                half = slice(h * N // 2, (h + 1) * N // 2)
+                nc.vector.scalar_tensor_tensor(p[:, half], t[:, half], 0.0, t[:, half], ALU.max, ALU.mult)
             w = sb.tile([P, NQ, PACK], BF16, name=f"w{b}", align_bytes=64)
             nc.vector.scalar_tensor_tensor(
                 w[:],
                 p[:].rearrange("p (j q) -> p q j", j=PACK),
                 CAP * CAP,
-                vsT[b][:, :, ROW : ROW + 1].rearrange("p j o -> p o j").to_broadcast([P, NQ, PACK]),
+                vsp[b][:].unsqueeze(1).to_broadcast([P, NQ, PACK]),
                 ALU.mult,
                 ALU.mult,
             )
-            ws.append(w)
-            pT = ps.tile([P, P], F32, name=f"pT{b}", tag=("s1", "a1")[b])
+            pT = ps.tile([P, P], F32, name=f"pT{b}", tag=f"b{b}")
             for j in range(PACK):
                 nc.tensor.matmul(
                     pT[:], p[:, j * NQ : (j + 1) * NQ], ident[:], start=(j == 0), stop=(j == PACK - 1), is_transpose=True
                 )
-            junk = sb.tile([P, P], BF16, name=f"junk{b}", tag="x")
+            junk = sb.tile([P, P], BF16, name=f"junk{b}")
             total = sb.tile([P, 1], F32, name=f"total{b}")
-            nc.scalar.activation(
-                junk[:], pT[:], ACT.Copy, bias=1.0 / P, scale=CAP * CAP, accum_out=total[:]
-            )
-            totals.append(total)
-
-        wq = [
-            quantise(
-                ws[0][:].rearrange("p q j -> p (q j)"),
-                "w0",
-                late.tile([P, NQ], U32, name="wc0", offset=4096, align_bytes=64),
-            )
-        ]
-        vq.append(quantise(vi1[:], "v1", sb.tile([P, DV], U32, name="vc1", align_bytes=64)))
-        wq.append(
-            quantise(ws[1][:].rearrange("p q j -> p (q j)"), "w1", sb.tile([P, NQ], U32, name="wc1", align_bytes=64))
-        )
-
-        for b in range(B):
+            nc.scalar.activation(junk[:], pT[:], ACT.Copy, bias=1.0 / P, scale=CAP * CAP, accum_out=total[:])
+            vq = quantise(vis[b][:], f"v{b}")
+            wq = quantise(w[:].rearrange("p q j -> p (q j)"), f"w{b}")
             inv = sb.tile([P, 1], F32, name=f"inv{b}")
-            nc.vector.reciprocal(inv[:], totals[b][:])
-            y = ps.tile([P, DV], F32, name=f"y{b}", tag=f"y{b}")
+            nc.vector.reciprocal(inv[:], total[:])
+            y = ps.tile([P, DV], F32, name=f"y{b}", tag=f"s{b}")
             nc.tensor.matmul_mx(
                 out=y[:],
-                lhsT=wq[b][0][:].bitcast(FP8X4),
-                lhsT_scale=wq[b][1][:],
-                rhs=vq[b][0][:].bitcast(FP8X4),
-                rhs_scale=vq[b][1][:],
+                lhsT=wq[0][:].bitcast(FP8X4),
+                lhsT_scale=wq[1][:],
+                rhs=vq[0][:].bitcast(FP8X4),
+                rhs_scale=vq[1][:],
                 start=True,
                 stop=True,
             )

@@ -46,31 +46,30 @@ def tile_attend_rel2_cap_kb_pgb2q128n512t2048_kernel(
 
         kb_pool = sb.tile([P, T], F32, name="kb_pool")
         nc.sync.dma_start(kb_pool[ROW : ROW + 1, :], kb[0:1, :])
-        vs_pool = sb.tile([P, T], F32, name="vs_pool")
-        nc.sync.dma_start(vs_pool[ROW : ROW + 1, :], vs[0:1, :])
 
         ks_pool = sb.tile([P, T // 4], I32, name="ks_pool")
         nc.vector.memset(ks_pool[:], 0)
+        qs = sb.tile([P, B * PASSES, NQ // 4], I32, name="qs", align_bytes=64)
+        nc.vector.memset(qs[:], 0)
+        vs_pool = sb.tile([P, T], F32, name="vs_pool")
         nc.vector.memset(kb_pool[0:ROW, :], 0.0)
         nc.vector.memset(vs_pool[0:ROW, :], 0.0)
+        nc.sync.dma_start(vs_pool[ROW : ROW + 1, :], vs[0:1, :])
         by_parity = k_scales.rearrange("o (a h r) t -> h (o a) r t", h=2, r=4)
         for h in range(2):
             nc.sync.dma_start(ks_pool[32 * h : 32 * h + 16, :], by_parity[h].bitcast(I32))
 
         kw_pool = sb.tile([P, T], I32, name="kw_pool")
         nc.sync.dma_start(kw_pool[:], k_words[0].rearrange("p t r -> p (t r)").bitcast(I32))
-        qw = sb.tile([P, B * PASSES, NQ], I32, name="qw", align_bytes=64)
-        nc.sync.dma_start(qw[:], q_words.rearrange("b o g q r -> g (b o) (q r)").bitcast(I32))
-        v_pool = sb.tile([P, T], F32, name="v_pool")
-        nc.sync.dma_start(v_pool[:], vT)
-
-        qs = sb.tile([P, B * PASSES, NQ // 4], I32, name="qs", align_bytes=64)
-        nc.gpsimd.memset(qs[:], 0)
         for row in range(4):
             nc.sync.dma_start(
                 qs[row:P:32, :, :],
                 q_scales[:, :, row:16:4, :].rearrange("b o f q -> f (b o) q").bitcast(I32),
             )
+        v_pool = sb.tile([P, T], F32, name="v_pool")
+        nc.sync.dma_start(v_pool[:], vT)
+        qw = sb.tile([P, B * PASSES, NQ], I32, name="qw", align_bytes=64)
+        nc.sync.dma_start(qw[:], q_words.rearrange("b o g q r -> g (b o) (q r)").bitcast(I32))
 
         ksg = sb.tile([P, B * N], U8, name="ksg", align_bytes=64)
         nc.vector.tensor_copy(
@@ -104,7 +103,7 @@ def tile_attend_rel2_cap_kb_pgb2q128n512t2048_kernel(
             vsp.append(col)
 
         def turn_values(b, vg):
-            bank = ps.tile([P, 2, P], F32, name=f"vt{b}", tag=f"a{b}")
+            bank = ps.tile([P, 2, P], F32, name=f"vt{b}", tag=f"s{b}")
             for u in range(2):
                 nc.tensor.transpose(bank[:, u, :], vg[:].bitcast(F32)[:, u : N // 2 : 2], ident[:])
             vi = sb.tile([P, DV * PACK], BF16, name=f"vi{b}", align_bytes=64)
@@ -134,24 +133,24 @@ def tile_attend_rel2_cap_kb_pgb2q128n512t2048_kernel(
 
             t = sb.tile([P, N], F32, name=f"t{b}")
             for j in range(PACK):
-                score = ps.tile([P, NQ], F32, name=f"score{b}{j}", tag=f"s{j}")
-                for o in range(PASSES):
+                score = ps.tile([P, NQ], F32, name=f"score{b}{j}", tag=(f"s{j}", ("a0", "a1", "b0", "b1")[j])[b])
+                for o in reversed(range(PASSES)):
                     nc.tensor.matmul_mx(
                         out=score[:],
                         lhsT=kp[:, o, 2 * P * j : 2 * P * (j + 1)].bitcast(FP4X4),
                         lhsT_scale=planes[o][:, P * (PACK * b + j) : P * (PACK * b + j + 1)],
                         rhs=qw[:, b * PASSES + o, :].bitcast(FP8X4),
                         rhs_scale=qs[:, b * PASSES + o, :].bitcast(U8),
-                        start=(o == 0),
-                        stop=(o == PASSES - 1),
+                        start=(o == PASSES - 1),
+                        stop=(o == 0),
                     )
                 nc.scalar.activation(
                     t[:, j * NQ : (j + 1) * NQ], score[:], ACT.Tanh, bias=biases[b][:, j : j + 1], scale=1.0 / CAP
                 )
             th.append(t)
 
-        vg1 = sb.tile([P, N], BF16, name="vg1", tag="bias0")
-        nc.scalar.activation(vg1[:], v_pool[:].indirect(lists[1]), ACT.Copy)
+        vg1 = sb.tile([P, N], BF16, name="vg1", tag="half0", align_bytes=64)
+        nc.vector.tensor_copy(vg1[:], v_pool[:].indirect(lists[1]))
         vis = [turn_values(0, vg0), turn_values(1, vg1)]
 
         def quantise(src, name):
@@ -175,7 +174,7 @@ def tile_attend_rel2_cap_kb_pgb2q128n512t2048_kernel(
                 ALU.mult,
                 ALU.mult,
             )
-            pT = ps.tile([P, P], F32, name=f"pT{b}", tag=f"b{b}")
+            pT = ps.tile([P, P], F32, name=f"pT{b}", tag=f"s{2 + b}")
             for j in range(PACK):
                 nc.tensor.matmul(
                     pT[:], p[:, j * NQ : (j + 1) * NQ], ident[:], start=(j == 0), stop=(j == PACK - 1), is_transpose=True
@@ -187,7 +186,7 @@ def tile_attend_rel2_cap_kb_pgb2q128n512t2048_kernel(
             wq = quantise(w[:].rearrange("p q j -> p (q j)"), f"w{b}")
             inv = sb.tile([P, 1], F32, name=f"inv{b}")
             nc.vector.reciprocal(inv[:], total[:])
-            y = ps.tile([P, DV], F32, name=f"y{b}", tag=f"s{b}")
+            y = ps.tile([P, DV], F32, name=f"y{b}", tag=f"a{b}")
             nc.tensor.matmul_mx(
                 out=y[:],
                 lhsT=wq[0][:].bitcast(FP8X4),

@@ -31,14 +31,14 @@ def tile_attend_rel2_cap_kb_pgb2q128n512t2048_kernel(
     nc = tc.nc
     with ExitStack() as ctx:
         sb = ctx.enter_context(tc.tile_pool(name="sb", bufs=1))
-        early = ctx.enter_context(tc.tile_pool(name="early", bufs=1))
         ps = ctx.enter_context(tc.psum_pool(name="ps", bufs=1))
 
-        ident_room = early.tile([P, 8 * N], BF16, name="ident_room", offset=0)
-        ident_bf = ident_room[:, 0:P]
-        make_identity(nc, ident_bf)
         ident = sb.tile([P, P], F32, name="ident")
-        nc.scalar.activation(ident[:], ident_bf, ACT.Copy)
+        make_identity(nc, ident[:])
+
+        warm = sb.tile([P, 2, 8], F32, name="warm")
+        nc.vector.memset(warm[:, 0, :], 0.0)
+        nc.scalar.activation(warm[:, 1, :], warm[:, 0, :], ACT.Tanh)
 
         offsets = sb.tile([P, B * COLS], U16, name="offsets")
         nc.sync.dma_start(offsets[:], offs)
@@ -85,7 +85,7 @@ def tile_attend_rel2_cap_kb_pgb2q128n512t2048_kernel(
 
         biases = []
         for b in range(B):
-            kbg = early.tile([P, N], F32, name=f"kbg{b}", offset=4 * N * b)
+            kbg = sb.tile([P, N], F32, name=f"kbg{b}")
             nc.scalar.activation(kbg[:], kb_pool[:].indirect(lists[b]), ACT.Copy)
             bank = ps.tile([P, PACK, P], F32, name=f"kbT{b}", tag=f"a{b}")
             for j in range(PACK):
@@ -94,12 +94,12 @@ def tile_attend_rel2_cap_kb_pgb2q128n512t2048_kernel(
             nc.scalar.activation(bias[:], bank[:, :, ROW], ACT.Copy, scale=1.0 / CAP)
             biases.append(bias)
 
+        vsg = sb.tile([P, B * N], F32, name="vsg")
+        nc.scalar.activation(vsg[:], vs_pool[:].indirect(offsets[:]), ACT.Copy)
         vsp = []
         for b in range(B):
-            vsg = early.tile([P, N], F32, name=f"vsg{b}", offset=4 * N * (B + b))
-            nc.scalar.activation(vsg[:], vs_pool[:].indirect(lists[b]), ACT.Copy)
             col = sb.tile([P, PACK], F32, name=f"vsp{b}")
-            nc.sync.dma_start(col[:], vsg[ROW : ROW + 1, :].rearrange("o (p j) -> o p j", j=PACK))
+            nc.sync.dma_start(col[:], vsg[ROW : ROW + 1, b * N : (b + 1) * N].rearrange("o (p j) -> o p j", j=PACK))
             vsp.append(col)
 
         def turn_values(b, vg):

@@ -48,16 +48,16 @@ def tile_attend_rel2_cap_kb_pgb2q128n512t2048_kernel(
         nc.sync.dma_start(kb_pool[ROW : ROW + 1, :], kb[0:1, :])
 
         ks_pool = sb.tile([P, T // 4], I32, name="ks_pool")
-        nc.vector.memset(ks_pool[:], 0)
+        scale_rows = k_scales.rearrange("o f t -> (o f) t").bitcast(I32)
+        for first, row, count in ((0, 0, 32), (32, 4, 16), (48, 12, 16), (64, 0, 32)):
+            nc.sync.dma_start(ks_pool[first : first + count, :], scale_rows[row : row + count, :])
         qs = sb.tile([P, B * PASSES, NQ // 4], I32, name="qs", align_bytes=64)
         nc.vector.memset(qs[:], 0)
-        vs_pool = sb.tile([P, T], F32, name="vs_pool")
         nc.vector.memset(kb_pool[0:ROW, :], 0.0)
+        nc.vector.memset(ks_pool[96:P, :], 0)
+        vs_pool = sb.tile([P, T], F32, name="vs_pool")
         nc.vector.memset(vs_pool[0:ROW, :], 0.0)
         nc.sync.dma_start(vs_pool[ROW : ROW + 1, :], vs[0:1, :])
-        by_parity = k_scales.rearrange("o (a h r) t -> h (o a) r t", h=2, r=4)
-        for h in range(2):
-            nc.sync.dma_start(ks_pool[32 * h : 32 * h + 16, :], by_parity[h].bitcast(I32))
 
         kw_pool = sb.tile([P, T], I32, name="kw_pool")
         nc.sync.dma_start(kw_pool[:], k_words[0].rearrange("p t r -> p (t r)").bitcast(I32))
@@ -79,7 +79,7 @@ def tile_attend_rel2_cap_kb_pgb2q128n512t2048_kernel(
         for o in range(PASSES):
             plane = sb.tile([P, B * N // 4], I32, name=f"plane{o}", align_bytes=64)
             for h in range(2):
-                first = 8 * o + 4 * h
+                first = 52 * o + 8 * h
                 nc.sync.dma_start(plane[64 * h : 64 * h + 64, :], ksg[:].bitcast(I32)[first : first + 64, :])
             planes.append(plane[:].bitcast(U8))
 
@@ -120,15 +120,12 @@ def tile_attend_rel2_cap_kb_pgb2q128n512t2048_kernel(
             for h in range(2):
                 kwg = sb.tile([P, N // 2], U32, name=f"kwg{b}{h}", tag=f"half{h}", align_bytes=64)
                 first = b * COLS + h * (COLS // 2)
-                nc.vector.tensor_copy(
-                    kwg[:].rearrange("p (j m) -> p m j", j=PACK),
-                    kw_pool[:].bitcast(U32).indirect(offsets[:, first : first + COLS // 2]),
-                )
+                nc.vector.tensor_copy(kwg[:], kw_pool[:].bitcast(U32).indirect(offsets[:, first : first + COLS // 2]))
                 halves.append(kwg)
             for h in range(2):
                 nc.vector.tensor_copy(
-                    kp[:].bitcast(U16).rearrange("p o (j m) -> p o j m", j=PACK)[:, :, :, 64 * h : 64 * h + 64],
-                    halves[h][:].bitcast(U16).rearrange("p (j m o) -> p o j m", j=PACK, o=PASSES),
+                    kp[:].bitcast(U16).rearrange("p o (j g i) -> p o g j i", j=PACK, i=4)[:, :, 16 * h : 16 * h + 16],
+                    halves[h][:].bitcast(U16).rearrange("p (g i j o) -> p o g j i", j=PACK, o=PASSES, i=4),
                 )
 
             t = sb.tile([P, N], F32, name=f"t{b}")
@@ -149,8 +146,8 @@ def tile_attend_rel2_cap_kb_pgb2q128n512t2048_kernel(
                 )
             th.append(t)
 
-        vg1 = sb.tile([P, N], BF16, name="vg1", tag="half0", align_bytes=64)
-        nc.vector.tensor_copy(vg1[:], v_pool[:].indirect(lists[1]))
+        vg1 = sb.tile([P, N], BF16, name="vg1")
+        nc.scalar.activation(vg1[:], v_pool[:].indirect(lists[1]), ACT.Copy)
         vis = [turn_values(0, vg0), turn_values(1, vg1)]
 
         def quantise(src, name):

@@ -23,6 +23,7 @@ PACK = 4
 PASSES = D // (P * PACK)
 ROW = 127
 COLS = N // 16
+VS_HEAD = 1408
 
 
 def tile_attend_rel2_cap_kb_pgb2q128n512t2048_kernel(
@@ -36,45 +37,61 @@ def tile_attend_rel2_cap_kb_pgb2q128n512t2048_kernel(
         ident = sb.tile([P, P], F32, name="ident")
         make_identity(nc, ident[:])
 
-        warm = sb.tile([P, 2, 8], F32, name="warm")
-        nc.vector.memset(warm[:, 0, :], 0.0)
-        nc.scalar.activation(warm[:, 1, :], warm[:, 0, :], ACT.Tanh)
+        qs = sb.tile([P, B * PASSES, NQ // 4], I32, name="qs", align_bytes=64)
+        nc.vector.memset(qs[:], 0)
 
         offsets = sb.tile([P, B * COLS], U16, name="offsets")
         nc.sync.dma_start(offsets[:], offs)
         lists = [offsets[:, b * COLS : (b + 1) * COLS] for b in range(B)]
 
         kb_pool = sb.tile([P, T], F32, name="kb_pool")
-        nc.sync.dma_start(kb_pool[ROW : ROW + 1, :], kb[0:1, :])
+        nc.scalar.dma_start(kb_pool[ROW : ROW + 1, :], kb[0:1, :])
 
-        ks_pool = sb.tile([P, T // 4], I32, name="ks_pool")
+        ks_pool = sb.tile([P, T // 4], I32, name="ks_pool", tag="ks_pool", align_bytes=64)
         scale_rows = k_scales.rearrange("o f t -> (o f) t").bitcast(I32)
-        for first, row, count in ((0, 0, 32), (32, 4, 16), (48, 12, 16), (64, 0, 32)):
-            nc.sync.dma_start(ks_pool[first : first + count, :], scale_rows[row : row + count, :])
-        qs = sb.tile([P, B * PASSES, NQ // 4], I32, name="qs", align_bytes=64)
-        nc.vector.memset(qs[:], 0)
+        for first, row, count, queue in (
+            (0, 0, 32, nc.sync),
+            (32, 4, 16, nc.scalar),
+            (64, 0, 32, nc.sync),
+            (48, 12, 16, nc.scalar),
+        ):
+            queue.dma_start(ks_pool[first : first + count, :], scale_rows[row : row + count, :])
+        kw_pool = sb.tile([P, T], I32, name="kw_pool")
+        nc.sync.dma_start(kw_pool[:], k_words[0].rearrange("p t r -> p (t r)").bitcast(I32))
+
+        warm = sb.tile([P, 2, 8], F32, name="warm")
+        nc.vector.memset(warm[:, 0, :], 0.0)
+        nc.scalar.activation(warm[:, 1, :], warm[:, 0, :], ACT.Tanh)
+
         nc.vector.memset(kb_pool[0:ROW, :], 0.0)
         nc.vector.memset(ks_pool[96:P, :], 0)
         vs_pool = sb.tile([P, T], F32, name="vs_pool")
-        nc.vector.memset(vs_pool[0:ROW, :], 0.0)
+        nc.vector.memset(vs_pool[0:ROW, 0:VS_HEAD], 0.0)
         nc.sync.dma_start(vs_pool[ROW : ROW + 1, :], vs[0:1, :])
 
-        kw_pool = sb.tile([P, T], I32, name="kw_pool")
-        nc.sync.dma_start(kw_pool[:], k_words[0].rearrange("p t r -> p (t r)").bitcast(I32))
-        for row in range(4):
+        def load_query_scales(row):
             nc.sync.dma_start(
                 qs[row:P:32, :, :],
                 q_scales[:, :, row:16:4, :].rearrange("b o f q -> f (b o) q").bitcast(I32),
             )
+
+        def load_queries(b, tag):
+            words = sb.tile([P, PASSES, NQ], I32, name=f"qw{b}", tag=tag, align_bytes=64)
+            nc.sync.dma_start(words[:], q_words[b].rearrange("o g q r -> g o (q r)").bitcast(I32))
+            return words
+
+        qw = [load_queries(0, "qw0")]
+        load_query_scales(0)
         v_pool = sb.tile([P, T], F32, name="v_pool")
         nc.sync.dma_start(v_pool[:], vT)
-        qw = sb.tile([P, B * PASSES, NQ], I32, name="qw", align_bytes=64)
-        nc.sync.dma_start(qw[:], q_words.rearrange("b o g q r -> g (b o) (q r)").bitcast(I32))
+        for row in range(1, 4):
+            load_query_scales(row)
 
         ksg = sb.tile([P, B * N], U8, name="ksg", align_bytes=64)
         nc.vector.tensor_copy(
             ksg[:].rearrange("p (b j m) -> p b m j", b=B, j=PACK), ks_pool[:].bitcast(U8).indirect(offsets[:])
         )
+        nc.vector.memset(vs_pool[0:ROW, VS_HEAD:T], 0.0)
         planes = []
         for o in range(PASSES):
             plane = sb.tile([P, B * N // 4], I32, name=f"plane{o}", align_bytes=64)
@@ -82,17 +99,18 @@ def tile_attend_rel2_cap_kb_pgb2q128n512t2048_kernel(
                 first = 52 * o + 8 * h
                 nc.sync.dma_start(plane[64 * h : 64 * h + 64, :], ksg[:].bitcast(I32)[first : first + 64, :])
             planes.append(plane[:].bitcast(U8))
+        qw.append(load_queries(1, "ks_pool"))
 
-        biases = []
+        vgs = [sb.tile([P, N], BF16, name=f"vg{b}") for b in range(B)]
+        bias1 = sb.tile([P, PACK], F32, name="bias1")
+        biases = [vgs[1][:].bitcast(F32)[:, N // 4 : N // 4 + PACK], bias1[:]]
         for b in range(B):
             kbg = sb.tile([P, N], F32, name=f"kbg{b}")
             nc.scalar.activation(kbg[:], kb_pool[:].indirect(lists[b]), ACT.Copy)
             bank = ps.tile([P, PACK, P], F32, name=f"kbT{b}", tag=f"a{b}")
             for j in range(PACK):
                 nc.tensor.transpose(bank[:, j, :], kbg[:, j:N:PACK], ident[:])
-            bias = sb.tile([P, PACK], F32, name=f"bias{b}", tag=f"bias{b}")
-            nc.scalar.activation(bias[:], bank[:, :, ROW], ACT.Copy, scale=1.0 / CAP)
-            biases.append(bias)
+            nc.scalar.activation(biases[b], bank[:, :, ROW], ACT.Copy, scale=1.0 / CAP)
 
         vsg = sb.tile([P, B * N], F32, name="vsg")
         nc.scalar.activation(vsg[:], vs_pool[:].indirect(offsets[:]), ACT.Copy)
@@ -102,16 +120,7 @@ def tile_attend_rel2_cap_kb_pgb2q128n512t2048_kernel(
             nc.sync.dma_start(col[:], vsg[ROW : ROW + 1, b * N : (b + 1) * N].rearrange("o (p j) -> o p j", j=PACK))
             vsp.append(col)
 
-        def turn_values(b, vg):
-            bank = ps.tile([P, 2, P], F32, name=f"vt{b}", tag=f"s{b}")
-            for u in range(2):
-                nc.tensor.transpose(bank[:, u, :], vg[:].bitcast(F32)[:, u : N // 2 : 2], ident[:])
-            vi = sb.tile([P, DV * PACK], BF16, name=f"vi{b}", align_bytes=64)
-            nc.scalar.copy(vi[:].bitcast(F32).rearrange("p (e u) -> p e u", u=2), bank[:].rearrange("p u e -> p e u"))
-            return vi
-
-        vg0 = sb.tile([P, N], BF16, name="vg0")
-        nc.scalar.activation(vg0[:], v_pool[:].indirect(lists[0]), ACT.Copy)
+        nc.scalar.activation(vgs[0][:], v_pool[:].indirect(lists[0]), ACT.Copy)
 
         th = []
         for b in range(B):
@@ -136,7 +145,7 @@ def tile_attend_rel2_cap_kb_pgb2q128n512t2048_kernel(
                         out=score[:],
                         lhsT=kp[:, o, 2 * P * j : 2 * P * (j + 1)].bitcast(FP4X4),
                         lhsT_scale=planes[o][:, P * (PACK * b + j) : P * (PACK * b + j + 1)],
-                        rhs=qw[:, b * PASSES + o, :].bitcast(FP8X4),
+                        rhs=qw[b][:, o, :].bitcast(FP8X4),
                         rhs_scale=qs[:, b * PASSES + o, :].bitcast(U8),
                         start=(o == PASSES - 1),
                         stop=(o == 0),
@@ -145,51 +154,82 @@ def tile_attend_rel2_cap_kb_pgb2q128n512t2048_kernel(
                     t[:, j * NQ : (j + 1) * NQ], score[:], ACT.Tanh, bias=biases[b][:, j : j + 1], scale=1.0 / CAP
                 )
             th.append(t)
+            if b == 0:
+                nc.scalar.activation(
+                    vgs[1][:, N // 2 : N], v_pool[:].indirect(lists[1][:, COLS // 2 : COLS]), ACT.Copy
+                )
 
-        vg1 = sb.tile([P, N], BF16, name="vg1")
-        nc.scalar.activation(vg1[:], v_pool[:].indirect(lists[1]), ACT.Copy)
-        vis = [turn_values(0, vg0), turn_values(1, vg1)]
+        nc.vector.tensor_copy(vgs[1][:, 0 : N // 2], v_pool[:].indirect(lists[1][:, 0 : COLS // 2]))
+        vi = sb.tile([P, B, DV * PACK], BF16, name="vi", align_bytes=64)
+        for b in range(B):
+            bank = ps.tile([P, 2, P], F32, name=f"vt{b}", tag=f"s{b}")
+            for u in range(2):
+                nc.tensor.transpose(bank[:, u, :], vgs[b][:].bitcast(F32)[:, u : N // 2 : 2], ident[:])
+            nc.scalar.copy(
+                vi[:, b, :].bitcast(F32).rearrange("p (e u) -> p e u", u=2), bank[:].rearrange("p u e -> p e u")
+            )
 
-        def quantise(src, name):
-            codes = sb.tile([P, P], U32, name=f"{name}_codes", align_bytes=64)
-            scales = sb.tile([P, P], U8, name=f"{name}_scales", align_bytes=64)
+        def quantise(src, width, name):
+            codes = sb.tile([P, width], U32, name=f"{name}_codes", align_bytes=64)
+            scales = sb.tile([P, width], U8, name=f"{name}_scales", align_bytes=64)
             nc.vector.quantize_mx(codes[:].bitcast(FP8X4), scales[:], src)
             return codes, scales
 
-        for b in range(B):
-            t = th[b]
-            p = sb.tile([P, N], F32, name=f"p{b}")
-            for h in range(2):
-                half = slice(h * N // 2, (h + 1) * N // 2)
-                nc.vector.scalar_tensor_tensor(p[:, half], t[:, half], 0.0, t[:, half], ALU.max, ALU.mult)
-            w = sb.tile([P, NQ, PACK], BF16, name=f"w{b}", align_bytes=64)
+        sq = [sb.tile([P, N], F32, name=f"p{b}") for b in range(B)]
+        ws = [sb.tile([P, NQ, PACK], BF16, name=f"w{b}", align_bytes=64) for b in range(B)]
+
+        def square(b, h):
+            half = slice(h * N // 2, (h + 1) * N // 2)
+            nc.vector.scalar_tensor_tensor(sq[b][:, half], th[b][:, half], 0.0, th[b][:, half], ALU.max, ALU.mult)
+
+        def weigh(b):
             nc.vector.scalar_tensor_tensor(
-                w[:],
-                p[:].rearrange("p (j q) -> p q j", j=PACK),
+                ws[b][:],
+                sq[b][:].rearrange("p (j q) -> p q j", j=PACK),
                 CAP * CAP,
                 vsp[b][:].unsqueeze(1).to_broadcast([P, NQ, PACK]),
                 ALU.mult,
                 ALU.mult,
             )
+
+        def row_sum(b):
             pT = ps.tile([P, P], F32, name=f"pT{b}", tag=f"s{2 + b}")
             for j in range(PACK):
                 nc.tensor.matmul(
-                    pT[:], p[:, j * NQ : (j + 1) * NQ], ident[:], start=(j == 0), stop=(j == PACK - 1), is_transpose=True
+                    pT[:],
+                    sq[b][:, j * NQ : (j + 1) * NQ],
+                    ident[:],
+                    start=(j == 0),
+                    stop=(j == PACK - 1),
+                    is_transpose=True,
                 )
             junk = sb.tile([P, P], BF16, name=f"junk{b}")
             total = sb.tile([P, 1], F32, name=f"total{b}")
             nc.scalar.activation(junk[:], pT[:], ACT.Copy, bias=1.0 / P, scale=CAP * CAP, accum_out=total[:])
-            vq = quantise(vis[b][:], f"v{b}")
-            wq = quantise(w[:].rearrange("p q j -> p (q j)"), f"w{b}")
+            return total
+
+        square(0, 0)
+        square(0, 1)
+        weigh(0)
+        totals = [row_sum(0)]
+        square(1, 0)
+        wq = [quantise(ws[0][:].rearrange("p q j -> p (q j)"), NQ, "w0")]
+        square(1, 1)
+        weigh(1)
+        totals.append(row_sum(1))
+        v_codes, v_scales = quantise(vi[:].rearrange("p b c -> p (b c)"), B * DV, "v")
+        wq.append(quantise(ws[1][:].rearrange("p q j -> p (q j)"), NQ, "w1"))
+
+        for b in range(B):
             inv = sb.tile([P, 1], F32, name=f"inv{b}")
-            nc.vector.reciprocal(inv[:], total[:])
+            nc.vector.reciprocal(inv[:], totals[b][:])
             y = ps.tile([P, DV], F32, name=f"y{b}", tag=f"a{b}")
             nc.tensor.matmul_mx(
                 out=y[:],
-                lhsT=wq[0][:].bitcast(FP8X4),
-                lhsT_scale=wq[1][:],
-                rhs=vq[0][:].bitcast(FP8X4),
-                rhs_scale=vq[1][:],
+                lhsT=wq[b][0][:].bitcast(FP8X4),
+                lhsT_scale=wq[b][1][:],
+                rhs=v_codes[:, b * DV : (b + 1) * DV].bitcast(FP8X4),
+                rhs_scale=v_scales[:, b * DV : (b + 1) * DV],
                 start=True,
                 stop=True,
             )

@@ -23,7 +23,6 @@ PACK = 4
 PASSES = D // (P * PACK)
 ROW = 127
 COLS = N // 16
-VS_HEAD = 1408
 
 
 def tile_attend_rel2_cap_kb_pgb2q128n512t2048_kernel(
@@ -66,7 +65,7 @@ def tile_attend_rel2_cap_kb_pgb2q128n512t2048_kernel(
         nc.vector.memset(kb_pool[0:ROW, :], 0.0)
         nc.vector.memset(ks_pool[96:P, :], 0)
         vs_pool = sb.tile([P, T], F32, name="vs_pool")
-        nc.vector.memset(vs_pool[0:ROW, 0:VS_HEAD], 0.0)
+        nc.vector.memset(vs_pool[0:ROW, :], 0.0)
         nc.sync.dma_start(vs_pool[ROW : ROW + 1, :], vs[0:1, :])
 
         def load_query_scales(row):
@@ -91,7 +90,6 @@ def tile_attend_rel2_cap_kb_pgb2q128n512t2048_kernel(
         nc.vector.tensor_copy(
             ksg[:].rearrange("p (b j m) -> p b m j", b=B, j=PACK), ks_pool[:].bitcast(U8).indirect(offsets[:])
         )
-        nc.vector.memset(vs_pool[0:ROW, VS_HEAD:T], 0.0)
         planes = []
         for o in range(PASSES):
             plane = sb.tile([P, B * N // 4], I32, name=f"plane{o}", align_bytes=64)
@@ -102,8 +100,7 @@ def tile_attend_rel2_cap_kb_pgb2q128n512t2048_kernel(
         qw.append(load_queries(1, "ks_pool"))
 
         vgs = [sb.tile([P, N], BF16, name=f"vg{b}") for b in range(B)]
-        bias1 = sb.tile([P, PACK], F32, name="bias1")
-        biases = [vgs[1][:].bitcast(F32)[:, N // 4 : N // 4 + PACK], bias1[:]]
+        biases = [sb.tile([P, PACK], F32, name=f"bias{b}")[:] for b in range(B)]
         for b in range(B):
             kbg = sb.tile([P, N], F32, name=f"kbg{b}")
             nc.scalar.activation(kbg[:], kb_pool[:].indirect(lists[b]), ACT.Copy)
@@ -154,50 +151,51 @@ def tile_attend_rel2_cap_kb_pgb2q128n512t2048_kernel(
                     t[:, j * NQ : (j + 1) * NQ], score[:], ACT.Tanh, bias=biases[b][:, j : j + 1], scale=1.0 / CAP
                 )
             th.append(t)
-            if b == 0:
-                nc.scalar.activation(
-                    vgs[1][:, N // 2 : N], v_pool[:].indirect(lists[1][:, COLS // 2 : COLS]), ACT.Copy
-                )
 
-        nc.vector.tensor_copy(vgs[1][:, 0 : N // 2], v_pool[:].indirect(lists[1][:, 0 : COLS // 2]))
+        nc.vector.tensor_copy(vgs[1][:], v_pool[:].indirect(lists[1]))
         vi = sb.tile([P, B, DV * PACK], BF16, name="vi", align_bytes=64)
         for b in range(B):
-            bank = ps.tile([P, 2, P], F32, name=f"vt{b}", tag=f"s{b}")
+            bank = ps.tile([P, 2, P], F32, name=f"vt{b}", tag=f"a{b}")
             for u in range(2):
                 nc.tensor.transpose(bank[:, u, :], vgs[b][:].bitcast(F32)[:, u : N // 2 : 2], ident[:])
             nc.scalar.copy(
                 vi[:, b, :].bitcast(F32).rearrange("p (e u) -> p e u", u=2), bank[:].rearrange("p u e -> p e u")
             )
 
-        def quantise(src, width, name):
-            codes = sb.tile([P, width], U32, name=f"{name}_codes", align_bytes=64)
-            scales = sb.tile([P, width], U8, name=f"{name}_scales", align_bytes=64)
-            nc.vector.quantize_mx(codes[:].bitcast(FP8X4), scales[:], src)
-            return codes, scales
-
-        sq = [sb.tile([P, N], F32, name=f"p{b}") for b in range(B)]
+        sq = [sb.tile([P, PACK, NQ], F32, name=f"p{b}") for b in range(B)]
         ws = [sb.tile([P, NQ, PACK], BF16, name=f"w{b}", align_bytes=64) for b in range(B)]
+        w_codes = [sb.tile([P, NQ], U32, name=f"w_codes{b}", align_bytes=64) for b in range(B)]
+        w_scales = [sb.tile([P, NQ], U8, name=f"w_scales{b}", align_bytes=64) for b in range(B)]
+        query_halves = [slice(h * NQ // 2, (h + 1) * NQ // 2) for h in range(2)]
 
-        def square(b, h):
-            half = slice(h * N // 2, (h + 1) * N // 2)
-            nc.vector.scalar_tensor_tensor(sq[b][:, half], th[b][:, half], 0.0, th[b][:, half], ALU.max, ALU.mult)
+        def weights(b):
+            t = th[b][:].rearrange("p (j q) -> p j q", j=PACK)
+            for half in query_halves:
+                nc.vector.scalar_tensor_tensor(sq[b][:, :, half], t[:, :, half], 0.0, t[:, :, half], ALU.max, ALU.mult)
+            for half in query_halves:
+                nc.vector.scalar_tensor_tensor(
+                    ws[b][:, half, :],
+                    sq[b][:, :, half].rearrange("p j q -> p q j"),
+                    CAP * CAP,
+                    vsp[b][:].unsqueeze(1).to_broadcast([P, NQ // 2, PACK]),
+                    ALU.mult,
+                    ALU.mult,
+                )
 
-        def weigh(b):
-            nc.vector.scalar_tensor_tensor(
-                ws[b][:],
-                sq[b][:].rearrange("p (j q) -> p q j", j=PACK),
-                CAP * CAP,
-                vsp[b][:].unsqueeze(1).to_broadcast([P, NQ, PACK]),
-                ALU.mult,
-                ALU.mult,
-            )
+        def quantise_weights(b):
+            for half in query_halves:
+                nc.vector.quantize_mx(
+                    w_codes[b][:, half].bitcast(FP8X4),
+                    w_scales[b][:, half],
+                    ws[b][:, half, :].rearrange("p q j -> p (q j)"),
+                )
 
         def row_sum(b):
-            pT = ps.tile([P, P], F32, name=f"pT{b}", tag=f"s{2 + b}")
+            pT = ps.tile([P, P], F32, name=f"pT{b}", tag=f"b{b}")
             for j in range(PACK):
                 nc.tensor.matmul(
                     pT[:],
-                    sq[b][:, j * NQ : (j + 1) * NQ],
+                    sq[b][:, j, :],
                     ident[:],
                     start=(j == 0),
                     stop=(j == PACK - 1),
@@ -208,31 +206,31 @@ def tile_attend_rel2_cap_kb_pgb2q128n512t2048_kernel(
             nc.scalar.activation(junk[:], pT[:], ACT.Copy, bias=1.0 / P, scale=CAP * CAP, accum_out=total[:])
             return total
 
-        square(0, 0)
-        square(0, 1)
-        weigh(0)
-        totals = [row_sum(0)]
-        square(1, 0)
-        wq = [quantise(ws[0][:].rearrange("p q j -> p (q j)"), NQ, "w0")]
-        square(1, 1)
-        weigh(1)
-        totals.append(row_sum(1))
-        v_codes, v_scales = quantise(vi[:].rearrange("p b c -> p (b c)"), B * DV, "v")
-        wq.append(quantise(ws[1][:].rearrange("p q j -> p (q j)"), NQ, "w1"))
+        weights(0)
+        quantise_weights(0)
+        weights(1)
+        totals = [row_sum(b) for b in range(B)]
+        v_codes = sb.tile([P, B * DV], U32, name="v_codes", align_bytes=64)
+        v_scales = sb.tile([P, B * DV], U8, name="v_scales", align_bytes=64)
+        nc.vector.quantize_mx(v_codes[:].bitcast(FP8X4), v_scales[:], vi[:].rearrange("p b c -> p (b c)"))
+        quantise_weights(1)
 
         for b in range(B):
             inv = sb.tile([P, 1], F32, name=f"inv{b}")
             nc.vector.reciprocal(inv[:], totals[b][:])
-            y = ps.tile([P, DV], F32, name=f"y{b}", tag=f"a{b}")
+            y = ps.tile([P, DV], F32, name=f"y{b}", tag=f"s{b}")
             nc.tensor.matmul_mx(
                 out=y[:],
-                lhsT=wq[b][0][:].bitcast(FP8X4),
-                lhsT_scale=wq[b][1][:],
+                lhsT=w_codes[b][:].bitcast(FP8X4),
+                lhsT_scale=w_scales[b][:],
                 rhs=v_codes[:, b * DV : (b + 1) * DV].bitcast(FP8X4),
                 rhs_scale=v_scales[:, b * DV : (b + 1) * DV],
                 start=True,
                 stop=True,
             )
             res = sb.tile([P, DV], F32, name=f"res{b}")
-            nc.scalar.activation(res[:], y[:], ACT.Copy, scale=inv[:])
+            if b == 0:
+                nc.vector.tensor_scalar(res[:], y[:], inv[:], None, ALU.mult)
+            else:
+                nc.scalar.activation(res[:], y[:], ACT.Copy, scale=inv[:])
             nc.sync.dma_start(out[b], res[:])

@@ -48,13 +48,10 @@ def tile_attend_rel2_cap_kb_pgb2q128n512t2048_kernel(
 
         ks_pool = sb.tile([P, T // 4], I32, name="ks_pool", tag="ks_pool", align_bytes=64)
         scale_rows = k_scales.rearrange("o f t -> (o f) t").bitcast(I32)
-        for first, row, count, queue in (
-            (0, 0, 32, nc.sync),
-            (32, 4, 16, nc.scalar),
-            (64, 0, 32, nc.sync),
-            (48, 12, 16, nc.scalar),
-        ):
-            queue.dma_start(ks_pool[first : first + count, :], scale_rows[row : row + count, :])
+        for first, row, count in ((0, 0, 32), (32, 4, 16), (48, 12, 16), (64, 0, 32)):
+            nc.sync.dma_start(ks_pool[first : first + count, :], scale_rows[row : row + count, :])
+        vs_pool = sb.tile([P, T], F32, name="vs_pool")
+        nc.scalar.dma_start(vs_pool[ROW : ROW + 1, :], vs[0:1, :])
         kw_pool = sb.tile([P, T], I32, name="kw_pool")
         nc.sync.dma_start(kw_pool[:], k_words[0].rearrange("p t r -> p (t r)").bitcast(I32))
 
@@ -64,9 +61,7 @@ def tile_attend_rel2_cap_kb_pgb2q128n512t2048_kernel(
 
         nc.vector.memset(kb_pool[0:ROW, :], 0.0)
         nc.vector.memset(ks_pool[96:P, :], 0)
-        vs_pool = sb.tile([P, T], F32, name="vs_pool")
         nc.vector.memset(vs_pool[0:ROW, :], 0.0)
-        nc.sync.dma_start(vs_pool[ROW : ROW + 1, :], vs[0:1, :])
 
         def load_query_scales(row):
             nc.sync.dma_start(
@@ -100,7 +95,8 @@ def tile_attend_rel2_cap_kb_pgb2q128n512t2048_kernel(
         qw.append(load_queries(1, "ks_pool"))
 
         vgs = [sb.tile([P, N], BF16, name=f"vg{b}") for b in range(B)]
-        biases = [sb.tile([P, PACK], F32, name=f"bias{b}")[:] for b in range(B)]
+        bias1 = sb.tile([P, PACK], F32, name="bias1")
+        biases = [vgs[1][:].bitcast(F32)[:, N // 4 : N // 4 + PACK], bias1[:]]
         for b in range(B):
             kbg = sb.tile([P, N], F32, name=f"kbg{b}")
             nc.scalar.activation(kbg[:], kb_pool[:].indirect(lists[b]), ACT.Copy)
@@ -118,44 +114,50 @@ def tile_attend_rel2_cap_kb_pgb2q128n512t2048_kernel(
             vsp.append(col)
 
         nc.scalar.activation(vgs[0][:], v_pool[:].indirect(lists[0]), ACT.Copy)
+        nc.scalar.activation(vgs[1][:, 0 : N // 2], v_pool[:].indirect(lists[1][:, 0 : COLS // 2]), ACT.Copy)
 
         th = []
         for b in range(B):
-            kp = sb.tile([P, PASSES, 2 * N], U8, name=f"kp{b}", align_bytes=64)
+            kp = [sb.tile([P, 2 * N], U8, name=f"kp{b}{o}", align_bytes=64) for o in range(PASSES)]
             halves = []
             for h in range(2):
                 kwg = sb.tile([P, N // 2], U32, name=f"kwg{b}{h}", tag=f"half{h}", align_bytes=64)
                 first = b * COLS + h * (COLS // 2)
                 nc.vector.tensor_copy(kwg[:], kw_pool[:].bitcast(U32).indirect(offsets[:, first : first + COLS // 2]))
                 halves.append(kwg)
-            for h in range(2):
-                nc.vector.tensor_copy(
-                    kp[:].bitcast(U16).rearrange("p o (j g i) -> p o g j i", j=PACK, i=4)[:, :, 16 * h : 16 * h + 16],
-                    halves[h][:].bitcast(U16).rearrange("p (g i j o) -> p o g j i", j=PACK, o=PASSES, i=4),
-                )
+            for o in range(PASSES):
+                for h in range(2):
+                    nc.vector.tensor_copy(
+                        kp[o][:].bitcast(U16).rearrange("p (j g i) -> p g j i", j=PACK, i=4)[:, 16 * h : 16 * h + 16],
+                        halves[h][:].bitcast(U16).rearrange("p (g i j o) -> p o g j i", j=PACK, o=PASSES, i=4)[:, o],
+                    )
 
             t = sb.tile([P, N], F32, name=f"t{b}")
-            for j in range(PACK):
-                score = ps.tile([P, NQ], F32, name=f"score{b}{j}", tag=(f"s{j}", ("a0", "a1", "b0", "b1")[j])[b])
-                for o in reversed(range(PASSES)):
+            scores = [ps.tile([P, NQ], F32, name=f"score{b}{j}", tag=f"s{j}") for j in range(PACK)]
+            for o in range(PASSES):
+                for j in range(PACK):
                     nc.tensor.matmul_mx(
-                        out=score[:],
-                        lhsT=kp[:, o, 2 * P * j : 2 * P * (j + 1)].bitcast(FP4X4),
+                        out=scores[j][:],
+                        lhsT=kp[o][:, 2 * P * j : 2 * P * (j + 1)].bitcast(FP4X4),
                         lhsT_scale=planes[o][:, P * (PACK * b + j) : P * (PACK * b + j + 1)],
                         rhs=qw[b][:, o, :].bitcast(FP8X4),
                         rhs_scale=qs[:, b * PASSES + o, :].bitcast(U8),
-                        start=(o == PASSES - 1),
-                        stop=(o == 0),
+                        start=(o == 0),
+                        stop=(o == PASSES - 1),
                     )
+            for j in range(PACK):
                 nc.scalar.activation(
-                    t[:, j * NQ : (j + 1) * NQ], score[:], ACT.Tanh, bias=biases[b][:, j : j + 1], scale=1.0 / CAP
+                    t[:, j * NQ : (j + 1) * NQ], scores[j][:], ACT.Tanh, bias=biases[b][:, j : j + 1], scale=1.0 / CAP
                 )
             th.append(t)
+            if b == 0:
+                nc.scalar.activation(
+                    vgs[1][:, N // 2 : N], v_pool[:].indirect(lists[1][:, COLS // 2 : COLS]), ACT.Copy
+                )
 
-        nc.vector.tensor_copy(vgs[1][:], v_pool[:].indirect(lists[1]))
         vi = sb.tile([P, B, DV * PACK], BF16, name="vi", align_bytes=64)
         for b in range(B):
-            bank = ps.tile([P, 2, P], F32, name=f"vt{b}", tag=f"a{b}")
+            bank = ps.tile([P, 2, P], F32, name=f"vt{b}", tag=f"s{b}")
             for u in range(2):
                 nc.tensor.transpose(bank[:, u, :], vgs[b][:].bitcast(F32)[:, u : N // 2 : 2], ident[:])
             nc.scalar.copy(
@@ -191,7 +193,7 @@ def tile_attend_rel2_cap_kb_pgb2q128n512t2048_kernel(
                 )
 
         def row_sum(b):
-            pT = ps.tile([P, P], F32, name=f"pT{b}", tag=f"b{b}")
+            pT = ps.tile([P, P], F32, name=f"pT{b}", tag=f"s{2 + b}")
             for j in range(PACK):
                 nc.tensor.matmul(
                     pT[:],
@@ -218,7 +220,7 @@ def tile_attend_rel2_cap_kb_pgb2q128n512t2048_kernel(
         for b in range(B):
             inv = sb.tile([P, 1], F32, name=f"inv{b}")
             nc.vector.reciprocal(inv[:], totals[b][:])
-            y = ps.tile([P, DV], F32, name=f"y{b}", tag=f"s{b}")
+            y = ps.tile([P, DV], F32, name=f"y{b}", tag=f"a{b}")
             nc.tensor.matmul_mx(
                 out=y[:],
                 lhsT=w_codes[b][:].bitcast(FP8X4),

@@ -55,10 +55,6 @@ def tile_attend_rel2_cap_kb_pgb2q128n512t2048_kernel(
         kw_pool = sb.tile([P, T], I32, name="kw_pool")
         nc.sync.dma_start(kw_pool[:], k_words[0].rearrange("p t r -> p (t r)").bitcast(I32))
 
-        warm = sb.tile([P, 2, 8], F32, name="warm")
-        nc.vector.memset(warm[:, 0, :], 0.0)
-        nc.scalar.activation(warm[:, 1, :], warm[:, 0, :], ACT.Tanh)
-
         nc.vector.memset(kb_pool[0:ROW, :], 0.0)
         nc.vector.memset(ks_pool[96:P, :], 0)
         nc.vector.memset(vs_pool[0:ROW, :], 0.0)

@@ -33,11 +33,12 @@ def tile_attend_rel2_cap_kb_pgb2q128n512t2048_kernel(
         sb = ctx.enter_context(tc.tile_pool(name="sb", bufs=1))
         ps = ctx.enter_context(tc.psum_pool(name="ps", bufs=1))
 
+        qs = sb.tile([P, B * PASSES, NQ // 4], I32, name="qs", align_bytes=64)
+        ks_pool = sb.tile([P, T // 4], I32, name="ks_pool", tag="late", align_bytes=64)
+        nc.gpsimd.memset(ks_pool[96:P, :], 0)
+        nc.gpsimd.memset(qs[:], 0)
         ident = sb.tile([P, P], F32, name="ident")
         make_identity(nc, ident[:])
-
-        qs = sb.tile([P, B * PASSES, NQ // 4], I32, name="qs", align_bytes=64)
-        nc.vector.memset(qs[:], 0)
 
         offsets = sb.tile([P, B * COLS], U16, name="offsets")
         nc.sync.dma_start(offsets[:], offs)
@@ -46,7 +47,6 @@ def tile_attend_rel2_cap_kb_pgb2q128n512t2048_kernel(
         kb_pool = sb.tile([P, T], F32, name="kb_pool")
         nc.scalar.dma_start(kb_pool[ROW : ROW + 1, :], kb[0:1, :])
 
-        ks_pool = sb.tile([P, T // 4], I32, name="ks_pool", tag="ks_pool", align_bytes=64)
         scale_rows = k_scales.rearrange("o f t -> (o f) t").bitcast(I32)
         for first, row, count in ((0, 0, 32), (32, 4, 16), (48, 12, 16), (64, 0, 32)):
             nc.sync.dma_start(ks_pool[first : first + count, :], scale_rows[row : row + count, :])
@@ -54,28 +54,17 @@ def tile_attend_rel2_cap_kb_pgb2q128n512t2048_kernel(
         nc.scalar.dma_start(vs_pool[ROW : ROW + 1, :], vs[0:1, :])
         kw_pool = sb.tile([P, T], I32, name="kw_pool")
         nc.sync.dma_start(kw_pool[:], k_words[0].rearrange("p t r -> p (t r)").bitcast(I32))
-
-        nc.vector.memset(kb_pool[0:ROW, :], 0.0)
-        nc.vector.memset(ks_pool[96:P, :], 0)
-        nc.vector.memset(vs_pool[0:ROW, :], 0.0)
-
-        def load_query_scales(row):
-            nc.sync.dma_start(
+        qw = sb.tile([P, B * PASSES, NQ], I32, name="qw", align_bytes=64)
+        nc.sync.dma_start(qw[:], q_words.rearrange("b o g q r -> g (b o) (q r)").bitcast(I32))
+        for row in range(4):
+            queue = nc.gpsimd if row < 2 else nc.sync
+            queue.dma_start(
                 qs[row:P:32, :, :],
                 q_scales[:, :, row:16:4, :].rearrange("b o f q -> f (b o) q").bitcast(I32),
             )
 
-        def load_queries(b, tag):
-            words = sb.tile([P, PASSES, NQ], I32, name=f"qw{b}", tag=tag, align_bytes=64)
-            nc.sync.dma_start(words[:], q_words[b].rearrange("o g q r -> g o (q r)").bitcast(I32))
-            return words
-
-        qw = [load_queries(0, "qw0")]
-        load_query_scales(0)
-        v_pool = sb.tile([P, T], F32, name="v_pool")
-        nc.sync.dma_start(v_pool[:], vT)
-        for row in range(1, 4):
-            load_query_scales(row)
+        nc.vector.memset(kb_pool[0:ROW, :], 0.0)
+        nc.vector.memset(vs_pool[0:ROW, :], 0.0)
 
         ksg = sb.tile([P, B * N], U8, name="ksg", align_bytes=64)
         nc.vector.tensor_copy(
@@ -88,29 +77,32 @@ def tile_attend_rel2_cap_kb_pgb2q128n512t2048_kernel(
                 first = 52 * o + 8 * h
                 nc.sync.dma_start(plane[64 * h : 64 * h + 64, :], ksg[:].bitcast(I32)[first : first + 64, :])
             planes.append(plane[:].bitcast(U8))
-        qw.append(load_queries(1, "ks_pool"))
+        v_pool = sb.tile([P, T], F32, name="v_pool", tag="late", align_bytes=64)
+        nc.sync.dma_start(v_pool[:], vT)
 
-        vgs = [sb.tile([P, N], BF16, name=f"vg{b}") for b in range(B)]
-        bias1 = sb.tile([P, PACK], F32, name="bias1")
-        biases = [vgs[1][:].bitcast(F32)[:, N // 4 : N // 4 + PACK], bias1[:]]
+        vg = sb.tile([P, B * N], BF16, name="vg")
+        vgs = [vg[:, b * N : (b + 1) * N] for b in range(B)]
+        bias0 = sb.tile([P, PACK], F32, name="bias0")
+
+        def turned_row(name, row, tag, scale, col):
+            bank = ps.tile([P, PACK, P], F32, name=f"{name}T", tag=tag)
+            for j in range(PACK):
+                nc.tensor.transpose(bank[:, j, :], row[:, j:N:PACK], ident[:])
+            nc.scalar.activation(col, bank[:, :, ROW], ACT.Copy, scale=scale)
+
+        biases = [bias0[:], vg[:].bitcast(F32)[:, N // 2 - 2 : N // 2 + 2]]
         for b in range(B):
             kbg = sb.tile([P, N], F32, name=f"kbg{b}")
             nc.scalar.activation(kbg[:], kb_pool[:].indirect(lists[b]), ACT.Copy)
-            bank = ps.tile([P, PACK, P], F32, name=f"kbT{b}", tag=f"a{b}")
-            for j in range(PACK):
-                nc.tensor.transpose(bank[:, j, :], kbg[:, j:N:PACK], ident[:])
-            nc.scalar.activation(biases[b], bank[:, :, ROW], ACT.Copy, scale=1.0 / CAP)
+            turned_row(f"kb{b}", kbg[:], f"a{b}", 1.0 / CAP, biases[b])
 
-        vsg = sb.tile([P, B * N], F32, name="vsg")
-        nc.scalar.activation(vsg[:], vs_pool[:].indirect(offsets[:]), ACT.Copy)
-        vsp = []
+        vsg = [sb.tile([P, N], F32, name=f"vsg{b}") for b in range(B)]
         for b in range(B):
-            col = sb.tile([P, PACK], F32, name=f"vsp{b}")
-            nc.sync.dma_start(col[:], vsg[ROW : ROW + 1, b * N : (b + 1) * N].rearrange("o (p j) -> o p j", j=PACK))
-            vsp.append(col)
-
-        nc.scalar.activation(vgs[0][:], v_pool[:].indirect(lists[0]), ACT.Copy)
-        nc.scalar.activation(vgs[1][:, 0 : N // 2], v_pool[:].indirect(lists[1][:, 0 : COLS // 2]), ACT.Copy)
+            nc.scalar.activation(vsg[b][:], vs_pool[:].indirect(lists[b]), ACT.Copy)
+        vsp1 = sb.tile([P, PACK], F32, name="vsp1")
+        vsp = [vg[:].bitcast(F32)[:, N - PACK : N], vsp1[:]]
+        turned_row("vs0", vsg[0][:], "c0", 1.0, vsp[0])
+        nc.sync.dma_start(vsp[1], vsg[1][ROW : ROW + 1, :].rearrange("o (p j) -> o p j", j=PACK))
 
         th = []
         for b in range(B):
@@ -129,36 +121,22 @@ def tile_attend_rel2_cap_kb_pgb2q128n512t2048_kernel(
                     )
 
             t = sb.tile([P, N], F32, name=f"t{b}")
-            scores = [ps.tile([P, NQ], F32, name=f"score{b}{j}", tag=f"s{j}") for j in range(PACK)]
-            for o in range(PASSES):
-                for j in range(PACK):
+            for j in range(PACK):
+                score = ps.tile([P, NQ], F32, name=f"score{b}{j}", tag=f"s{j}")
+                for o in range(PASSES):
                     nc.tensor.matmul_mx(
-                        out=scores[j][:],
+                        out=score[:],
                         lhsT=kp[o][:, 2 * P * j : 2 * P * (j + 1)].bitcast(FP4X4),
                         lhsT_scale=planes[o][:, P * (PACK * b + j) : P * (PACK * b + j + 1)],
-                        rhs=qw[b][:, o, :].bitcast(FP8X4),
+                        rhs=qw[:, b * PASSES + o, :].bitcast(FP8X4),
                         rhs_scale=qs[:, b * PASSES + o, :].bitcast(U8),
                         start=(o == 0),
                         stop=(o == PASSES - 1),
                     )
-            for j in range(PACK):
                 nc.scalar.activation(
-                    t[:, j * NQ : (j + 1) * NQ], scores[j][:], ACT.Tanh, bias=biases[b][:, j : j + 1], scale=1.0 / CAP
+                    t[:, j * NQ : (j + 1) * NQ], score[:], ACT.Tanh, bias=biases[b][:, j : j + 1], scale=1.0 / CAP
                 )
             th.append(t)
-            if b == 0:
-                nc.scalar.activation(
-                    vgs[1][:, N // 2 : N], v_pool[:].indirect(lists[1][:, COLS // 2 : COLS]), ACT.Copy
-                )
-
-        vi = sb.tile([P, B, DV * PACK], BF16, name="vi", align_bytes=64)
-        for b in range(B):
-            bank = ps.tile([P, 2, P], F32, name=f"vt{b}", tag=f"s{b}")
-            for u in range(2):
-                nc.tensor.transpose(bank[:, u, :], vgs[b][:].bitcast(F32)[:, u : N // 2 : 2], ident[:])
-            nc.scalar.copy(
-                vi[:, b, :].bitcast(F32).rearrange("p (e u) -> p e u", u=2), bank[:].rearrange("p u e -> p e u")
-            )
 
         sq = [sb.tile([P, PACK, NQ], F32, name=f"p{b}") for b in range(B)]
         ws = [sb.tile([P, NQ, PACK], BF16, name=f"w{b}", align_bytes=64) for b in range(B)]
@@ -175,12 +153,10 @@ def tile_attend_rel2_cap_kb_pgb2q128n512t2048_kernel(
                     ws[b][:, half, :],
                     sq[b][:, :, half].rearrange("p j q -> p q j"),
                     CAP * CAP,
-                    vsp[b][:].unsqueeze(1).to_broadcast([P, NQ // 2, PACK]),
+                    vsp[b].unsqueeze(1).to_broadcast([P, NQ // 2, PACK]),
                     ALU.mult,
                     ALU.mult,
                 )
-
-        def quantise_weights(b):
             for half in query_halves:
                 nc.vector.quantize_mx(
                     w_codes[b][:, half].bitcast(FP8X4),
@@ -188,47 +164,50 @@ def tile_attend_rel2_cap_kb_pgb2q128n512t2048_kernel(
                     ws[b][:, half, :].rearrange("p q j -> p (q j)"),
                 )
 
-        def row_sum(b):
+        weights(0)
+        nc.vector.tensor_copy(vgs[1][:, N // 2 : N], v_pool[:].indirect(lists[1][:, COLS // 2 : COLS]))
+        weights(1)
+        nc.scalar.activation(vgs[0], v_pool[:].indirect(lists[0]), ACT.Copy)
+        nc.scalar.activation(vgs[1][:, 0 : N // 2], v_pool[:].indirect(lists[1][:, 0 : COLS // 2]), ACT.Copy)
+
+        v_codes = []
+        v_scales = []
+        for b in range(B):
+            bank = ps.tile([P, 2, P], F32, name=f"vt{b}", tag=f"s{b}")
+            for u in range(2):
+                nc.tensor.transpose(bank[:, u, :], vgs[b].bitcast(F32)[:, u : N // 2 : 2], ident[:])
+            vi = sb.tile([P, DV * PACK], BF16, name=f"vi{b}", align_bytes=64)
+            nc.scalar.copy(vi[:].bitcast(F32).rearrange("p (e u) -> p e u", u=2), bank[:].rearrange("p u e -> p e u"))
+            codes = sb.tile([P, DV], U32, name=f"v_codes{b}", align_bytes=64)
+            scales = sb.tile([P, DV], U8, name=f"v_scales{b}", align_bytes=64)
+            nc.vector.quantize_mx(codes[:].bitcast(FP8X4), scales[:], vi[:])
+            v_codes.append(codes)
+            v_scales.append(scales)
+
+        for b in range(B):
             pT = ps.tile([P, P], F32, name=f"pT{b}", tag=f"s{2 + b}")
             for j in range(PACK):
                 nc.tensor.matmul(
-                    pT[:],
-                    sq[b][:, j, :],
-                    ident[:],
-                    start=(j == 0),
-                    stop=(j == PACK - 1),
-                    is_transpose=True,
+                    pT[:], sq[b][:, j, :], ident[:], start=(j == 0), stop=(j == PACK - 1), is_transpose=True
                 )
             junk = sb.tile([P, P], BF16, name=f"junk{b}")
             total = sb.tile([P, 1], F32, name=f"total{b}")
             nc.scalar.activation(junk[:], pT[:], ACT.Copy, bias=1.0 / P, scale=CAP * CAP, accum_out=total[:])
-            return total
-
-        weights(0)
-        quantise_weights(0)
-        weights(1)
-        totals = [row_sum(b) for b in range(B)]
-        v_codes = sb.tile([P, B * DV], U32, name="v_codes", align_bytes=64)
-        v_scales = sb.tile([P, B * DV], U8, name="v_scales", align_bytes=64)
-        nc.vector.quantize_mx(v_codes[:].bitcast(FP8X4), v_scales[:], vi[:].rearrange("p b c -> p (b c)"))
-        quantise_weights(1)
-
-        for b in range(B):
             inv = sb.tile([P, 1], F32, name=f"inv{b}")
-            nc.vector.reciprocal(inv[:], totals[b][:])
+            nc.vector.reciprocal(inv[:], total[:])
             y = ps.tile([P, DV], F32, name=f"y{b}", tag=f"a{b}")
             nc.tensor.matmul_mx(
                 out=y[:],
                 lhsT=w_codes[b][:].bitcast(FP8X4),
                 lhsT_scale=w_scales[b][:],
-                rhs=v_codes[:, b * DV : (b + 1) * DV].bitcast(FP8X4),
-                rhs_scale=v_scales[:, b * DV : (b + 1) * DV],
+                rhs=v_codes[b][:].bitcast(FP8X4),
+                rhs_scale=v_scales[b][:],
                 start=True,
                 stop=True,
             )
             res = sb.tile([P, DV], F32, name=f"res{b}")
             if b == 0:
-                nc.vector.tensor_scalar(res[:], y[:], inv[:], None, ALU.mult)
-            else:
                 nc.scalar.activation(res[:], y[:], ACT.Copy, scale=inv[:])
+            else:
+                nc.vector.tensor_scalar(res[:], y[:], inv[:], None, ALU.mult)
             nc.sync.dma_start(out[b], res[:])

@@ -33,10 +33,12 @@ def tile_attend_rel2_cap_kb_pgb2q128n512t2048_kernel(
         sb = ctx.enter_context(tc.tile_pool(name="sb", bufs=1))
         ps = ctx.enter_context(tc.psum_pool(name="ps", bufs=1))
 
+        warm = sb.tile([P, 2], F32, name="warm")
+        nc.vector.memset(warm[:, 0:1], 0.0)
+        nc.scalar.activation(warm[:, 1:2], warm[:, 0:1], ACT.Tanh)
+
         qs = sb.tile([P, B * PASSES, NQ // 4], I32, name="qs", align_bytes=64)
-        ks_pool = sb.tile([P, T // 4], I32, name="ks_pool", tag="late", align_bytes=64)
-        nc.gpsimd.memset(ks_pool[96:P, :], 0)
-        nc.gpsimd.memset(qs[:], 0)
+        nc.vector.memset(qs[:], 0)
         ident = sb.tile([P, P], F32, name="ident")
         make_identity(nc, ident[:])
 
@@ -47,6 +49,7 @@ def tile_attend_rel2_cap_kb_pgb2q128n512t2048_kernel(
         kb_pool = sb.tile([P, T], F32, name="kb_pool")
         nc.scalar.dma_start(kb_pool[ROW : ROW + 1, :], kb[0:1, :])
 
+        ks_pool = sb.tile([P, T // 4], I32, name="ks_pool", align_bytes=64)
         scale_rows = k_scales.rearrange("o f t -> (o f) t").bitcast(I32)
         for first, row, count in ((0, 0, 32), (32, 4, 16), (48, 12, 16), (64, 0, 32)):
             nc.sync.dma_start(ks_pool[first : first + count, :], scale_rows[row : row + count, :])
@@ -54,15 +57,23 @@ def tile_attend_rel2_cap_kb_pgb2q128n512t2048_kernel(
         nc.scalar.dma_start(vs_pool[ROW : ROW + 1, :], vs[0:1, :])
         kw_pool = sb.tile([P, T], I32, name="kw_pool")
         nc.sync.dma_start(kw_pool[:], k_words[0].rearrange("p t r -> p (t r)").bitcast(I32))
-        qw = sb.tile([P, B * PASSES, NQ], I32, name="qw", align_bytes=64)
-        nc.sync.dma_start(qw[:], q_words.rearrange("b o g q r -> g (b o) (q r)").bitcast(I32))
-        for row in range(4):
-            queue = nc.gpsimd if row < 2 else nc.sync
-            queue.dma_start(
+
+        def load_query_scales(row):
+            nc.sync.dma_start(
                 qs[row:P:32, :, :],
                 q_scales[:, :, row:16:4, :].rearrange("b o f q -> f (b o) q").bitcast(I32),
             )
 
+        for row in range(2):
+            load_query_scales(row)
+        qw = sb.tile([P, B * PASSES, NQ], I32, name="qw", align_bytes=64)
+        nc.sync.dma_start(qw[:], q_words.rearrange("b o g q r -> g (b o) (q r)").bitcast(I32))
+        for row in range(2, 4):
+            load_query_scales(row)
+        v_pool = sb.tile([P, T], F32, name="v_pool")
+        nc.sync.dma_start(v_pool[:], vT)
+
+        nc.vector.memset(ks_pool[96:P, :], 0)
         nc.vector.memset(kb_pool[0:ROW, :], 0.0)
         nc.vector.memset(vs_pool[0:ROW, :], 0.0)
 
@@ -70,15 +81,6 @@ def tile_attend_rel2_cap_kb_pgb2q128n512t2048_kernel(
         nc.vector.tensor_copy(
             ksg[:].rearrange("p (b j m) -> p b m j", b=B, j=PACK), ks_pool[:].bitcast(U8).indirect(offsets[:])
         )
-        planes = []
-        for o in range(PASSES):
-            plane = sb.tile([P, B * N // 4], I32, name=f"plane{o}", align_bytes=64)
-            for h in range(2):
-                first = 52 * o + 8 * h
-                nc.sync.dma_start(plane[64 * h : 64 * h + 64, :], ksg[:].bitcast(I32)[first : first + 64, :])
-            planes.append(plane[:].bitcast(U8))
-        v_pool = sb.tile([P, T], F32, name="v_pool", tag="late", align_bytes=64)
-        nc.sync.dma_start(v_pool[:], vT)
 
         vg = sb.tile([P, B * N], BF16, name="vg")
         vgs = [vg[:, b * N : (b + 1) * N] for b in range(B)]
@@ -91,10 +93,20 @@ def tile_attend_rel2_cap_kb_pgb2q128n512t2048_kernel(
             nc.scalar.activation(col, bank[:, :, ROW], ACT.Copy, scale=scale)
 
         biases = [bias0[:], vg[:].bitcast(F32)[:, N // 2 - 2 : N // 2 + 2]]
+        kbg = [sb.tile([P, N], F32, name=f"kbg{b}") for b in range(B)]
         for b in range(B):
-            kbg = sb.tile([P, N], F32, name=f"kbg{b}")
-            nc.scalar.activation(kbg[:], kb_pool[:].indirect(lists[b]), ACT.Copy)
-            turned_row(f"kb{b}", kbg[:], f"a{b}", 1.0 / CAP, biases[b])
+            nc.scalar.activation(kbg[b][:], kb_pool[:].indirect(lists[b]), ACT.Copy)
+        turned_row("kb0", kbg[0][:], "a0", 1.0 / CAP, biases[0])
+
+        planes = []
+        for o in range(PASSES):
+            plane = sb.tile([P, B * N // 4], I32, name=f"plane{o}", align_bytes=64)
+            for h in range(2):
+                first = 52 * o + 8 * h
+                nc.scalar.dma_start(plane[64 * h : 64 * h + 64, :], ksg[:].bitcast(I32)[first : first + 64, :])
+            planes.append(plane[:].bitcast(U8))
+
+        turned_row("kb1", kbg[1][:], "a1", 1.0 / CAP, biases[1])
 
         vsg = [sb.tile([P, N], F32, name=f"vsg{b}") for b in range(B)]
         for b in range(B):

@@ -53,7 +53,7 @@ def tile_attend_rel2_cap_kb_pgb2q128n512t2048_kernel(
         scale_rows = k_scales.rearrange("o f t -> (o f) t").bitcast(I32)
         for first, row, count in ((0, 0, 32), (32, 4, 16), (48, 12, 16), (64, 0, 32)):
             nc.sync.dma_start(ks_pool[first : first + count, :], scale_rows[row : row + count, :])
-        vs_pool = sb.tile([P, T], F32, name="vs_pool")
+        vs_pool = sb.tile([P, T], F32, name="vs_pool", tag="late")
         nc.scalar.dma_start(vs_pool[ROW : ROW + 1, :], vs[0:1, :])
         kw_pool = sb.tile([P, T], I32, name="kw_pool")
         nc.sync.dma_start(kw_pool[:], k_words[0].rearrange("p t r -> p (t r)").bitcast(I32))
@@ -64,14 +64,10 @@ def tile_attend_rel2_cap_kb_pgb2q128n512t2048_kernel(
                 q_scales[:, :, row:16:4, :].rearrange("b o f q -> f (b o) q").bitcast(I32),
             )
 
-        for row in range(2):
+        for row in range(4):
             load_query_scales(row)
         qw = sb.tile([P, B * PASSES, NQ], I32, name="qw", align_bytes=64)
         nc.sync.dma_start(qw[:], q_words.rearrange("b o g q r -> g (b o) (q r)").bitcast(I32))
-        for row in range(2, 4):
-            load_query_scales(row)
-        v_pool = sb.tile([P, T], F32, name="v_pool")
-        nc.sync.dma_start(v_pool[:], vT)
 
         nc.vector.memset(ks_pool[96:P, :], 0)
         nc.vector.memset(kb_pool[0:ROW, :], 0.0)
@@ -103,7 +99,7 @@ def tile_attend_rel2_cap_kb_pgb2q128n512t2048_kernel(
             plane = sb.tile([P, B * N // 4], I32, name=f"plane{o}", align_bytes=64)
             for h in range(2):
                 first = 52 * o + 8 * h
-                nc.scalar.dma_start(plane[64 * h : 64 * h + 64, :], ksg[:].bitcast(I32)[first : first + 64, :])
+                nc.sync.dma_start(plane[64 * h : 64 * h + 64, :], ksg[:].bitcast(I32)[first : first + 64, :])
             planes.append(plane[:].bitcast(U8))
 
         turned_row("kb1", kbg[1][:], "a1", 1.0 / CAP, biases[1])
@@ -111,11 +107,15 @@ def tile_attend_rel2_cap_kb_pgb2q128n512t2048_kernel(
         vsg = [sb.tile([P, N], F32, name=f"vsg{b}") for b in range(B)]
         for b in range(B):
             nc.scalar.activation(vsg[b][:], vs_pool[:].indirect(lists[b]), ACT.Copy)
-        vsp1 = sb.tile([P, PACK], F32, name="vsp1")
-        vsp = [vg[:].bitcast(F32)[:, N - PACK : N], vsp1[:]]
-        turned_row("vs0", vsg[0][:], "c0", 1.0, vsp[0])
-        nc.sync.dma_start(vsp[1], vsg[1][ROW : ROW + 1, :].rearrange("o (p j) -> o p j", j=PACK))
+        vsp = []
+        for b in range(B):
+            col = sb.tile([P, PACK], F32, name=f"vsp{b}")
+            nc.sync.dma_start(col[:], vsg[b][ROW : ROW + 1, :].rearrange("o (p j) -> o p j", j=PACK))
+            vsp.append(col[:])
+        v_pool = sb.tile([P, T], F32, name="v_pool", tag="late")
+        nc.sync.dma_start(v_pool[:], vT)
 
+        score_banks = [("s0", "s1", "s2", "s3"), ("c0", "c1", "a0", "a1")]
         th = []
         for b in range(B):
             kp = [sb.tile([P, 2 * N], U8, name=f"kp{b}{o}", align_bytes=64) for o in range(PASSES)]
@@ -133,11 +133,11 @@ def tile_attend_rel2_cap_kb_pgb2q128n512t2048_kernel(
                     )
 
             t = sb.tile([P, N], F32, name=f"t{b}")
-            for j in range(PACK):
-                score = ps.tile([P, NQ], F32, name=f"score{b}{j}", tag=f"s{j}")
-                for o in range(PASSES):
+            scores = [ps.tile([P, NQ], F32, name=f"score{b}{j}", tag=score_banks[b][j]) for j in range(PACK)]
+            for o in range(PASSES):
+                for j in range(PACK):
                     nc.tensor.matmul_mx(
-                        out=score[:],
+                        out=scores[j][:],
                         lhsT=kp[o][:, 2 * P * j : 2 * P * (j + 1)].bitcast(FP4X4),
                         lhsT_scale=planes[o][:, P * (PACK * b + j) : P * (PACK * b + j + 1)],
                         rhs=qw[:, b * PASSES + o, :].bitcast(FP8X4),
@@ -145,8 +145,9 @@ def tile_attend_rel2_cap_kb_pgb2q128n512t2048_kernel(
                         start=(o == 0),
                         stop=(o == PASSES - 1),
                     )
+            for j in range(PACK):
                 nc.scalar.activation(
-                    t[:, j * NQ : (j + 1) * NQ], score[:], ACT.Tanh, bias=biases[b][:, j : j + 1], scale=1.0 / CAP
+                    t[:, j * NQ : (j + 1) * NQ], scores[j][:], ACT.Tanh, bias=biases[b][:, j : j + 1], scale=1.0 / CAP
                 )
             th.append(t)
 
@@ -158,8 +159,8 @@ def tile_attend_rel2_cap_kb_pgb2q128n512t2048_kernel(
 
         def weights(b):
             t = th[b][:].rearrange("p (j q) -> p j q", j=PACK)
-            for half in query_halves:
-                nc.vector.scalar_tensor_tensor(sq[b][:, :, half], t[:, :, half], 0.0, t[:, :, half], ALU.max, ALU.mult)
+            for pair in (slice(0, 2), slice(2, 4)):
+                nc.vector.scalar_tensor_tensor(sq[b][:, pair, :], t[:, pair, :], 0.0, t[:, pair, :], ALU.max, ALU.mult)
             for half in query_halves:
                 nc.vector.scalar_tensor_tensor(
                     ws[b][:, half, :],
@@ -177,10 +178,9 @@ def tile_attend_rel2_cap_kb_pgb2q128n512t2048_kernel(
                 )
 
         weights(0)
-        nc.vector.tensor_copy(vgs[1][:, N // 2 : N], v_pool[:].indirect(lists[1][:, COLS // 2 : COLS]))
         weights(1)
-        nc.scalar.activation(vgs[0], v_pool[:].indirect(lists[0]), ACT.Copy)
-        nc.scalar.activation(vgs[1][:, 0 : N // 2], v_pool[:].indirect(lists[1][:, 0 : COLS // 2]), ACT.Copy)
+        for b in range(B):
+            nc.scalar.activation(vgs[b], v_pool[:].indirect(lists[b]), ACT.Copy)
 
         v_codes = []
         v_scales = []

@@ -31,6 +31,7 @@ def tile_attend_rel2_cap_kb_pgb2q128n512t2048_kernel(
     nc = tc.nc
     with ExitStack() as ctx:
         sb = ctx.enter_context(tc.tile_pool(name="sb", bufs=1))
+        shared = ctx.enter_context(tc.tile_pool(name="shared", bufs=1))
         ps = ctx.enter_context(tc.psum_pool(name="ps", bufs=1))
 
         warm = sb.tile([P, 2], F32, name="warm")
@@ -53,7 +54,7 @@ def tile_attend_rel2_cap_kb_pgb2q128n512t2048_kernel(
         scale_rows = k_scales.rearrange("o f t -> (o f) t").bitcast(I32)
         for first, row, count in ((0, 0, 32), (32, 4, 16), (48, 12, 16), (64, 0, 32)):
             nc.sync.dma_start(ks_pool[first : first + count, :], scale_rows[row : row + count, :])
-        vs_pool = sb.tile([P, T], F32, name="vs_pool", tag="late")
+        vs_pool = shared.tile([P, T], F32, name="vs_pool", offset=0, align_bytes=64)
         nc.scalar.dma_start(vs_pool[ROW : ROW + 1, :], vs[0:1, :])
         kw_pool = sb.tile([P, T], I32, name="kw_pool")
         nc.sync.dma_start(kw_pool[:], k_words[0].rearrange("p t r -> p (t r)").bitcast(I32))
@@ -68,6 +69,8 @@ def tile_attend_rel2_cap_kb_pgb2q128n512t2048_kernel(
             load_query_scales(row)
         qw = sb.tile([P, B * PASSES, NQ], I32, name="qw", align_bytes=64)
         nc.sync.dma_start(qw[:], q_words.rearrange("b o g q r -> g (b o) (q r)").bitcast(I32))
+        v_pool = sb.tile([P, T], F32, name="v_pool")
+        nc.sync.dma_start(v_pool[:], vT)
 
         nc.vector.memset(ks_pool[96:P, :], 0)
         nc.vector.memset(kb_pool[0:ROW, :], 0.0)
@@ -78,42 +81,33 @@ def tile_attend_rel2_cap_kb_pgb2q128n512t2048_kernel(
             ksg[:].rearrange("p (b j m) -> p b m j", b=B, j=PACK), ks_pool[:].bitcast(U8).indirect(offsets[:])
         )
 
-        vg = sb.tile([P, B * N], BF16, name="vg")
-        vgs = [vg[:, b * N : (b + 1) * N] for b in range(B)]
-        bias0 = sb.tile([P, PACK], F32, name="bias0")
-
-        def turned_row(name, row, tag, scale, col):
-            bank = ps.tile([P, PACK, P], F32, name=f"{name}T", tag=tag)
-            for j in range(PACK):
-                nc.tensor.transpose(bank[:, j, :], row[:, j:N:PACK], ident[:])
-            nc.scalar.activation(col, bank[:, :, ROW], ACT.Copy, scale=scale)
-
-        biases = [bias0[:], vg[:].bitcast(F32)[:, N // 2 - 2 : N // 2 + 2]]
         kbg = [sb.tile([P, N], F32, name=f"kbg{b}") for b in range(B)]
         for b in range(B):
             nc.scalar.activation(kbg[b][:], kb_pool[:].indirect(lists[b]), ACT.Copy)
-        turned_row("kb0", kbg[0][:], "a0", 1.0 / CAP, biases[0])
+        vsg = sb.tile([P, B * N], F32, name="vsg")
+        nc.scalar.activation(vsg[:], vs_pool[:].indirect(offsets[:]), ACT.Copy)
 
         planes = []
         for o in range(PASSES):
-            plane = sb.tile([P, B * N // 4], I32, name=f"plane{o}", align_bytes=64)
+            plane = shared.tile([P, B * N // 4], I32, name=f"plane{o}", offset=o * B * N, align_bytes=64)
             for h in range(2):
                 first = 52 * o + 8 * h
-                nc.sync.dma_start(plane[64 * h : 64 * h + 64, :], ksg[:].bitcast(I32)[first : first + 64, :])
+                nc.scalar.dma_start(plane[64 * h : 64 * h + 64, :], ksg[:].bitcast(I32)[first : first + 64, :])
             planes.append(plane[:].bitcast(U8))
-
-        turned_row("kb1", kbg[1][:], "a1", 1.0 / CAP, biases[1])
-
-        vsg = [sb.tile([P, N], F32, name=f"vsg{b}") for b in range(B)]
-        for b in range(B):
-            nc.scalar.activation(vsg[b][:], vs_pool[:].indirect(lists[b]), ACT.Copy)
         vsp = []
         for b in range(B):
             col = sb.tile([P, PACK], F32, name=f"vsp{b}")
-            nc.sync.dma_start(col[:], vsg[b][ROW : ROW + 1, :].rearrange("o (p j) -> o p j", j=PACK))
+            nc.scalar.dma_start(col[:], vsg[ROW : ROW + 1, b * N : (b + 1) * N].rearrange("o (p j) -> o p j", j=PACK))
             vsp.append(col[:])
-        v_pool = sb.tile([P, T], F32, name="v_pool", tag="late")
-        nc.sync.dma_start(v_pool[:], vT)
+
+        vg = shared.tile([P, B * N], BF16, name="vg", offset=PASSES * B * N, align_bytes=64)
+        vgs = [vg[:, b * N : (b + 1) * N] for b in range(B)]
+        biases = [vgs[b].bitcast(F32)[:, 0:PACK] for b in range(B)]
+        for b in range(B):
+            bank = ps.tile([P, PACK, P], F32, name=f"kbT{b}", tag=f"a{b}")
+            for j in range(PACK):
+                nc.tensor.transpose(bank[:, j, :], kbg[b][:, j:N:PACK], ident[:])
+            nc.scalar.activation(biases[b], bank[:, :, ROW], ACT.Copy, scale=1.0 / CAP)
 
         score_banks = [("s0", "s1", "s2", "s3"), ("c0", "c1", "a0", "a1")]
         th = []
@@ -134,8 +128,8 @@ def tile_attend_rel2_cap_kb_pgb2q128n512t2048_kernel(
 
             t = sb.tile([P, N], F32, name=f"t{b}")
             scores = [ps.tile([P, NQ], F32, name=f"score{b}{j}", tag=score_banks[b][j]) for j in range(PACK)]
-            for o in range(PASSES):
-                for j in range(PACK):
+            for j in range(PACK):
+                for o in range(PASSES):
                     nc.tensor.matmul_mx(
                         out=scores[j][:],
                         lhsT=kp[o][:, 2 * P * j : 2 * P * (j + 1)].bitcast(FP4X4),
@@ -145,7 +139,6 @@ def tile_attend_rel2_cap_kb_pgb2q128n512t2048_kernel(
                         start=(o == 0),
                         stop=(o == PASSES - 1),
                     )
-            for j in range(PACK):
                 nc.scalar.activation(
                     t[:, j * NQ : (j + 1) * NQ], scores[j][:], ACT.Tanh, bias=biases[b][:, j : j + 1], scale=1.0 / CAP
                 )

@@ -50,7 +50,7 @@ def tile_attend_rel2_cap_kb_pgb2q128n512t2048_kernel(
         kb_pool = sb.tile([P, T], F32, name="kb_pool")
         nc.scalar.dma_start(kb_pool[ROW : ROW + 1, :], kb[0:1, :])
 
-        ks_pool = sb.tile([P, T // 4], I32, name="ks_pool", align_bytes=64)
+        ks_pool = shared.tile([P, T // 4], I32, name="ks_pool", offset=4 * T, align_bytes=64)
         scale_rows = k_scales.rearrange("o f t -> (o f) t").bitcast(I32)
         for first, row, count in ((0, 0, 32), (32, 4, 16), (48, 12, 16), (64, 0, 32)):
             nc.sync.dma_start(ks_pool[first : first + count, :], scale_rows[row : row + count, :])
@@ -69,8 +69,6 @@ def tile_attend_rel2_cap_kb_pgb2q128n512t2048_kernel(
             load_query_scales(row)
         qw = sb.tile([P, B * PASSES, NQ], I32, name="qw", align_bytes=64)
         nc.sync.dma_start(qw[:], q_words.rearrange("b o g q r -> g (b o) (q r)").bitcast(I32))
-        v_pool = sb.tile([P, T], F32, name="v_pool")
-        nc.sync.dma_start(v_pool[:], vT)
 
         nc.vector.memset(ks_pool[96:P, :], 0)
         nc.vector.memset(kb_pool[0:ROW, :], 0.0)
@@ -89,18 +87,20 @@ def tile_attend_rel2_cap_kb_pgb2q128n512t2048_kernel(
 
         planes = []
         for o in range(PASSES):
-            plane = shared.tile([P, B * N // 4], I32, name=f"plane{o}", offset=o * B * N, align_bytes=64)
+            plane = sb.tile([P, B * N // 4], I32, name=f"plane{o}", align_bytes=64)
             for h in range(2):
                 first = 52 * o + 8 * h
-                nc.scalar.dma_start(plane[64 * h : 64 * h + 64, :], ksg[:].bitcast(I32)[first : first + 64, :])
+                nc.sync.dma_start(plane[64 * h : 64 * h + 64, :], ksg[:].bitcast(I32)[first : first + 64, :])
             planes.append(plane[:].bitcast(U8))
+        v_pool = shared.tile([P, T], F32, name="v_pool", offset=4 * T + 64 * B, align_bytes=64)
+        nc.sync.dma_start(v_pool[:], vT)
         vsp = []
         for b in range(B):
-            col = sb.tile([P, PACK], F32, name=f"vsp{b}")
-            nc.scalar.dma_start(col[:], vsg[ROW : ROW + 1, b * N : (b + 1) * N].rearrange("o (p j) -> o p j", j=PACK))
+            col = shared.tile([P, PACK], F32, name=f"vsp{b}", offset=4 * T + 64 * b, align_bytes=64)
+            nc.sync.dma_start(col[:], vsg[ROW : ROW + 1, b * N : (b + 1) * N].rearrange("o (p j) -> o p j", j=PACK))
             vsp.append(col[:])
 
-        vg = shared.tile([P, B * N], BF16, name="vg", offset=PASSES * B * N, align_bytes=64)
+        vg = shared.tile([P, B * N], BF16, name="vg", offset=0, align_bytes=64)
         vgs = [vg[:, b * N : (b + 1) * N] for b in range(B)]
         biases = [vgs[b].bitcast(F32)[:, 0:PACK] for b in range(B)]
         for b in range(B):

from contextlib import ExitStack

import concourse.mybir as mybir
from concourse.masks import make_identity

B, N, T, D, DV, NQ = 2, 512, 2048, 1024, 128, 128
CAP = 2.0
FLOPS = 2 * B * NQ * N * (D + DV)

F32 = mybir.dt.float32
BF16 = mybir.dt.bfloat16
I32 = mybir.dt.int32
U32 = mybir.dt.uint32
U16 = mybir.dt.uint16
U8 = mybir.dt.uint8
FP8X4 = mybir.dt.float8_e4m3fn_x4
FP4X4 = mybir.dt.float4_e2m1fn_x4
ACT = mybir.ActivationFunctionType
ALU = mybir.AluOpType

P = 128
PACK = 4
PASSES = D // (P * PACK)
ROW = 127
COLS = N // 16


def tile_attend_rel2_cap_kb_pgb2q128n512t2048_kernel(
    tc, q_words, q_scales, k_words, k_scales, vT, vs, kb, offs, out
):
    nc = tc.nc
    with ExitStack() as ctx:
        sb = ctx.enter_context(tc.tile_pool(name="sb", bufs=1))
        shared = ctx.enter_context(tc.tile_pool(name="shared", bufs=1))
        ps = ctx.enter_context(tc.psum_pool(name="ps", bufs=1))

        warm = sb.tile([P, 2], F32, name="warm")
        nc.vector.memset(warm[:, 0:1], 0.0)
        nc.scalar.activation(warm[:, 1:2], warm[:, 0:1], ACT.Tanh)

        qs = sb.tile([P, B * PASSES, NQ // 4], I32, name="qs", align_bytes=64)
        nc.vector.memset(qs[:], 0)
        ident = sb.tile([P, P], F32, name="ident")
        make_identity(nc, ident[:])

        offsets = sb.tile([P, B * COLS], U16, name="offsets")
        nc.sync.dma_start(offsets[:], offs)
        lists = [offsets[:, b * COLS : (b + 1) * COLS] for b in range(B)]

        kb_pool = sb.tile([P, T], F32, name="kb_pool")
        nc.scalar.dma_start(kb_pool[ROW : ROW + 1, :], kb[0:1, :])

        ks_pool = shared.tile([P, T // 4], I32, name="ks_pool", offset=4 * T, align_bytes=64)
        scale_rows = k_scales.rearrange("o f t -> (o f) t").bitcast(I32)
        for first, row, count in ((0, 0, 32), (32, 4, 16), (48, 12, 16), (64, 0, 32)):
            nc.sync.dma_start(ks_pool[first : first + count, :], scale_rows[row : row + count, :])
        vs_pool = shared.tile([P, T], F32, name="vs_pool", offset=0, align_bytes=64)
        nc.scalar.dma_start(vs_pool[ROW : ROW + 1, :], vs[0:1, :])
        kw_pool = sb.tile([P, T], I32, name="kw_pool")
        nc.sync.dma_start(kw_pool[:], k_words[0].rearrange("p t r -> p (t r)").bitcast(I32))

        def load_query_scales(row):
            nc.sync.dma_start(
                qs[row:P:32, :, :],
                q_scales[:, :, row:16:4, :].rearrange("b o f q -> f (b o) q").bitcast(I32),
            )

        for row in range(4):
            load_query_scales(row)
        qw = sb.tile([P, B * PASSES, NQ], I32, name="qw", align_bytes=64)
        nc.sync.dma_start(qw[:], q_words.rearrange("b o g q r -> g (b o) (q r)").bitcast(I32))

        nc.vector.memset(ks_pool[96:P, :], 0)
        nc.vector.memset(kb_pool[0:ROW, :], 0.0)
        nc.vector.memset(vs_pool[0:ROW, :], 0.0)

        ksg = sb.tile([P, B * N], U8, name="ksg", align_bytes=64)
        nc.vector.tensor_copy(
            ksg[:].rearrange("p (b j m) -> p b m j", b=B, j=PACK), ks_pool[:].bitcast(U8).indirect(offsets[:])
        )

        kbg = [sb.tile([P, N], F32, name=f"kbg{b}") for b in range(B)]
        for b in range(B):
            nc.scalar.activation(kbg[b][:], kb_pool[:].indirect(lists[b]), ACT.Copy)
        vsg = sb.tile([P, B * N], F32, name="vsg")
        nc.scalar.activation(vsg[:], vs_pool[:].indirect(offsets[:]), ACT.Copy)

        planes = []
        for o in range(PASSES):
            plane = sb.tile([P, B * N // 4], I32, name=f"plane{o}", align_bytes=64)
            for h in range(2):
                first = 52 * o + 8 * h
                nc.sync.dma_start(plane[64 * h : 64 * h + 64, :], ksg[:].bitcast(I32)[first : first + 64, :])
            planes.append(plane[:].bitcast(U8))
        v_pool = shared.tile([P, T], F32, name="v_pool", offset=4 * T + 64 * B, align_bytes=64)
        nc.sync.dma_start(v_pool[:], vT)
        vsp = []
        for b in range(B):
            col = shared.tile([P, PACK], F32, name=f"vsp{b}", offset=4 * T + 64 * b, align_bytes=64)
            nc.sync.dma_start(col[:], vsg[ROW : ROW + 1, b * N : (b + 1) * N].rearrange("o (p j) -> o p j", j=PACK))
            vsp.append(col[:])

        vg = shared.tile([P, B * N], BF16, name="vg", offset=0, align_bytes=64)
        vgs = [vg[:, b * N : (b + 1) * N] for b in range(B)]
        biases = [vgs[b].bitcast(F32)[:, 0:PACK] for b in range(B)]
        for b in range(B):
            bank = ps.tile([P, PACK, P], F32, name=f"kbT{b}", tag=f"a{b}")
            for j in range(PACK):
                nc.tensor.transpose(bank[:, j, :], kbg[b][:, j:N:PACK], ident[:])
            nc.scalar.activation(biases[b], bank[:, :, ROW], ACT.Copy, scale=1.0 / CAP)

        score_banks = [("s0", "s1", "s2", "s3"), ("c0", "c1", "a0", "a1")]
        th = []
        for b in range(B):
            kp = [sb.tile([P, 2 * N], U8, name=f"kp{b}{o}", align_bytes=64) for o in range(PASSES)]
            halves = []
            for h in range(2):
                kwg = sb.tile([P, N // 2], U32, name=f"kwg{b}{h}", tag=f"half{h}", align_bytes=64)
                first = b * COLS + h * (COLS // 2)
                nc.vector.tensor_copy(kwg[:], kw_pool[:].bitcast(U32).indirect(offsets[:, first : first + COLS // 2]))
                halves.append(kwg)
            for o in range(PASSES):
                for h in range(2):
                    nc.vector.tensor_copy(
                        kp[o][:].bitcast(U16).rearrange("p (j g i) -> p g j i", j=PACK, i=4)[:, 16 * h : 16 * h + 16],
                        halves[h][:].bitcast(U16).rearrange("p (g i j o) -> p o g j i", j=PACK, o=PASSES, i=4)[:, o],
                    )

            t = sb.tile([P, N], F32, name=f"t{b}")
            scores = [ps.tile([P, NQ], F32, name=f"score{b}{j}", tag=score_banks[b][j]) for j in range(PACK)]
            for j in range(PACK):
                for o in range(PASSES):
                    nc.tensor.matmul_mx(
                        out=scores[j][:],
                        lhsT=kp[o][:, 2 * P * j : 2 * P * (j + 1)].bitcast(FP4X4),
                        lhsT_scale=planes[o][:, P * (PACK * b + j) : P * (PACK * b + j + 1)],
                        rhs=qw[:, b * PASSES + o, :].bitcast(FP8X4),
                        rhs_scale=qs[:, b * PASSES + o, :].bitcast(U8),
                        start=(o == 0),
                        stop=(o == PASSES - 1),
                    )
                nc.scalar.activation(
                    t[:, j * NQ : (j + 1) * NQ], scores[j][:], ACT.Tanh, bias=biases[b][:, j : j + 1], scale=1.0 / CAP
                )
            th.append(t)

        sq = [sb.tile([P, PACK, NQ], F32, name=f"p{b}") for b in range(B)]
        ws = [sb.tile([P, NQ, PACK], BF16, name=f"w{b}", align_bytes=64) for b in range(B)]
        w_codes = [sb.tile([P, NQ], U32, name=f"w_codes{b}", align_bytes=64) for b in range(B)]
        w_scales = [sb.tile([P, NQ], U8, name=f"w_scales{b}", align_bytes=64) for b in range(B)]
        query_halves = [slice(h * NQ // 2, (h + 1) * NQ // 2) for h in range(2)]

        def weights(b):
            t = th[b][:].rearrange("p (j q) -> p j q", j=PACK)
            for pair in (slice(0, 2), slice(2, 4)):
                nc.vector.scalar_tensor_tensor(sq[b][:, pair, :], t[:, pair, :], 0.0, t[:, pair, :], ALU.max, ALU.mult)
            for half in query_halves:
                nc.vector.scalar_tensor_tensor(
                    ws[b][:, half, :],
                    sq[b][:, :, half].rearrange("p j q -> p q j"),
                    CAP * CAP,
                    vsp[b].unsqueeze(1).to_broadcast([P, NQ // 2, PACK]),
                    ALU.mult,
                    ALU.mult,
                )
            for half in query_halves:
                nc.vector.quantize_mx(
                    w_codes[b][:, half].bitcast(FP8X4),
                    w_scales[b][:, half],
                    ws[b][:, half, :].rearrange("p q j -> p (q j)"),
                )

        weights(0)
        weights(1)
        for b in range(B):
            nc.scalar.activation(vgs[b], v_pool[:].indirect(lists[b]), ACT.Copy)

        v_codes = []
        v_scales = []
        for b in range(B):
            bank = ps.tile([P, 2, P], F32, name=f"vt{b}", tag=f"s{b}")
            for u in range(2):
                nc.tensor.transpose(bank[:, u, :], vgs[b].bitcast(F32)[:, u : N // 2 : 2], ident[:])
            vi = sb.tile([P, DV * PACK], BF16, name=f"vi{b}", align_bytes=64)
            nc.scalar.copy(vi[:].bitcast(F32).rearrange("p (e u) -> p e u", u=2), bank[:].rearrange("p u e -> p e u"))
            codes = sb.tile([P, DV], U32, name=f"v_codes{b}", align_bytes=64)
            scales = sb.tile([P, DV], U8, name=f"v_scales{b}", align_bytes=64)
            nc.vector.quantize_mx(codes[:].bitcast(FP8X4), scales[:], vi[:])
            v_codes.append(codes)
            v_scales.append(scales)

        for b in range(B):
            pT = ps.tile([P, P], F32, name=f"pT{b}", tag=f"s{2 + b}")
            for j in range(PACK):
                nc.tensor.matmul(
                    pT[:], sq[b][:, j, :], ident[:], start=(j == 0), stop=(j == PACK - 1), is_transpose=True
                )
            junk = sb.tile([P, P], BF16, name=f"junk{b}")
            total = sb.tile([P, 1], F32, name=f"total{b}")
            nc.scalar.activation(junk[:], pT[:], ACT.Copy, bias=1.0 / P, scale=CAP * CAP, accum_out=total[:])
            inv = sb.tile([P, 1], F32, name=f"inv{b}")
            nc.vector.reciprocal(inv[:], total[:])
            y = ps.tile([P, DV], F32, name=f"y{b}", tag=f"a{b}")
            nc.tensor.matmul_mx(
                out=y[:],
                lhsT=w_codes[b][:].bitcast(FP8X4),
                lhsT_scale=w_scales[b][:],
                rhs=v_codes[b][:].bitcast(FP8X4),
                rhs_scale=v_scales[b][:],
                start=True,
                stop=True,
            )
            res = sb.tile([P, DV], F32, name=f"res{b}")
            if b == 0:
                nc.scalar.activation(res[:], y[:], ACT.Copy, scale=inv[:])
            else:
                nc.vector.tensor_scalar(res[:], y[:], inv[:], None, ALU.mult)
            nc.sync.dma_start(out[b], res[:])
